import numpy as np, ml_dtypes
CORES = [16,18,20,22]
N = 4
import mx_ref
BF = ml_dtypes.bfloat16
def gentries(a):
    return np.ascontiguousarray(a.reshape(8, 16, -1).transpose(0, 2, 1)).reshape(8, -1)
def gtable(e):
    e = np.asarray(e); return np.ascontiguousarray(e.reshape(8, -1, 16).transpose(0, 2, 1)).reshape(128, -1).astype(np.int32)
def gcols(t, e):
    v = np.concatenate([t.reshape(8, 16, -1, 4), np.zeros((8, 16, 1, 4), BF)], axis=2)
    return np.ascontiguousarray(np.stack([v[g][:, e[g]] for g in range(8)])).reshape(128, -1)
def tile(rs):
    return np.stack(rs, axis=2).reshape(128, -1).astype(BF)
def pick(q, e):
    c = np.concatenate([q[0].reshape(128, -1, 4), np.zeros((128, 1, 4), np.uint8)], axis=1); s = np.concatenate([q[1], np.ones((16, 1), np.uint8)], axis=1)
    return (np.ascontiguousarray(c[:, e].reshape(128, -1)), np.ascontiguousarray(s[:, e]))
def join(*qs):
    return (np.concatenate([q[0] for q in qs], axis=1), np.concatenate([q[1] for q in qs], axis=1))
def put(q, e, v):
    c, s = q[0].reshape(128, -1, 4).copy(), q[1].copy(); c[:, e] = v[0].reshape(128, -1, 4); s[:, e] = v[1]
    return (c.reshape(128, -1), s)
def pk(c, s):
    return (np.ascontiguousarray(c), mx_ref.live(s))
def emit(q):
    return q[0], q[1]
def packed(v, rng):
    q = [mx_ref.quantize(np.ascontiguousarray(v[r])) for r in range(N)]
    return np.stack([a for a, b in q]), np.stack([mx_ref.plane(b, rng) for a, b in q])
def values_of_codes():
    e, c = np.zeros((128, 128, 4), np.float32), np.zeros((128, 2, 4), np.uint8)
    e[np.arange(128), np.arange(128), 0] = 1
    c[:127, :, 0] = np.arange(256).reshape(2, 128).T[:127]
    return mx_ref.matmul(mx_ref.quantize(e.reshape(128, 512).astype(BF)), (c.reshape(128, 8), np.full((16, 2), 127, np.uint8))).T.reshape(-1).astype(np.float64)
CODE_VALUE, SCALE_VALUE = values_of_codes(), 2.0 ** (np.arange(256) - 127.0)
def decode(q):
    return (CODE_VALUE[q[0]].reshape(16, 8, -1, 4) * SCALE_VALUE[q[1]][:, None, :, None] + 0.0).reshape(128, -1).astype(np.float32)
def f(rng, *shape):
    return mx_ref.flush((rng.standard_normal(shape, dtype=np.float32) * np.exp2(rng.integers(-2, 3, shape[:-1] + (1,)))).astype(BF))
def wide(rng, *shape, cols=0):
    v = rng.standard_normal(shape, dtype=np.float32) * np.exp2(rng.integers(-12, 13, shape)).astype(np.float32)
    if cols: v *= np.repeat(np.exp2(rng.integers(-cols, cols + 1, shape[:-2] + (1, shape[-1] // 4))) * (rng.random(shape[:-2] + (1, shape[-1] // 4)) > 0.0625), 4, axis=-1).astype(np.float32)
    return mx_ref.flush(v.astype(BF))
C, G, E, K, S = 384, 12, 6, 64, 256
STRIDE = [4, 2, 1]
DIR = [(-1, 0), (-1, 1), (0, 1), (1, 1), (1, 0), (1, -1), (0, -1), (-1, -1)]
def around(e, h):
    return np.stack([np.roll(e[:, g].reshape(N * G, 32), (-h * DIR[g][0], -h * DIR[g][1]), axis=(0, 1)).reshape(N, C) for g in range(8)], axis=1)
def numbers_of(rng):
    return {"x": np.array(f(rng, N, 128, 4 * C)), "u": np.array(f(rng, N, 128, 512)), "v": np.array(f(rng, N, 128, 512))}
def pointers(rng):
    return np.stack([gtable(rng.integers(0, S, (8, C))) for r in range(N)])
def same(rng, w):
    c, s = packed(np.stack([w] * N), rng)
    return {"wc": c, "ws": np.stack([s[0]] * N)}
def weights(rng, still=[]):
    w = np.array(f(rng, 128, 2048)).reshape(8, 16, 4, 8, 16, 4)
    for i in still:
        w[:, i] = 0
        w[:, :, :, :, i] = 0
    return same(rng, w.reshape(128, 2048))
def setup_inputs(rng):
    return {**numbers_of(rng), "p": pointers(rng), **weights(rng)}
def setup_inputs_ties(rng):
    d = numbers_of(rng)
    x = d["x"].reshape(N, 8, 16, C, 4)
    k = np.where(rng.random((N, 1, C)) < 0.5, 4, rng.integers(0, 3, (N, 1, C))) * np.ones((1, 8, 1))
    k[:, :, ::E] = rng.integers(0, 3, (N, 8, K))
    x[:, :, 0] = 0
    x[:, :, 0, :, 0] = k.astype(np.float32).astype(BF)
    u = d["u"].reshape(N, 128, 128, 4)
    u[:, :, ::16] = 0
    o = rng.permutation(N)
    for r in range(N):
        for h in range(0, 128, 16): u[r, h, h, 0] = 0.0 if r == o[0] else -1.0 if r == o[1] else 1.0
    return {"x": x.reshape(N, 128, 4 * C), "u": u.reshape(N, 128, 512), "v": d["v"], "p": pointers(rng), **weights(rng, [0])}
def setup_inputs_near(rng):
    d = numbers_of(rng)
    x = d["x"].astype(np.float32).reshape(N, 8, 16, C, 4)
    x[:, :, 0] = 0
    x[:, :, 8:] = 0
    x[:, :, 0, :, 0] = rng.integers(0, 2, (N, 1, C)) * 2.0 - 1.0
    x[:, :, 0, ::E] = 0
    s = rng.integers(0, 16, (N, 8, K))
    x[:, :, 8, ::E] = ((s[:, :, :, None] >> np.arange(4)) & 1) * np.exp2(np.arange(4) - 23.0)
    x[:, :, 10, :, 0] = (np.where(np.arange(8) < 4, -1.0, -1.125) * 2.0 ** -30)[:, None]
    x[:, :, 10, ::E, 0] = rng.integers(0, 2, (N, 8, K)) * 2.0 ** -30
    u = d["u"].reshape(N, 128, 128, 4)
    u[:, :, ::16] = 0
    o = rng.permutation(N) % 4
    for r in range(N):
        k = 1.0 if o[r] == 0 else 2.0 ** -30
        far = rng.permutation(8)
        if o[r] < 2:
            x[r, :, 11, :, 0] = -2.0 ** -10
            x[r, :, 11, ::E, 0] = 0
        for h in range(0, 128, 16):
            if o[r] < 2:
                u[r, h, h, 0] = k
                u[r, h + 11, h, 0] = k
            if o[r] == 2 and 16 * far[0] == h: u[r, h, h, 0] = 1.0
            if o[r] == 2 and 16 * far[1] == h: u[r, h, h, 0] = -1.0
            if o[r] < 3: u[r, h + 8, h] = k
            else: u[r, h + 10, h, 0] = k * 1.125 if h >= 64 else k * 1.25
    return {"x": x.reshape(N, 128, 4 * C).astype(BF), "u": u.reshape(N, 128, 512), "v": d["v"], "p": pointers(rng), **weights(rng, [0, 8, 9, 10, 11, 12, 13, 14, 15])}
def setup_inputs_huge(rng):
    d = numbers_of(rng)
    o = rng.permutation(N)
    c = rng.integers(0, 2, (N, 1, 1, C, 1)) * 2.0 - 1.0
    x = (0.6 + 0.09 * rng.random((N, 8, 16, C, 4))) * 2.0 ** 30 * c
    x[o == 0] = 0.875 * 2.0 ** 30 * c[o == 0]
    x[:, :, :, ::E] = (rng.random((N, 8, 1, K, 1)) * 2.0 - 1.0) * (0.8 + 0.2 * rng.random((N, 8, 16, K, 4))) * 2.0 ** 26
    a = 2.0 ** 29 * (1.0 - 0.1 * rng.random((N, 8, 16, 8, 4)))
    for g in range(8): a[:, g, :, g] *= 2.0
    for r in range(N):
        if o[r] == 0:
            a[r] = 2.0 ** 30
            for g in range(8): a[r, 0, :7 - g, g] *= 0.5
        if o[r] < N // 2: a[r] *= (rng.permutation(8) % 2 * 2.0 - 1.0)[None, None, :, None]
    u = d["u"].reshape(N, 128, 128, 4)
    u[:, :, ::16] = a.reshape(N, 128, 8, 4).astype(np.float32).astype(BF)
    w = np.zeros((128, 4, 128, 4), np.float32)
    i = np.arange(128)
    for b in range(4): w[i, b, i, b] = 4
    return {"x": x.astype(np.float32).reshape(N, 128, 4 * C).astype(BF), "u": u.reshape(N, 128, 512), "v": d["v"], "p": pointers(rng), **same(rng, w.reshape(128, 2048).astype(BF))}
def setup_inputs_few(rng):
    d = numbers_of(rng)
    e = rng.permutation(N)
    t = K * e[0] + rng.integers(0, K, (N, 8, C))
    t[e[0]] = S - 1
    t[e[1]] = 0
    t[e[2]] = K * e[2] + rng.integers(0, K, (8, C))
    t[e[3]] = rng.integers(0, S, (8, 1))
    return {**d, "p": np.stack([gtable(t[r]) for r in range(N)]), **weights(rng)}
def setup_inputs_spread(rng):
    d = setup_inputs(rng)
    d["x"] = wide(rng, N, 128, 4 * C, cols=6)
    return d
def check_inputs(d):
    b = []
    for k in ("x", "u", "v"):
        a = np.abs(d[k].astype(np.float32))
        if not (np.isfinite(a).all() and ((a == 0) | (a >= 2.0 ** -30) & (a <= 2.0 ** 30)).all()): b.append("a value of " + k)
    if not ((d["p"] >= 0) & (d["p"] < S)).all(): b.append("an entry of p")
    if ((d["wc"] & 0x7F) == 0x7F).any(): b.append("a code of wc that is no number")
    for k in ("wc", "ws"):
        if (d[k] != d[k][:1]).any(): b.append(k + " isn't the same on all ranks")
    z = np.zeros((128, 4, 4), np.float32)
    z[:, 1] = 2.0 ** -30
    z[:, 2] = 2.0 ** 30
    c, s = emit(mx_ref.quantize(z.reshape(128, 16).astype(BF)))
    for r in range(N):
        a = mx_ref.live(d["ws"][r])
        if not ((a == s[0, 0]) | (a >= s[0, 1]) & (a <= s[0, 2])).all(): b.append("a scale of ws")
    return b
def reference(x, u, v, p, wc, ws):
    qu = [mx_ref.quantize(u[r]) for r in range(N)]
    lay = [pk(wc[r], ws[r]) for r in range(N)]
    now = [x[r] for r in range(N)]
    ptr = np.stack([gentries(p[r]) for r in range(N)])
    for h in STRIDE:
        own = [decode(mx_ref.quantize(now[r])) for r in range(N)]
        seeds = np.concatenate([own[r].reshape(128, C, 4)[:, ::E] for r in range(N)], axis=1).reshape(128, 4 * S).astype(BF)
        came, new = around(ptr, h), []
        for r in range(N):
            z = (gcols(seeds, came[r]).astype(np.float32) - own[r]).astype(BF)
            s = mx_ref.matmul(qu[r], mx_ref.quantize(z))[::16] + np.float32(0.0)
            new.append(np.take_along_axis(came[r], np.argsort(-s, axis=0, kind="stable"), axis=0))
        ptr = np.stack(new)
        again = around(ptr, h)
        for r in range(N):
            q = mx_ref.quantize(gcols(seeds, again[r]))
            now[r] = tile([np.maximum(mx_ref.matmul(pick(lay[r], np.arange(128 * b, 128 * b + 128)), q), np.float32(0.0)) * np.float32(0.015625) + own[r][:, b::4] for b in range(4)])
    y, op = np.zeros((N, 128, C), np.float32), np.zeros((N, 8, C), np.float32)
    oc, osc = np.zeros((N, 128, 4 * C), np.uint8), np.zeros((N, 16, C), np.uint8)
    for r in range(N):
        q = mx_ref.quantize(now[r])
        y[r] = mx_ref.matmul(mx_ref.quantize(v[r]), q)
        op[r] = ptr[r]
        oc[r], osc[r] = emit(q)
    return {"y": y, "op": op, "oc": oc, "osc": osc}

@@ -1,0 +1,598 @@
+from concourse.bass import DstId, RemoteDMATransfer
+from concourse.mybir import dt, AluOpType, ActivationFunctionType
+
+C = 384
+H = [4, 2, 1]
+DC = [0, 1, 1, 1, 0, -1, -1, -1]
+
+SCRATCH = {}
+
+
+def _b(name, cols, dtype, where="sbuf"):
+    SCRATCH[name] = (where, [128, cols], dtype)
+
+
+X4, U8, BF, F32, I32, U16 = "float8_e4m3fn_x4", "uint8", "bfloat16", "float32", "int32", "uint16"
+for _i in range(8):
+    _b("ps%d" % _i, 512, F32, "psum")
+for _r in range(4):
+    _b("xt%d" % _r, 4 * C, BF)
+    _b("qx%d" % _r, C, X4)
+    _b("sx%d" % _r, C, U8)
+    _b("ext%d" % _r, 48, F32)
+for _r in range(3):
+    _b("bc%d" % _r, 256, X4)
+    _b("bs%d" % _r, 256, U8)
+    _b("qs%d" % _r, 128, X4)
+    _b("ss%d" % _r, 128, U8)
+    SCRATCH["fan%d" % _r] = ("dram", [48, 8, 24], F32)
+for _n, _c, _t in (("fp", 4 * C, BF), ("bp", 1024, BF), ("gz", 2 * C, BF), ("zt", 4 * C, BF), ("yt", 4 * C, BF), ("ys", 512, BF), ("yh", 512, BF), ("xsd", 512, BF), ("fh", 256, BF),
+                   ("exs", 40, F32), ("exr", 48, F32), ("lf", 32, F32), ("lw", 32, F32), ("lu", 32, U16), ("mi", 32, U16), ("mu", 32, U16), ("sv", 8, U16), ("lsh", 192, F32),
+                   ("qz", C, X4), ("sz", C, U8), ("qy", C, X4), ("sy", C, U8), ("qys", 128, X4), ("sys0", 128, U8), ("qh", 128, X4), ("sh0", 128, U8),
+                   ("sc", 192, F32), ("fl", 192, F32), ("f1", 96, F32), ("f2", 96, F32), ("f3", 48, F32), ("rk", 32, F32), ("exo", 48, F32),
+                   ("et", 768, BF), ("qe", 192, X4), ("se", 192, U8), ("eq", 192, F32), ("pr", 192, F32), ("p1", 96, F32), ("p2", 48, F32),
+                   ("sg", 32, F32), ("sm", 24, F32), ("s1", 8, F32), ("s2", 8, F32), ("rs", 256, F32), ("yo", C, F32), ("yo2", 64, F32), ("mh", 16, U16),
+                   ("ut", 512, BF), ("vt", 512, BF), ("qu", 128, X4), ("suu", 128, U8), ("qua", 128, X4), ("sua", 128, U8), ("qv", 128, X4), ("svv", 128, U8),
+                   ("wq", 512, X4), ("wsc", 512, U8), ("one", 528, BF), ("wd", 528, BF), ("ce", 512, X4), ("cs", 512, U8), ("ct", 1536, BF), ("cc", 384, X4), ("ccs", 384, U8),
+                   ("pi", 28, I32), ("kk", 128, I32), ("pf", 28, F32), ("pd", 12, F32), ("pe", 12, F32),
+                   ("ip", 16, I32), ("i12", 12, I32), ("cl", 32, F32), ("it", 240, I32), ("ul", 8, U16), ("sl", 4, U16), ("sh", 6, U16), ("shh", 2, U16), ("sd", 6, U16), ("el", 24, U16),
+                   ("q0", 128, F32), ("gk", 192, F32), ("sgn", 96, F32), ("dm", 24, F32), ("on", 32, F32), ("ot", 32, F32)):
+    _b(_n, _c, _t)
+SEMAPHORES = ["kv", "ks", "kt", "kg", "lx", "lp", "lu", "lw", "lv", "st", "loc", "ha0", "ha1", "ha2", "ha3"]
+for _r in range(3):
+    SEMAPHORES += ["se%d" % _r, "ow%d" % _r, "rr%d" % _r, "fw%d" % _r, "fr%d" % _r]
+
+
+def rank_program(g, core, T, topo):
+    rank = T.rank_of(core)
+    if rank is None:
+        return
+    A, F = AluOpType, ActivationFunctionType
+    N = len(T.cores)
+    vec, sca, ten, syn = g.vector, g.scalar, g.tensor, g.sync
+    queue = {"v": vec, "s": sca, "t": ten, "g": g, "y": syn}
+    total, seen, log, hold = {}, {q: {} for q in queue}, {}, []
+
+    def w(name, a, b, step=1, p0=0, p1=128):
+        return (name, a, b, step, p0, p1)
+
+    def ap(v):
+        name, a, b, step, p0, p1 = v
+        t = T[name]
+        if p0 == 0 and p1 == 128:
+            return t[:, a:b] if step == 1 else t[:, a:b:step]
+        return t[p0:p1, a:b] if step == 1 else t[p0:p1, a:b:step]
+
+    def meet(x, y):
+        if x[1] >= y[2] or y[1] >= x[2] or x[4] >= y[5] or y[4] >= x[5]:
+            return False
+        return not (x[3] == y[3] and x[3] > 1 and (x[1] - y[1]) % x[3])
+
+    def wait(q, sem, val):
+        if seen[q].get(sem, 0) < val:
+            queue[q].wait_ge(T.sem[sem], int(val))
+            seen[q][sem] = val
+
+    def order(q, reads, writes, acc, dma):
+        for vs, wr in ((reads, False), (writes, True)):
+            for v in vs:
+                bank = v[0][:2] == "ps"
+                for (o, owr, oq, osem, oval, odma) in log.get(v[0], ()):
+                    if not (bank or meet(v, o)):
+                        continue
+                    if not (wr or owr or (bank and oq != q)):
+                        continue
+                    if oq == q and not odma and not dma:
+                        if (acc and wr) or not owr:
+                            continue
+                    wait(q, osem, total[osem] if odma else oval)
+
+    def note(q, reads, writes, sem, val, dma):
+        for v in writes:
+            old = log.get(v[0], [])
+            log[v[0]] = [e for e in old if not (v[3] == 1 and v[1] <= e[0][1] and v[2] >= e[0][2] and v[4] <= e[0][4] and v[5] >= e[0][5])]
+            log[v[0]].append((v, True, q, sem, val, dma))
+        for v in reads:
+            log.setdefault(v[0], []).append((v, False, q, sem, val, dma))
+
+    def op(q, call, reads, writes, acc=False):
+        if hold:
+            hold[-1].append((q, call, reads, writes, acc))
+            return
+        order(q, reads, writes, acc, False)
+        sem = "k" + q
+        total[sem] = total.get(sem, 0) + 1
+        call().then_inc(T.sem[sem], 1)
+        note(q, reads, writes, sem, total[sem], False)
+
+    def weave(*chains):
+        lists = []
+        for c in chains:
+            hold.append([])
+            c()
+            lists.append(hold.pop())
+        for i in range(max(len(x) for x in lists)):
+            for x in lists:
+                if i < len(x):
+                    op(*x[i])
+
+    def dma(q, out, in_, sem, reads, writes, after=()):
+        order(q, reads, writes, False, True)
+        for s in after:
+            wait(q, s, total[s])
+        total[sem] = total.get(sem, 0) + 16
+        queue[q].dma_start(out, in_).then_inc(T.sem[sem], 16)
+        note(q, reads, writes, sem, total[sem], True)
+
+    def arrive(v, sem, val):
+        total[sem] = val
+        log.setdefault(v[0], []).append((v, True, "r", sem, val, True))
+
+    def at(v, ind):
+        return ap(v) if ind is None else ap(v).indirect(ap(ind))
+
+    def rd(v, ind):
+        return [v] if ind is None else [v, ind]
+
+    def copy(out, in_, ind=None):
+        op("v", lambda: vec.tensor_copy(ap(out), at(in_, ind)), rd(in_, ind), [out])
+
+    def tt(out, a, b, o, ind=None):
+        op("v", lambda: vec.tensor_tensor(ap(out), at(a, ind), ap(b), o), rd(a, ind) + [b], [out])
+
+    def ts(out, a, s1, o1, s2=None, o2=None, ind=None):
+        more = [s for s in (s1, s2) if isinstance(s, tuple)]
+        n1, n2 = [ap(s) if isinstance(s, tuple) else s for s in (s1, s2)]
+        if o2 is None:
+            op("v", lambda: vec.tensor_scalar(ap(out), at(a, ind), n1, None, o1), rd(a, ind) + more, [out])
+        else:
+            op("v", lambda: vec.tensor_scalar(ap(out), at(a, ind), n1, n2, o1, o2), rd(a, ind) + more, [out])
+
+    def fill(out, val):
+        op("v", lambda: vec.memset(ap(out), val), [], [out])
+
+    def act(out, in_, func=None, scale=1.0, ind=None):
+        f = F.Copy if func is None else func
+        if scale == 1.0:
+            op("s", lambda: sca.activation(ap(out), at(in_, ind), f), rd(in_, ind), [out])
+        else:
+            op("s", lambda: sca.activation(ap(out), at(in_, ind), f, scale=scale), rd(in_, ind), [out])
+
+    def quant(q, s, in_):
+        op("v", lambda: vec.quantize_mx(ap(q), ap(s), ap(in_)), [in_], [q, s])
+
+    def mm(out, l, ls, r, rs, start=True, stop=True):
+        op("t", lambda: ten.matmul_mx(ap(out), ap(l), ap(ls), ap(r), ap(rs), start, stop), [l, ls, r, rs], [out], acc=not start)
+
+    def iota(out, pat, base, cm):
+        if SCRATCH[out[0]][2] != I32:
+            op("g", lambda: g.iota(ap(out), pat, base, cm, allow_small_or_imprecise_dtypes=True), [], [out])
+        else:
+            op("g", lambda: g.iota(ap(out), pat, base, cm), [], [out])
+
+    def pick(qo, so, qi, si, ind):
+        op("v", lambda: vec.tensor_copy(ap(qo).bitcast(dt.uint32), ap(qi).bitcast(dt.uint32).indirect(ap(ind))), [qi, ind], [qo])
+        act(so, si, ind=ind)
+
+    up, down = (rank - 1) % N, (rank + 1) % N
+    others = [r for r in range(N) if r != rank]
+
+    def dst(r):
+        rid, pid, _ = topo.addr(T.cores[r])
+        return DstId(rid=rid, pnc=pid)
+
+    def bits(es):
+        return sum(1 << e for e in es)
+
+    def fused(trs, reads):
+        order("g", reads, [], False, True)
+        total["loc"] = total.get("loc", 0) + sum(bin(m).count("1") for _, m, _, _, _ in trs)
+        g.remote_dma_fused([RemoteDMATransfer(dst_ids=ids, dma_engine_mask=m, remote_sem=T.sem[sem], srcs=[src], dsts=dsts) for ids, m, sem, src, dsts in trs], local_sem=T.sem["loc"])
+
+    def halo(k):
+        e, s = "ext%d" % k, "ha%d" % k
+        eu, ed = topo.engines(core, T.cores[up]), topo.engines(core, T.cores[down])
+        hu, hd = eu[:len(eu) // 2], ed[len(ed) // 2:]
+        lo, hi = w(e, 8, 16), w(e, 24, 32)
+        fused([([dst(up)], bits(hu), s, ap(lo), [ap(w(e, 32, 40))]), ([dst(down)], bits(hd), s, ap(hi), [ap(w(e, 0, 8))])], [lo, hi])
+        arrive(w(e, 0, 8), s, len(hu) + len(hd))
+        arrive(w(e, 32, 40), s, len(hu) + len(hd))
+
+    def seeds(k):
+        m = bits(topo.engines(core, T.cores[others[0]]))
+        ids = [dst(r) for r in others]
+        a, b = 64 * rank, 64 * rank + 64
+        q, s, bq, bs = w("qs%d" % k, 0, 64), w("ss%d" % k, 0, 64), w("bc%d" % k, a, b), w("bs%d" % k, a, b)
+        fused([(ids, m, "se%d" % k, ap(q).bitcast(dt.uint8), [ap(bq).bitcast(dt.uint8) for r in others])], [q])
+        fused([(ids, m, "se%d" % k, ap(s), [ap(bs) for r in others])], [s])
+        dma("y", ap(bq).bitcast(dt.uint8), ap(q).bitcast(dt.uint8), "ow%d" % k, [q], [bq])
+        dma("y", ap(bs), ap(s), "ow%d" % k, [s], [bs])
+        n = 2 * len(others) * bin(m).count("1")
+        for r in others:
+            arrive(w("bc%d" % k, 64 * r, 64 * r + 64), "se%d" % k, n)
+            arrive(w("bs%d" % k, 64 * r, 64 * r + 64), "se%d" % k, n)
+
+    def turned(s):
+        for m in range(8):
+            d = s * DC[m]
+            if d == 0:
+                yield m, 0, 16, 0, False
+            elif d > 0:
+                yield m, 0, 16 - d, d, False
+                yield m, 16 - d, 16, 0, True
+            else:
+                yield m, -d, 16, 0, False
+                yield m, 0, -d, 16 + d, True
+
+    dma("y", ap(w("xt0", 0, 4 * C)), T.x[:, :], "lx", [], [w("xt0", 0, 4 * C)])
+    for m, a, b, o, _ in turned(H[0]):
+        v = w("pi", 0, 24, 1, 16 * m + a, 16 * m + b)
+        dma("s", ap(v), T.p[16 * m + o:16 * m + o + b - a, :], "lp", [], [v])
+    dma("y", ap(w("ut", 0, 512)), T.u[:, :], "lu", [], [w("ut", 0, 512)])
+    dma("y", ap(w("wq", 0, 512)).bitcast(dt.uint8), T.wc[:, :], "lw", [], [w("wq", 0, 512)])
+    dma("y", ap(w("wsc", 0, 512)), T.ws[:, :], "lw", [], [w("wsc", 0, 512)])
+    dma("y", ap(w("vt", 0, 512)), T.v[:, :], "lv", [], [w("vt", 0, 512)])
+
+    def ic(i):
+        return w("ip", i, i + 1)
+
+    def fc(i):
+        return w("cl", i, i + 1)
+
+    def it(i, n):
+        return w("it", 12 * i, 12 * i + n)
+
+    P, GI, QI = ic(0), ic(1), ic(2)
+    GF, QF, G16, DR1, CAR, DEL, GX = [fc(i) for i in range(7)]
+    idx, i4, i2 = it(0, 12), it(0, 4), it(0, 2)
+
+    fill(w("one", 0, 515), 1.0)
+    iota(P, [[0, 1]], 0, 1)
+    iota(w("i12", 0, 12), [[16, 12]], 0, 1)
+    op("g", lambda: g.affine_select(ap(w("wd", 0, 515)), ap(w("one", 0, 515)), [[-1, 515]], A.is_equal, 0.0, 3, 4), [w("one", 0, 515)], [w("wd", 0, 515)])
+    iota(w("sgn", 0, 96), [[2, 4], [-1, 8], [0, 3]], 0, 0)
+    iota(w("gk", 0, 192), [[-1, 8], [0, 24]], 0, 0)
+    iota(w("q0", 0, 128), [[0, 8], [1, 16]], 0, 0)
+    iota(w("ct", 0, 512), [[0, 512]], 0, 0)
+
+    ts(GI, P, 4, A.arith_shift_right)
+    ts(QI, P, 15, A.bitwise_and)
+    copy(GF, GI)
+    copy(QF, QI)
+    ts(G16, GF, -16.0, A.mult)
+    ts(idx, w("i12", 0, 12), G16, A.add)
+
+    def c_rows():
+        ts(fc(8), GF, 2.0, A.is_ge)
+        ts(fc(9), GF, 3.0, A.is_ge, fc(8), A.add)
+        tt(DR1, fc(9), fc(11), A.subtract)
+        for i, h in enumerate(H):
+            ts(fc(20 + i), DR1, 2.0 * h, A.mult, 8.0 - 2.0 * h, A.add)
+        ts(w("sh", 0, 2), i2, fc(20), A.add)
+
+    def c_rows2():
+        ts(fc(10), GF, 6.0, A.is_ge)
+        ts(fc(11), GF, 7.0, A.is_ge, fc(10), A.add)
+
+    def c_carry():
+        ts(fc(12), GF, 4.0, A.is_ge)
+        ts(fc(13), GF, 1.0, A.is_ge, fc(12), A.subtract)
+        ts(fc(15), GF, 5.0, A.is_ge)
+        ts(fc(14), QF, float(16 - H[0]), A.is_ge, fc(13), A.mult)
+        ts(fc(16), QF, float(H[0]), A.is_lt, fc(15), A.mult)
+        tt(CAR, fc(14), fc(16), A.add)
+
+    def c_pairs():
+        ts(it(1, 4), i4, 3, A.arith_shift_right, 3, A.bitwise_and)
+        ts(it(2, 4), i4, 5, A.arith_shift_right)
+        ts(it(3, 4), i4, 7, A.bitwise_and)
+        ts(it(1, 4), it(1, 4), 2, A.mult)
+        tt(it(1, 4), it(1, 4), it(2, 4), A.add)
+        tt(it(4, 4), it(1, 4), it(3, 4), A.max)
+        tt(w("it", 52, 56), it(1, 4), it(3, 4), A.min)
+        ts(w("ul", 0, 8), it(4, 8), 16, A.mult)
+
+    def c_half():
+        ts(ic(3), GI, 1, A.bitwise_and)
+        ts(fc(7), ic(3), -2.0, A.mult, 1.0, A.add)
+        tt(GX, fc(7), GF, A.add)
+
+    c_rows2()
+    weave(c_rows, c_carry, c_half)
+
+    def relabel(out, p, n):
+        k = [w("kk", 32 * i, 32 * i + n) for i in range(4)]
+        ts(k[0], p, 7, A.bitwise_and)
+        ts(k[1], k[0], 3, A.mult)
+        ts(k[2], k[1], 7, A.bitwise_and)
+        tt(k[3], k[2], k[0], A.subtract)
+        tt(out, k[3], p, A.add)
+
+    def c_pointers():
+        copy(w("pi", 24, 28), i4)
+        relabel(w("pf", 0, 28), w("pi", 0, 28), 28)
+        tt(w("pd", 0, 12), w("pf", 1, 24, 2), w("pf", 0, 24, 2), A.subtract)
+        ts(w("sl", 0, 4), w("pf", 24, 28), 6.0, A.mult)
+        ts(w("pe", 0, 12), w("pd", 0, 12), CAR, A.mult)
+        tt(w("ext0", 8, 32, 2), w("pf", 0, 24, 2), w("pe", 0, 12), A.add)
+        tt(w("ext0", 9, 32, 2), w("pf", 1, 24, 2), w("pe", 0, 12), A.subtract)
+
+    weave(c_pointers, c_pairs)
+    halo(0)
+
+    quant(w("qx0", 0, C), w("sx0", 0, C), w("xt0", 0, 4 * C))
+    pick(w("qs0", 0, 64), w("ss0", 0, 64), w("qx0", 0, C), w("sx0", 0, C), w("sl", 0, 4))
+    seeds(0)
+    iota(w("et", 0, 768), [[0, 768]], 0, 0)
+    iota(w("dm", 0, 24), [[1, 3], [0, 8]], 0, 0)
+    iota(w("ct", 512, 1536), [[0, 1024]], 0, 0)
+    for b in range(4):
+        quant(w("ce", 128 * b, 128 * b + 128), w("cs", 128 * b, 128 * b + 128), w("wd", 3 - b, 515 - b))
+
+    def bank(b, n, a=0, step=1):
+        return w("ps%d" % b, a, n, step)
+
+    def ceb(b):
+        return w("ce", 128 * b, 128 * b + 128), w("cs", 128 * b, 128 * b + 128)
+
+    def fpw(b, a=0, e=C):
+        return w("fp", C * b + a, C * b + e)
+
+    def unpack_f(k, bs):
+        for b in bs:
+            mm(bank(b, C), *ceb(b), w("qx%d" % k, 0, C), w("sx%d" % k, 0, C))
+            if b < 2:
+                act(fpw(b), bank(b, C))
+
+    unpack_f(0, (0, 1))
+
+    def lists(k, src):
+        copy(w("lf", 0, 32), w(src, 0, 48), w("sh", 2 * k, 2 * k + 2))
+        copy(w("lu", 0, 32), w("lf", 0, 32))
+
+    def fan(k):
+        t = T["fan%d" % k]
+        act(w("lw", 0, 24, 2), w("lf", 1, 24, 2))
+        act(w("lw", 1, 24, 2), w("lf", 0, 24, 2))
+        for j, n in ((1, "lf"), (0, "lw"), (2, "lw")):
+            for m in range(8):
+                v = w(n, 0, 24, 1, 16 * m, 16 * m + 16)
+                dma("y", t[16 * j:16 * j + 16, m, :], ap(v), "fw%d" % k, [v], [])
+        for m in range(8):
+            o = w("lsh", 0, 192, 1, 16 * m, 16 * m + 16)
+            a = 16 + H[k] * DC[m]
+            dma("y", ap(o), t[a:a + 16, :, :], "fr%d" % k, [], [o], ["fw%d" % k])
+
+    def turn(k, s, a, b):
+        e = "ext%d" % (k + 1)
+        act(w("exs", a, b, 2), w(e, a + 1, b, 2))
+        act(w("exs", a + 1, b, 2), w(e, a, b, 2))
+        for m, p, q, o, swap in turned(s):
+            v, d = w("exs" if swap else e, a, b, 1, 16 * m + o, 16 * m + o + q - p), w("exr", a, b, 1, 16 * m + p, 16 * m + q)
+            dma("y", ap(d), ap(v), "rr%d" % k, [v], [d])
+
+    quant(w("qu", 0, 128), w("suu", 0, 128), w("ut", 0, 512))
+    pick(w("qua", 0, 128), w("sua", 0, 128), w("qu", 0, 128), w("suu", 0, 128), w("ul", 0, 8))
+    fill(w("ext0", 40, 48), 0.0)
+
+    def c_spread():
+        n = [it(i, 12) for i in range(6, 13)]
+        ts(n[0], idx, 171, A.mult)
+        ts(n[0], n[0], 12, A.arith_shift_right)
+        ts(n[1], n[0], -24, A.mult)
+        tt(n[1], n[1], idx, A.add)
+        ts(n[2], n[1], 3, A.arith_shift_right)
+        ts(n[3], n[1], 7, A.bitwise_and)
+        ts(n[4], n[0], 3, A.mult, -24, A.add)
+        tt(n[4], n[4], n[2], A.add)
+        ts(n[5], n[3], GF, A.is_equal)
+        ts(n[6], n[3], GX, A.is_equal)
+        tt(n[5], n[5], n[4], A.mult)
+        tt(n[6], n[6], n[4], A.mult)
+        ts(w("el", 0, 12), n[5], 24, A.add)
+        ts(w("el", 12, 24), n[6], 24, A.add)
+
+    def c_misc():
+        ts(w("sgn", 0, 96), w("sgn", 0, 96), 0.0, A.is_ge, 2.0, A.mult)
+        ts(w("gk", 0, 192), w("gk", 0, 192), GF, A.add)
+        ts(w("sgn", 0, 96), w("sgn", 0, 96), -1.0, A.add)
+        fill(w("rk", 24, 32), 0.0)
+
+    def turner(i):
+        h = H[i]
+        for (g0, g1, d, e) in ((0, 1, 0, 0), (1, 4, h, 0), (1, 4, h - 16, 1), (4, 5, 0, 0), (5, 8, -h, 0), (5, 8, 16 - h, 1)):
+            ts(w("ct", 512 * i + 64 * g0 + e, 512 * i + 64 * g1, 4), w("q0", 16 * g0, 16 * g1), float(d), A.add, QF, A.is_equal)
+        quant(w("cc", 128 * i, 128 * i + 128), w("ccs", 128 * i, 128 * i + 128), w("ct", 512 * i, 512 * i + 512))
+
+    def c_seeds():
+        ts(ic(4), P, 15, A.bitwise_and, 1, A.arith_shift_right)
+        ts(it(13, 2), i2, 7, A.bitwise_and)
+        ts(ic(5), ic(4), 11, A.mult)
+        ts(it(14, 2), i2, 3, A.arith_shift_right)
+        ts(ic(5), ic(5), 5, A.arith_shift_right)
+        ts(it(13, 2), it(13, 2), 3, A.mult)
+        ts(ic(5), ic(5), -3, A.mult)
+        tt(it(13, 2), it(13, 2), it(14, 2), A.add)
+        tt(DEL, ic(5), ic(4), A.add)
+        for i in range(2):
+            ts(w("sd", 2 * i, 2 * i + 2), it(13, 2), fc(20 + i), A.add)
+        ts(w("dm", 0, 24), w("dm", 0, 24), DEL, A.is_equal)
+
+    weave(c_spread, c_misc)
+    lists(0, "ext0")
+    fan(0)
+    turner(0)
+
+    def bwin(b):
+        return w("bp", 256 * b, 256 * b + 256)
+
+    def wb(b):
+        return w("wq", 128 * b, 128 * b + 128), w("wsc", 128 * b, 128 * b + 128)
+
+    def gather(out, b, ind):
+        if b < 2:
+            ts(out, bwin(b), 0.015625, A.mult, ind=ind)
+        else:
+            act(out, bwin(b), scale=0.015625, ind=ind)
+
+    for k in range(3):
+        h, last = H[k], k == 2
+        e = "ext%d" % (k + 1)
+        lu, sv = w("lu", 0, 24), w("sv", 0, 8)
+        sh = w("sh", 2 * k, 2 * k + 2)
+
+        def unpack_b(b):
+            mm(bank(4 + b, 256), *ceb(b), w("bc%d" % k, 0, 256), w("bs%d" % k, 0, 256))
+            if b < 2:
+                copy(bwin(b), bank(4 + b, 256))
+            else:
+                act(bwin(b), bank(4 + b, 256))
+
+        def z_of(b):
+            z, gz = w("zt", b, 4 * C, 4), w("gz", C * (b % 2), C * (b % 2) + C)
+            if b < 2:
+                tt(z, bwin(b), fpw(b), A.subtract, ind=lu)
+            else:
+                act(gz, bwin(b), ind=lu)
+                tt(z, gz, bank(b, C), A.subtract)
+
+        unpack_b(0)
+        z_of(0)
+        unpack_b(2)
+        unpack_b(1)
+        unpack_f(k, (2,))
+        z_of(2)
+        unpack_b(3)
+        unpack_f(k, (3,))
+        z_of(1)
+        z_of(3)
+        for t in range(3):
+            qz, sz = w("qz", 128 * t, 128 * t + 128), w("sz", 128 * t, 128 * t + 128)
+            quant(qz, sz, w("zt", 512 * t, 512 * t + 512))
+            mm(bank(4 + t, 128), qz, sz, w("qua", 0, 128), w("sua", 0, 128))
+            act(w("sc", 64 * t, 64 * t + 64), bank(4 + t, 128, 64))
+        for t in range(3):
+            tt(w("fl", t, 192, 3), bank(4 + t, 64), w("sc", 64 * t, 64 * t + 64), A.is_gt)
+        tt(w("f1", 0, 96), w("fl", 0, 96), w("fl", 96, 192), A.add)
+        tt(w("f2", 0, 96), w("f1", 0, 96), w("sgn", 0, 96), A.mult)
+        tt(w("f3", 0, 48), w("f2", 0, 48), w("f2", 48, 96), A.add)
+        tt(w("rk", 0, 24), w("f3", 0, 24), w("f3", 24, 48), A.add)
+        copy(w("et", 0, 768, 4), w("rk", 0, 32), w("el", 0, 12))
+        act(w("et", 1, 768, 4), w("rk", 0, 32), ind=w("el", 12, 24))
+        quant(w("qe", 0, 192), w("se", 0, 192), w("et", 0, 768))
+        mm(bank(7, 192), w("cc", 128 * k, 128 * k + 128), w("ccs", 128 * k, 128 * k + 128), w("qe", 0, 192), w("se", 0, 192))
+        for b in (2, 3):
+            act(fpw(b), bank(b, C))
+        tt(w("eq", 0, 192), bank(7, 192), w("gk", 0, 192), A.is_equal)
+        tt(w("pr", 0, 192), w("eq", 0, 192), w("lsh", 0, 192), A.mult)
+        tt(w("p1", 0, 96), w("pr", 0, 96), w("pr", 96, 192), A.add)
+        tt(w("p2", 0, 48), w("p1", 0, 48), w("p1", 48, 96), A.add)
+        tt(w(e, 8, 32), w("p2", 0, 24), w("p2", 24, 48), A.add)
+        halo(k + 1)
+        if last:
+            turn(k, -h, 8, 32)
+            for b in range(4):
+                act(w("fh", 64 * b, 64 * b + 32), fpw(b, 0, 32))
+                act(w("fh", 64 * b + 32, 64 * b + 64), fpw(b, 352, 384))
+        if k == 0:
+            fill(w("exo", 0, 48), 0.0)
+            weave(c_seeds)
+            for i in range(1, 4):
+                fill(w("ext%d" % i, 40, 48), 0.0)
+            fill(w("exr", 40, 48), 0.0)
+            for i in (1, 2):
+                ts(w("sh", 2 * i, 2 * i + 2), i2, fc(20 + i), A.add)
+            fill(w("xsd", 256, 512), 0.0)
+        tt(w("exo", 8, 32), w("p2", 0, 24), w("p2", 24, 48), A.add)
+        copy(w("mi", 0, 32), w("exo", 0, 48), sh)
+        a, z = 32 * h, C - 32 * h
+        for b in (0, 2, 1, 3):
+            gather(w("yt", 4 * a + b, 4 * z, 4), b, w("mi", a // 16, z // 16))
+        if k == 0:
+            turner(1)
+        if not last:
+            turn(k, H[k + 1] - h, 0, 40)
+            copy(w("sg", 0, 32), w(e, 0, 48), w("sd", 2 * k, 2 * k + 2))
+            tt(w("sm", 0, 24), w("sg", 0, 24), w("dm", 0, 24), A.mult)
+            tt(w("s1", 0, 8), w("sm", 0, 8), w("sm", 8, 16), A.add)
+            tt(w("s2", 0, 8), w("s1", 0, 8), w("sm", 16, 24), A.add)
+            copy(sv, w("s2", 0, 8))
+            for b in (0, 2, 1, 3):
+                gather(w("ys", b, 512, 4), b, sv)
+            quant(w("qys", 0, 128), w("sys0", 0, 128), w("ys", 0, 512))
+            for b in range(4):
+                mm(bank(b, 128), *wb(b), w("qys", 0, 128), w("sys0", 0, 128))
+                act(w("rs", 64 * b, 64 * b + 64), bank(b, 128, 0, 2), F.Relu)
+            copy(w("mu", 0, 32), w(e, 0, 48), sh)
+            for b in range(4):
+                tt(w("xsd", b, 256, 4), w("rs", 64 * b, 64 * b + 64), w("bp", 256 * b + 64 * rank, 256 * b + 64 * rank + 64), A.add)
+            quant(w("qs%d" % (k + 1), 0, 128), w("ss%d" % (k + 1), 0, 128), w("xsd", 0, 512))
+            seeds(k + 1)
+            for b in (0, 2, 1, 3):
+                gather(w("yt", b, 4 * a, 4), b, w("mu", 0, a // 16))
+                gather(w("yt", 4 * z + b, 4 * C, 4), b, w("mu", z // 16, 24))
+            a, z = 0, C
+        xn, n = "xt%d" % (k + 1), z - a
+        qy, sy = w("qy", a, z), w("sy", a, z)
+        quant(qy, sy, w("yt", 4 * a, 4 * z))
+        for b in range(4):
+            mm(bank(4 + b, n), *ceb(b), w("qx%d" % k, a, z), w("sx%d" % k, a, z), True, False)
+        for b in range(4):
+            mm(bank(4 + b, n), *wb(b), qy, sy, False, True)
+            tt(w(xn, 4 * a + b, 4 * z, 4), bank(4 + b, n), fpw(b, a, z), A.max)
+        if not last:
+            lists(k + 1, "exr")
+        quant(w("qx%d" % (k + 1), a, z), w("sx%d" % (k + 1), a, z), w(xn, 4 * a, 4 * z))
+        if not last:
+            unpack_f(k + 1, (0, 1))
+            fan(k + 1)
+        if k == 0:
+            fill(w("yh", 256, 512), 0.0)
+        if k == 1:
+            quant(w("qv", 0, 128), w("svv", 0, 128), w("vt", 0, 512))
+            ts(it(15, 1), it(0, 1), 2, A.is_ge, 20, A.mult)
+            tt(it(15, 1), it(15, 1), it(0, 1), A.add)
+            ts(w("shh", 0, 1), it(15, 1), fc(22), A.add)
+            turner(2)
+
+    qv, svv = w("qv", 0, 128), w("svv", 0, 128)
+    x3, s3 = w("qx3", 32, 352), w("sx3", 32, 352)
+    mm(bank(4, 320), qv, svv, x3, s3)
+    act(w("yo", 32, 352), bank(4, 320))
+
+    def out_scales(c0, c1, name, a, b):
+        for i in range(4):
+            dma("y", T.osc[4 * i:4 * i + 4, c0:c1], ap(w(name, a, b, 1, 32 * i, 32 * i + 4)), "st", [w(name, a, b)], [])
+
+    copy(w("mh", 0, 16), w("ext3", 0, 48), w("shh", 0, 1))
+    for b in (0, 2, 1, 3):
+        gather(w("yh", b, 256, 4), b, w("mh", 0, 4))
+    quant(w("qys", 0, 128), w("sys0", 0, 128), w("yh", 0, 512))
+    for b in range(4):
+        mm(bank(b, 128), *wb(b), w("qys", 0, 128), w("sys0", 0, 128))
+        act(w("rs", 64 * b, 64 * b + 64), bank(b, 64), F.Relu)
+    for b in range(4):
+        tt(w("xsd", b, 256, 4), w("rs", 64 * b, 64 * b + 64), w("fh", 64 * b, 64 * b + 64), A.add)
+    quant(w("qh", 0, 128), w("sh0", 0, 128), w("xsd", 0, 512))
+    mm(bank(7, 128), qv, svv, w("qh", 0, 128), w("sh0", 0, 128))
+    act(w("yo2", 0, 64), bank(7, 64))
+    pn = w("pi", 0, 24)
+    fill(w("on", 24, 32), 0.0)
+    copy(pn, w("exr", 8, 32))
+    relabel(w("on", 0, 24), pn, 24)
+    op("v", lambda: vec.transpose(ap(w("ot", 0, 32)), ap(w("on", 0, 32))), [w("on", 0, 32)], [w("ot", 0, 32)])
+    dma("y", T.oc[:, 128:1408], ap(x3).bitcast(dt.uint8), "st", [x3], [])
+    out_scales(32, 352, "sx3", 32, 352)
+    dma("y", T.y[:, 32:352], ap(w("yo", 32, 352)), "st", [w("yo", 32, 352)], [])
+    for a, b in ((0, 0), (32, 352)):
+        v = w("qh", a, a + 32)
+        dma("y", T.oc[:, 4 * b:4 * b + 128], ap(v).bitcast(dt.uint8), "st", [v], [])
+        out_scales(b, b + 32, "sh0", a, a + 32)
+        v = w("yo2", a, a + 32)
+        dma("s", T.y[:, b:b + 32], ap(v), "st", [v], [])
+    for m in range(8):
+        v = w("ot", 16 * (m % 2), 16 * (m % 2) + 16, 1, 32 * (m // 2), 32 * (m // 2) + 24)
+        dma("y", T.op[m:m + 1, :], ap(v), "st", [v], [])
+    for sem in SEMAPHORES:
+        if total.get(sem, 0):
+            wait("g", sem, total[sem])

@@ -4,6 +4,7 @@ from concourse.mybir import dt, AluOpType, ActivationFunctionType
 C = 384
 H = [4, 2, 1]
 DC = [0, 1, 1, 1, 0, -1, -1, -1]
+ROT = 128
 
 SCRATCH = {}
 
@@ -19,28 +20,35 @@ for _r in range(4):
     _b("xt%d" % _r, 4 * C, BF)
     _b("qx%d" % _r, C, X4)
     _b("sx%d" % _r, C, U8)
-    _b("ext%d" % _r, 48, F32)
+_b("ext0", 40, I32)
 for _r in range(3):
+    _b("ext%d" % (_r + 1), 192 + 32 * H[_r], BF)
     _b("bc%d" % _r, 256, X4)
     _b("bs%d" % _r, 256, U8)
+    SCRATCH["fan%d" % _r] = ("dram", [16 + 2 * H[_r], 8, 24], BF)
+for _r in (1, 2):
     _b("qs%d" % _r, 128, X4)
     _b("ss%d" % _r, 128, U8)
-    SCRATCH["fan%d" % _r] = ("dram", [48, 8, 24], F32)
-for _n, _c, _t in (("fp", 4 * C, BF), ("bp", 1024, BF), ("gz", 2 * C, BF), ("zt", 4 * C, BF), ("yt", 4 * C, BF), ("ys", 512, BF), ("yh", 512, BF), ("xsd", 512, BF), ("fh", 256, BF),
-                   ("exs", 40, F32), ("exr", 48, F32), ("lf", 32, F32), ("lw", 32, F32), ("lu", 32, U16), ("mi", 32, U16), ("mu", 32, U16), ("sv", 8, U16), ("lsh", 192, F32),
-                   ("qz", C, X4), ("sz", C, U8), ("qy", C, X4), ("sy", C, U8), ("qys", 128, X4), ("sys0", 128, U8), ("qh", 128, X4), ("sh0", 128, U8),
-                   ("sc", 192, F32), ("fl", 192, F32), ("f1", 96, F32), ("f2", 96, F32), ("f3", 48, F32), ("rk", 32, F32), ("exo", 48, F32),
-                   ("et", 768, BF), ("qe", 192, X4), ("se", 192, U8), ("eq", 192, F32), ("pr", 192, F32), ("p1", 96, F32), ("p2", 48, F32),
-                   ("sg", 32, F32), ("sm", 24, F32), ("s1", 8, F32), ("s2", 8, F32), ("rs", 256, F32), ("yo", C, F32), ("yo2", 64, F32), ("mh", 16, U16),
+for _n, _c, _t in (("fp", 4 * C, BF), ("bp", 1024, BF), ("gz", 2 * C, BF), ("zt", 4 * C, BF), ("yt", 4 * C, BF), ("ys", 512, BF), ("xsd", 512, BF),
+                   ("lfw", 64, BF), ("tl", 64, BF), ("tg", 32, BF), ("lf", 32, BF), ("lu", 32, U16), ("mi", 32, U16), ("mu", 32, U16), ("sv", 8, U16), ("lsh", 192, BF),
+                   ("qz", C, X4), ("sz", C, U8), ("qy", C, X4), ("sy", C, U8), ("qys", 128, X4), ("sys0", 128, U8),
+                   ("sc", 192, F32), ("fl", 192, BF), ("rk", 256, BF), ("et", 1056, BF), ("qe", 200, X4), ("se", 200, U8), ("eq", 192, BF), ("pr", 192, BF),
+                   ("sm", 32, BF), ("sn", 24, BF), ("rs", 256, F32), ("yo", C, F32), ("ot", 32, F32),
                    ("ut", 512, BF), ("vt", 512, BF), ("qu", 128, X4), ("suu", 128, U8), ("qua", 128, X4), ("sua", 128, U8), ("qv", 128, X4), ("svv", 128, U8),
-                   ("wq", 512, X4), ("wsc", 512, U8), ("one", 528, BF), ("wd", 528, BF), ("ce", 512, X4), ("cs", 512, U8), ("ct", 1536, BF), ("cc", 384, X4), ("ccs", 384, U8),
-                   ("pi", 28, I32), ("kk", 128, I32), ("pf", 28, F32), ("pd", 12, F32), ("pe", 12, F32),
-                   ("ip", 16, I32), ("i12", 12, I32), ("cl", 32, F32), ("it", 240, I32), ("ul", 8, U16), ("sl", 4, U16), ("sh", 6, U16), ("shh", 2, U16), ("sd", 6, U16), ("el", 24, U16),
-                   ("q0", 128, F32), ("gk", 192, F32), ("sgn", 96, F32), ("dm", 24, F32), ("on", 32, F32), ("ot", 32, F32)):
+                   ("wq", 512, X4), ("wsc", 512, U8), ("wd", 528, BF), ("ce", 512, X4), ("cs", 512, U8), ("ct", 528, BF), ("cc", 768, X4), ("ccs", 768, U8),
+                   ("ci", 8, I32), ("cf", 40, F32), ("dd", 16, F32), ("da", 16, F32), ("io2", 12, F32), ("ib", 4, F32), ("bt", 16, F32), ("tw", 32, F32), ("sw", 12, F32),
+                   ("i64", 64, F32), ("i128", 128, F32), ("eye", 64, BF), ("d24", 24, F32), ("d3", 24, I32), ("d4", 24, F32), ("dm", 32, BF), ("c3", 24, BF),
+                   ("gk", 192, BF), ("sc1", 192, BF), ("c8", 192, BF), ("ls", 96, U16)):
     _b(_n, _c, _t)
 SEMAPHORES = ["kv", "ks", "kt", "kg", "lx", "lp", "lu", "lw", "lv", "st", "loc", "ha0", "ha1", "ha2", "ha3"]
 for _r in range(3):
-    SEMAPHORES += ["se%d" % _r, "ow%d" % _r, "rr%d" % _r, "fw%d" % _r, "fr%d" % _r]
+    SEMAPHORES += ["se%d" % _r, "ow%d" % _r, "fw%d" % _r, "fr%d" % _r]
+
+LISTS, _at = {}, 0
+for _n, _c in (("rows0", 4), ("rows1", 4), ("rows2", 4), ("rows3", 4), ("turn", 6), ("rot", 2), ("seed", 4), ("nat", 4), ("pair", 8), ("spread", 2), ("cand", 12),
+               ("tn0", 8), ("tn1", 8), ("tn2", 8), ("all0", 4), ("all1", 4), ("all2", 4), ("own0", 2), ("own1", 2), ("own2", 2)):
+    LISTS[_n] = (_at, _at + _c)
+    _at += _c
 
 
 def rank_program(g, core, T, topo):
@@ -51,7 +59,7 @@ def rank_program(g, core, T, topo):
     N = len(T.cores)
     vec, sca, ten, syn = g.vector, g.scalar, g.tensor, g.sync
     queue = {"v": vec, "s": sca, "t": ten, "g": g, "y": syn}
-    total, seen, log, hold = {}, {q: {} for q in queue}, {}, []
+    total, seen, log = {}, {q: {} for q in queue}, {}
 
     def w(name, a, b, step=1, p0=0, p1=128):
         return (name, a, b, step, p0, p1)
@@ -96,25 +104,11 @@ def rank_program(g, core, T, topo):
             log.setdefault(v[0], []).append((v, False, q, sem, val, dma))
 
     def op(q, call, reads, writes, acc=False):
-        if hold:
-            hold[-1].append((q, call, reads, writes, acc))
-            return
         order(q, reads, writes, acc, False)
         sem = "k" + q
         total[sem] = total.get(sem, 0) + 1
         call().then_inc(T.sem[sem], 1)
         note(q, reads, writes, sem, total[sem], False)
-
-    def weave(*chains):
-        lists = []
-        for c in chains:
-            hold.append([])
-            c()
-            lists.append(hold.pop())
-        for i in range(max(len(x) for x in lists)):
-            for x in lists:
-                if i < len(x):
-                    op(*x[i])
 
     def dma(q, out, in_, sem, reads, writes, after=()):
         order(q, reads, writes, False, True)
@@ -148,6 +142,12 @@ def rank_program(g, core, T, topo):
         else:
             op("v", lambda: vec.tensor_scalar(ap(out), at(a, ind), n1, n2, o1, o2), rd(a, ind) + more, [out])
 
+    def scan(out, keep, add):
+        op("v", lambda: vec.tensor_tensor_scan(ap(out), ap(keep), ap(add), 0.0, A.mult, A.add), [keep, add], [out])
+
+    def flip(out, in_):
+        op("v", lambda: vec.transpose(ap(out), ap(in_)), [in_], [out])
+
     def fill(out, val):
         op("v", lambda: vec.memset(ap(out), val), [], [out])
 
@@ -157,6 +157,11 @@ def rank_program(g, core, T, topo):
             op("s", lambda: sca.activation(ap(out), at(in_, ind), f), rd(in_, ind), [out])
         else:
             op("s", lambda: sca.activation(ap(out), at(in_, ind), f, scale=scale), rd(in_, ind), [out])
+
+    def lin(out, in_, scale, bias, func=None):
+        col = isinstance(bias, tuple)
+        op("s", lambda: sca.activation(ap(out), ap(in_), F.Identity if func is None else func, bias=ap(bias) if col else float(bias), scale=float(scale)),
+           [in_, bias] if col else [in_], [out])
 
     def quant(q, s, in_):
         op("v", lambda: vec.quantize_mx(ap(q), ap(s), ap(in_)), [in_], [q, s])
@@ -170,9 +175,17 @@ def rank_program(g, core, T, topo):
         else:
             op("g", lambda: g.iota(ap(out), pat, base, cm), [], [out])
 
+    def keep_if(v, pat, cmp, other, src=None):
+        src = v if src is None else src
+        op("g", lambda: g.affine_select(ap(v), ap(src), pat, cmp, other, 0, 0), [src], [v])
+
     def pick(qo, so, qi, si, ind):
         op("v", lambda: vec.tensor_copy(ap(qo).bitcast(dt.uint32), ap(qi).bitcast(dt.uint32).indirect(ap(ind))), [qi, ind], [qo])
         act(so, si, ind=ind)
+
+    def L(name, a=0, b=None):
+        s, e = LISTS[name]
+        return w("ls", s + a, e if b is None else s + b)
 
     up, down = (rank - 1) % N, (rank + 1) % N
     others = [r for r in range(N) if r != rank]
@@ -189,151 +202,117 @@ def rank_program(g, core, T, topo):
         total["loc"] = total.get("loc", 0) + sum(bin(m).count("1") for _, m, _, _, _ in trs)
         g.remote_dma_fused([RemoteDMATransfer(dst_ids=ids, dma_engine_mask=m, remote_sem=T.sem[sem], srcs=[src], dsts=dsts) for ids, m, sem, src, dsts in trs], local_sem=T.sem["loc"])
 
-    def halo(k):
+    def halo(k, n, m):
         e, s = "ext%d" % k, "ha%d" % k
         eu, ed = topo.engines(core, T.cores[up]), topo.engines(core, T.cores[down])
         hu, hd = eu[:len(eu) // 2], ed[len(ed) // 2:]
-        lo, hi = w(e, 8, 16), w(e, 24, 32)
-        fused([([dst(up)], bits(hu), s, ap(lo), [ap(w(e, 32, 40))]), ([dst(down)], bits(hd), s, ap(hi), [ap(w(e, 0, 8))])], [lo, hi])
-        arrive(w(e, 0, 8), s, len(hu) + len(hd))
-        arrive(w(e, 32, 40), s, len(hu) + len(hd))
+        lo, hi, top, low = w(e, n, 2 * n), w(e, m, m + n), w(e, 0, n), w(e, n + m, 2 * n + m)
+        fused([([dst(up)], bits(hu), s, ap(lo), [ap(low)]), ([dst(down)], bits(hd), s, ap(hi), [ap(top)])], [lo, hi])
+        arrive(top, s, len(hu) + len(hd))
+        arrive(low, s, len(hu) + len(hd))
 
     def seeds(k):
         m = bits(topo.engines(core, T.cores[others[0]]))
         ids = [dst(r) for r in others]
         a, b = 64 * rank, 64 * rank + 64
-        q, s, bq, bs = w("qs%d" % k, 0, 64), w("ss%d" % k, 0, 64), w("bc%d" % k, a, b), w("bs%d" % k, a, b)
+        bq, bs = w("bc%d" % k, a, b), w("bs%d" % k, a, b)
+        q, s = (bq, bs) if k == 0 else (w("qs%d" % k, 0, 64), w("ss%d" % k, 0, 64))
         fused([(ids, m, "se%d" % k, ap(q).bitcast(dt.uint8), [ap(bq).bitcast(dt.uint8) for r in others])], [q])
         fused([(ids, m, "se%d" % k, ap(s), [ap(bs) for r in others])], [s])
-        dma("y", ap(bq).bitcast(dt.uint8), ap(q).bitcast(dt.uint8), "ow%d" % k, [q], [bq])
-        dma("y", ap(bs), ap(s), "ow%d" % k, [s], [bs])
+        if k:
+            dma("y", ap(bq).bitcast(dt.uint8), ap(q).bitcast(dt.uint8), "ow%d" % k, [q], [bq])
+            dma("y", ap(bs), ap(s), "ow%d" % k, [s], [bs])
         n = 2 * len(others) * bin(m).count("1")
         for r in others:
             arrive(w("bc%d" % k, 64 * r, 64 * r + 64), "se%d" % k, n)
             arrive(w("bs%d" % k, 64 * r, 64 * r + 64), "se%d" % k, n)
 
-    def turned(s):
-        for m in range(8):
-            d = s * DC[m]
-            if d == 0:
-                yield m, 0, 16, 0, False
-            elif d > 0:
-                yield m, 0, 16 - d, d, False
-                yield m, 16 - d, 16, 0, True
-            else:
-                yield m, -d, 16, 0, False
-                yield m, 0, -d, 16 + d, True
+    cut = 4 * (C - ROT)
+    dma("s", ap(w("ext0", 8, 32)), T.p[:, :], "lp", [], [w("ext0", 8, 32)])
+    dma("y", ap(w("xt0", 0, cut)), T.x[:, 4 * ROT:4 * C], "lx", [], [w("xt0", 0, cut)])
+    dma("y", ap(w("xt0", cut, 4 * C)), T.x[:, 0:4 * ROT], "lx", [], [w("xt0", cut, 4 * C)])
 
-    dma("y", ap(w("xt0", 0, 4 * C)), T.x[:, :], "lx", [], [w("xt0", 0, 4 * C)])
-    for m, a, b, o, _ in turned(H[0]):
-        v = w("pi", 0, 24, 1, 16 * m + a, 16 * m + b)
-        dma("s", ap(v), T.p[16 * m + o:16 * m + o + b - a, :], "lp", [], [v])
-    dma("y", ap(w("ut", 0, 512)), T.u[:, :], "lu", [], [w("ut", 0, 512)])
-    dma("y", ap(w("wq", 0, 512)).bitcast(dt.uint8), T.wc[:, :], "lw", [], [w("wq", 0, 512)])
-    dma("y", ap(w("wsc", 0, 512)), T.ws[:, :], "lw", [], [w("wsc", 0, 512)])
-    dma("y", ap(w("vt", 0, 512)), T.v[:, :], "lv", [], [w("vt", 0, 512)])
+    def fc(i, n=1):
+        return w("cf", i, i + n)
 
-    def ic(i):
-        return w("ip", i, i + 1)
+    Q, LO, L3, C31, O1, P, G16, H8, B32, X64, PM8, Q6, HL, HI, LO16, E0, LH, Q16, GF, TMP = [fc(i) for i in range(20)]
+    X7, EL = fc(20, 3), fc(24, 2)
+    DR, D2, DROW = w("dd", 0, 1), w("dd", 1, 3), w("dd", 3, 11)
+    io2 = lambda n: w("io2", 0, n)
 
-    def fc(i):
-        return w("cl", i, i + 1)
+    iota(w("ci", 5, 6), [[0, 1]], 0, 1)
+    iota(w("ci", 6, 7), [[0, 1]], 0, 3)
+    iota(io2(12), [[2, 12]], 0, 0)
+    iota(w("ib", 0, 4), [[-8, 2], [16, 2]], 8, 1)
+    iota(w("i128", 0, 128), [[1, 128]], 0, 0)
+    iota(w("i64", 0, 64), [[0, 2], [-16, 2], [1, 16]], 16, 0)
+    halo(0, 8, 24)
 
-    def it(i, n):
-        return w("it", 12 * i, 12 * i + n)
+    fill(w("wd", 0, 516), 0.0)
+    ts(w("ci", 0, 1), w("ci", 5, 6), 15, A.bitwise_and)
+    ts(w("ci", 3, 4), w("ci", 5, 6), 31, A.bitwise_and)
+    ts(w("ci", 4, 5), w("ci", 5, 6), 1, A.bitwise_and)
+    ts(w("ci", 1, 3), w("ci", 5, 7), 7, A.bitwise_and)
+    copy(fc(0, 6), w("ci", 0, 6))
+    lin(w("da", 3, 11), io2(8), 0.5, -2, F.Abs)
+    lin(Q6, Q, 6, 0)
+    lin(G16, P, -1, Q)
+    lin(B32, C31, -1, P)
+    lin(H8, LO, -1, Q)
+    lin(w("da", 0, 1), G16, -0.0625, -4, F.Abs)
+    lin(w("da", 1, 2), B32, 0.0625, -2, F.Abs)
+    lin(w("da", 2, 3), B32, 0.0625, -1, F.Abs)
+    lin(PM8, O1, -16, 8)
+    lin(Q16, Q, 1, 16)
 
-    P, GI, QI = ic(0), ic(1), ic(2)
-    GF, QF, G16, DR1, CAR, DEL, GX = [fc(i) for i in range(7)]
-    idx, i4, i2 = it(0, 12), it(0, 4), it(0, 2)
-
-    fill(w("one", 0, 515), 1.0)
-    iota(P, [[0, 1]], 0, 1)
-    iota(w("i12", 0, 12), [[16, 12]], 0, 1)
-    op("g", lambda: g.affine_select(ap(w("wd", 0, 515)), ap(w("one", 0, 515)), [[-1, 515]], A.is_equal, 0.0, 3, 4), [w("one", 0, 515)], [w("wd", 0, 515)])
-    iota(w("sgn", 0, 96), [[2, 4], [-1, 8], [0, 3]], 0, 0)
-    iota(w("gk", 0, 192), [[-1, 8], [0, 24]], 0, 0)
-    iota(w("q0", 0, 128), [[0, 8], [1, 16]], 0, 0)
-    iota(w("ct", 0, 512), [[0, 512]], 0, 0)
-
-    ts(GI, P, 4, A.arith_shift_right)
-    ts(QI, P, 15, A.bitwise_and)
-    copy(GF, GI)
-    copy(QF, QI)
-    ts(G16, GF, -16.0, A.mult)
-    ts(idx, w("i12", 0, 12), G16, A.add)
-
-    def c_rows():
-        ts(fc(8), GF, 2.0, A.is_ge)
-        ts(fc(9), GF, 3.0, A.is_ge, fc(8), A.add)
-        tt(DR1, fc(9), fc(11), A.subtract)
-        for i, h in enumerate(H):
-            ts(fc(20 + i), DR1, 2.0 * h, A.mult, 8.0 - 2.0 * h, A.add)
-        ts(w("sh", 0, 2), i2, fc(20), A.add)
-
-    def c_rows2():
-        ts(fc(10), GF, 6.0, A.is_ge)
-        ts(fc(11), GF, 7.0, A.is_ge, fc(10), A.add)
-
-    def c_carry():
-        ts(fc(12), GF, 4.0, A.is_ge)
-        ts(fc(13), GF, 1.0, A.is_ge, fc(12), A.subtract)
-        ts(fc(15), GF, 5.0, A.is_ge)
-        ts(fc(14), QF, float(16 - H[0]), A.is_ge, fc(13), A.mult)
-        ts(fc(16), QF, float(H[0]), A.is_lt, fc(15), A.mult)
-        tt(CAR, fc(14), fc(16), A.add)
-
-    def c_pairs():
-        ts(it(1, 4), i4, 3, A.arith_shift_right, 3, A.bitwise_and)
-        ts(it(2, 4), i4, 5, A.arith_shift_right)
-        ts(it(3, 4), i4, 7, A.bitwise_and)
-        ts(it(1, 4), it(1, 4), 2, A.mult)
-        tt(it(1, 4), it(1, 4), it(2, 4), A.add)
-        tt(it(4, 4), it(1, 4), it(3, 4), A.max)
-        tt(w("it", 52, 56), it(1, 4), it(3, 4), A.min)
-        ts(w("ul", 0, 8), it(4, 8), 16, A.mult)
-
-    def c_half():
-        ts(ic(3), GI, 1, A.bitwise_and)
-        ts(fc(7), ic(3), -2.0, A.mult, 1.0, A.add)
-        tt(GX, fc(7), GF, A.add)
-
-    c_rows2()
-    weave(c_rows, c_carry, c_half)
-
-    def relabel(out, p, n):
-        k = [w("kk", 32 * i, 32 * i + n) for i in range(4)]
-        ts(k[0], p, 7, A.bitwise_and)
-        ts(k[1], k[0], 3, A.mult)
-        ts(k[2], k[1], 7, A.bitwise_and)
-        tt(k[3], k[2], k[0], A.subtract)
-        tt(out, k[3], p, A.add)
-
-    def c_pointers():
-        copy(w("pi", 24, 28), i4)
-        relabel(w("pf", 0, 28), w("pi", 0, 28), 28)
-        tt(w("pd", 0, 12), w("pf", 1, 24, 2), w("pf", 0, 24, 2), A.subtract)
-        ts(w("sl", 0, 4), w("pf", 24, 28), 6.0, A.mult)
-        ts(w("pe", 0, 12), w("pd", 0, 12), CAR, A.mult)
-        tt(w("ext0", 8, 32, 2), w("pf", 0, 24, 2), w("pe", 0, 12), A.add)
-        tt(w("ext0", 9, 32, 2), w("pf", 1, 24, 2), w("pe", 0, 12), A.subtract)
-
-    weave(c_pointers, c_pairs)
-    halo(0)
-
-    quant(w("qx0", 0, C), w("sx0", 0, C), w("xt0", 0, 4 * C))
-    pick(w("qs0", 0, 64), w("ss0", 0, 64), w("qx0", 0, C), w("sx0", 0, C), w("sl", 0, 4))
-    seeds(0)
-    iota(w("et", 0, 768), [[0, 768]], 0, 0)
-    iota(w("dm", 0, 24), [[1, 3], [0, 8]], 0, 0)
-    iota(w("ct", 512, 1536), [[0, 1024]], 0, 0)
-    for b in range(4):
-        quant(w("ce", 128 * b, 128 * b + 128), w("cs", 128 * b, 128 * b + 128), w("wd", 3 - b, 515 - b))
-
-    def bank(b, n, a=0, step=1):
-        return w("ps%d" % b, a, n, step)
+    ts(w("sw", 0, 4), io2(4), 48.0, A.mult, Q6, A.add)
+    ts(w("wd", 3, 515, 4), w("i128", 0, 128), P, A.is_equal)
+    ts(w("sw", 4, 8), w("sw", 0, 4), float(ROT), A.is_lt, float(C), A.mult)
+    ts(w("bt", 8, 12), w("ib", 0, 4), G16, A.add, 8.0, A.mult)
+    tt(w("sw", 8, 12), w("sw", 0, 4), w("sw", 4, 8), A.add)
+    ts(w("bt", 12, 16), w("bt", 8, 12), 192.0, A.is_ge, -192.0, A.mult)
+    ts(L("seed"), w("sw", 8, 12), -float(ROT), A.add)
+    tt(w("bt", 0, 4), w("bt", 8, 12), w("bt", 12, 16), A.add)
+    ts(w("da", 0, 11), w("da", 0, 11), -1.0, A.mult, 2.0, A.add)
+    ts(w("eye", 0, 64), w("i64", 0, 64), C31, A.is_equal)
+    ts(w("dd", 0, 11), w("da", 0, 11), -1.0, A.max, 1.0, A.min)
+    fill(w("ct", 512, 516), 0.0)
+    lin(w("bt", 4, 6), w("bt", 2, 4), 1, PM8)
+    lin(HI, H8, 2, 0)
+    lin(LO16, LO, 16, 0)
+    lin(w("sw", 0, 4), io2(4), 16, HI)
+    lin(X64, DR, 64, 64)
+    for i, s in enumerate((H[0], H[1] - H[0], -1)):
+        lin(w("tw", 2 * i, 2 * i + 2), D2, s, Q)
 
     def ceb(b):
         return w("ce", 128 * b, 128 * b + 128), w("cs", 128 * b, 128 * b + 128)
+
+    quant(*ceb(0), w("wd", 3, 515))
+    ts(L("tn0"), DROW, float(H[0]), A.mult, Q16, A.add)
+    ts(L("tn1"), DROW, float(H[1]), A.mult, Q16, A.add)
+
+    quant(w("qx0", 0, C), w("sx0", 0, C), w("xt0", 0, 4 * C))
+    pick(w("bc0", 64 * rank, 64 * rank + 64), w("bs0", 64 * rank, 64 * rank + 64), w("qx0", 0, C), w("sx0", 0, C), L("seed"))
+    seeds(0)
+    dma("y", ap(w("ut", 0, 512)), T.u[:, :], "lu", [], [w("ut", 0, 512)], ["lx"])
+    dma("y", ap(w("wq", 0, 512)).bitcast(dt.uint8), T.wc[:, :], "lw", [], [w("wq", 0, 512)])
+    dma("y", ap(w("wsc", 0, 512)), T.ws[:, :], "lw", [], [w("wsc", 0, 512)])
+    iota(w("et", 0, 800), [[0, 800]], 0, 0)
+    iota(w("rk", 192, 256), [[0, 64]], 0, 0)
+    iota(w("c8", 0, 192), [[0, 192]], 1, 0)
+    keep_if(w("sc1", 0, 192), [[0, 3], [1, 8], [-1, 8]], A.not_equal, -1.0, w("c8", 0, 192))
+    keep_if(w("sc1", 0, 192), [[0, 24], [1, 8]], A.is_gt, 0.0)
+    keep_if(w("c8", 0, 192), [[0, 24], [1, 8]], A.is_gt, 0.0)
+    iota(w("gk", 0, 192), [[0, 24], [-1, 8]], 0, 0)
+    iota(w("d24", 0, 24), [[0, 8], [1, 3]], 0, 1)
+    iota(w("c3", 0, 24), [[0, 24]], 1, 0)
+    keep_if(w("c3", 0, 24), [[0, 8], [1, 3]], A.is_gt, 0.0)
+    iota(w("dm", 24, 32), [[0, 8]], 0, 0)
+    iota(w("xsd", 256, 512), [[0, 256]], 0, 0)
+
+    def bank(b, n, a=0, step=1):
+        return w("ps%d" % b, a, n, step)
 
     def fpw(b, a=0, e=C):
         return w("fp", C * b + a, C * b + e)
@@ -344,84 +323,103 @@ def rank_program(g, core, T, topo):
             if b < 2:
                 act(fpw(b), bank(b, C))
 
+    def turner(i):
+        for e in range(2):
+            act(w("ct", 2 * (i % 2) + e, 512, 4), w("eye", 16 * e, 16 * e + 48), ind=L("tn%d" % i))
+
+    def ccw(i, e):
+        a = 256 * i + 128 * e
+        return w("cc", a, a + 128), w("ccs", a, a + 128)
+
+    def turner_q(i):
+        for e in range(2):
+            o = 2 * (i % 2) + e
+            quant(*ccw(i, e), w("ct", o, o + 512))
+
+    ts(w("tw", 8, 14), w("tw", 0, 6), 0.0, A.is_lt, 48.0, A.mult)
+    ts(w("tw", 16, 22), w("tw", 0, 6), 16.0, A.is_ge, 16.0, A.mult)
+    ts(L("rows0"), w("bt", 2, 6), X64, A.add, 0.125, A.mult)
+    tt(w("tw", 8, 14), w("tw", 8, 14), w("tw", 16, 22), A.add)
+    ts(L("rot"), w("bt", 0, 2), 0.125, A.mult)
+    tt(w("tw", 24, 30), w("tw", 8, 14), w("tw", 0, 6), A.add)
+    for b in (1, 2, 3):
+        quant(*ceb(b), w("wd", 3 - b, 515 - b))
+    t0 = LISTS["turn"][0]
+    copy(w("ls", t0, t0 + 6, 2), w("tw", 24, 30, 2))
+    ts(w("ls", t0 + 1, t0 + 6, 2), w("tw", 25, 30, 2), 16.0, A.add)
     unpack_f(0, (0, 1))
+    turner(0)
+    turner(1)
+    ts(L("pair", 0, 4), w("sw", 0, 4), LO16, A.max)
+    ts(L("pair", 4, 8), w("sw", 0, 4), LO16, A.min)
 
-    def lists(k, src):
-        copy(w("lf", 0, 32), w(src, 0, 48), w("sh", 2 * k, 2 * k + 2))
-        copy(w("lu", 0, 32), w("lf", 0, 32))
+    def rows(k, src, on):
+        if on == "v":
+            copy(w("lfw", 0, 64), src, L("rows%d" % k))
+        else:
+            act(w("lfw", 0, 64), src, ind=L("rows%d" % k))
 
-    def fan(k):
-        t = T["fan%d" % k]
-        act(w("lw", 0, 24, 2), w("lf", 1, 24, 2))
-        act(w("lw", 1, 24, 2), w("lf", 0, 24, 2))
-        for j, n in ((1, "lf"), (0, "lw"), (2, "lw")):
-            for m in range(8):
-                v = w(n, 0, 24, 1, 16 * m, 16 * m + 16)
-                dma("y", t[16 * j:16 * j + 16, m, :], ap(v), "fw%d" % k, [v], [])
+    def turn(k, on):
+        j = min(k, 2)
+        flip(w("tl", 0, 64), w("lfw", 0, 64))
+        out = w("ot" if k == 3 else "tg", 0, 32)
+        if on == "v":
+            copy(out, w("tl", 0, 64), L("turn", 2 * j, 2 * j + 2))
+        else:
+            act(out, w("tl", 0, 64), ind=L("turn", 2 * j, 2 * j + 2))
+
+    def turn_back():
+        flip(w("lf", 0, 32), w("tg", 0, 32))
+        copy(w("lu", 0, 32), w("lf", 0, 32), L("rot"))
+
+    def fan_out(k):
+        t, h = T["fan%d" % k], H[k]
+        for m in range(8):
+            d = (h - (H[k - 1] if k else 0)) * DC[m]
+            for lo, hi, col in ((-16, 0, 32), (0, 16, 0), (16, 32, 32)):
+                a, b = max(lo, d - h), min(hi, 16 + d + h)
+                if a < b:
+                    v = w("lfw", col, col + 24, 1, 16 * m + a - lo, 16 * m + b - lo)
+                    dma("y", t[a - d + h:b - d + h, m, :], ap(v), "fw%d" % k, [v], [])
+
+    def fan_in(k):
+        t, h = T["fan%d" % k], H[k]
         for m in range(8):
             o = w("lsh", 0, 192, 1, 16 * m, 16 * m + 16)
-            a = 16 + H[k] * DC[m]
+            a = h + h * DC[m]
             dma("y", ap(o), t[a:a + 16, :, :], "fr%d" % k, [], [o], ["fw%d" % k])
 
-    def turn(k, s, a, b):
-        e = "ext%d" % (k + 1)
-        act(w("exs", a, b, 2), w(e, a + 1, b, 2))
-        act(w("exs", a + 1, b, 2), w(e, a, b, 2))
-        for m, p, q, o, swap in turned(s):
-            v, d = w("exs" if swap else e, a, b, 1, 16 * m + o, 16 * m + o + q - p), w("exr", a, b, 1, 16 * m + p, 16 * m + q)
-            dma("y", ap(d), ap(v), "rr%d" % k, [v], [d])
-
+    rows(0, w("ext0", 0, 40), "v")
+    fan_out(0)
+    fan_in(0)
+    dma("y", ap(w("vt", 0, 512)), T.v[:, :], "lv", [], [w("vt", 0, 512)])
+    turn(0, "v")
+    turn_back()
     quant(w("qu", 0, 128), w("suu", 0, 128), w("ut", 0, 512))
-    pick(w("qua", 0, 128), w("sua", 0, 128), w("qu", 0, 128), w("suu", 0, 128), w("ul", 0, 8))
-    fill(w("ext0", 40, 48), 0.0)
+    pick(w("qua", 0, 128), w("sua", 0, 128), w("qu", 0, 128), w("suu", 0, 128), L("pair"))
+    lin(TMP, B32, 2, 32)
+    lin(LH, H8, 0.125, 0)
+    lin(E0, LO, 4, TMP)
+    lin(LH, LO, 24, LH)
+    lin(fc(25), H8, 96, E0)
+    lin(TMP, E0, 1, 256)
+    lin(GF, G16, -0.0625, 0)
+    lin(fc(24), H8, 32, TMP)
+    lin(HL, H8, 1, L3)
+    for i, h in enumerate(H):
+        lin(fc(20 + i), DR, 16 * h, 7)
+    turner_q(0)
+    copy(L("spread"), EL)
+    ts(L("cand"), io2(12), LH, A.add)
 
-    def c_spread():
-        n = [it(i, 12) for i in range(6, 13)]
-        ts(n[0], idx, 171, A.mult)
-        ts(n[0], n[0], 12, A.arith_shift_right)
-        ts(n[1], n[0], -24, A.mult)
-        tt(n[1], n[1], idx, A.add)
-        ts(n[2], n[1], 3, A.arith_shift_right)
-        ts(n[3], n[1], 7, A.bitwise_and)
-        ts(n[4], n[0], 3, A.mult, -24, A.add)
-        tt(n[4], n[4], n[2], A.add)
-        ts(n[5], n[3], GF, A.is_equal)
-        ts(n[6], n[3], GX, A.is_equal)
-        tt(n[5], n[5], n[4], A.mult)
-        tt(n[6], n[6], n[4], A.mult)
-        ts(w("el", 0, 12), n[5], 24, A.add)
-        ts(w("el", 12, 24), n[6], 24, A.add)
-
-    def c_misc():
-        ts(w("sgn", 0, 96), w("sgn", 0, 96), 0.0, A.is_ge, 2.0, A.mult)
-        ts(w("gk", 0, 192), w("gk", 0, 192), GF, A.add)
-        ts(w("sgn", 0, 96), w("sgn", 0, 96), -1.0, A.add)
-        fill(w("rk", 24, 32), 0.0)
-
-    def turner(i):
+    def row_lists(i):
         h = H[i]
-        for (g0, g1, d, e) in ((0, 1, 0, 0), (1, 4, h, 0), (1, 4, h - 16, 1), (4, 5, 0, 0), (5, 8, -h, 0), (5, 8, 16 - h, 1)):
-            ts(w("ct", 512 * i + 64 * g0 + e, 512 * i + 64 * g1, 4), w("q0", 16 * g0, 16 * g1), float(d), A.add, QF, A.is_equal)
-        quant(w("cc", 128 * i, 128 * i + 128), w("ccs", 128 * i, 128 * i + 128), w("ct", 512 * i, 512 * i + 512))
-
-    def c_seeds():
-        ts(ic(4), P, 15, A.bitwise_and, 1, A.arith_shift_right)
-        ts(it(13, 2), i2, 7, A.bitwise_and)
-        ts(ic(5), ic(4), 11, A.mult)
-        ts(it(14, 2), i2, 3, A.arith_shift_right)
-        ts(ic(5), ic(5), 5, A.arith_shift_right)
-        ts(it(13, 2), it(13, 2), 3, A.mult)
-        ts(ic(5), ic(5), -3, A.mult)
-        tt(it(13, 2), it(13, 2), it(14, 2), A.add)
-        tt(DEL, ic(5), ic(4), A.add)
-        for i in range(2):
-            ts(w("sd", 2 * i, 2 * i + 2), it(13, 2), fc(20 + i), A.add)
-        ts(w("dm", 0, 24), w("dm", 0, 24), DEL, A.is_equal)
-
-    weave(c_spread, c_misc)
-    lists(0, "ext0")
-    fan(0)
-    turner(0)
+        ts(L("own%d" % i), w("bt", 0, 2), fc(20 + i), A.add, 191.0, A.min)
+        ts(L("all%d" % i), w("bt", 0, 4), fc(20 + i), A.add, 16.0 * h, A.add)
+        if i < 2:
+            ts(L("rows%d" % (i + 1)), w("bt", 2, 6), fc(21 + i), A.add, 16.0 * h, A.add)
+        else:
+            ts(L("rows3"), w("bt", 2, 6), 7.0, A.add)
 
     def bwin(b):
         return w("bp", 256 * b, 256 * b + 256)
@@ -429,17 +427,56 @@ def rank_program(g, core, T, topo):
     def wb(b):
         return w("wq", 128 * b, 128 * b + 128), w("wsc", 128 * b, 128 * b + 128)
 
-    def gather(out, b, ind):
-        if b < 2:
-            ts(out, bwin(b), 0.015625, A.mult, ind=ind)
-        else:
-            act(out, bwin(b), scale=0.015625, ind=ind)
+    def gather(lst, a, z, bs, on):
+        for b in bs:
+            out, ind = w("yt", 64 * a + b, 64 * z, 4), w(lst, a, z)
+            if on == "v":
+                ts(out, bwin(b), 0.015625, A.mult, ind=ind)
+            else:
+                act(out, bwin(b), scale=0.015625, ind=ind)
+
+    def add_f(k, a, z, b0):
+        for b in range(4):
+            mm(bank(b0 + b, z - a), *ceb(b), w("qx%d" % k, a, z), w("sx%d" % k, a, z), True, False)
+
+    def layer(k, a, z, b0):
+        qy, sy = w("qy", a, z), w("sy", a, z)
+        quant(qy, sy, w("yt", 4 * a, 4 * z))
+        for b in range(4):
+            mm(bank(b0 + b, z - a), *wb(b), qy, sy, False, True)
+
+    def new_x(k, a, z, b0):
+        for b in range(4):
+            tt(w("xt%d" % (k + 1), 4 * a + b, 4 * z, 4), bank(b0 + b, z - a), fpw(b, a, z), A.max)
+
+    def quant_x(k, a, z):
+        quant(w("qx%d" % k, a, z), w("sx%d" % k, a, z), w("xt%d" % k, 4 * a, 4 * z))
+
+    def runs(a, z):
+        for lo, hi, d in ((0, C - ROT, ROT), (C - ROT, C, ROT - C)):
+            if max(a, lo) < min(z, hi):
+                yield max(a, lo), min(z, hi), max(a, lo) + d
+
+    def put_codes(a, z):
+        for s, e, o in runs(a, z):
+            v = w("qx3", s, e)
+            dma("y", T.oc[:, 4 * o:4 * (o + e - s)], ap(v).bitcast(dt.uint8), "st", [v], [])
+            for i in range(4):
+                dma("y", T.osc[4 * i:4 * i + 4, o:o + e - s], ap(w("sx3", s, e, 1, 32 * i, 32 * i + 4)), "st", [w("sx3", s, e)], [])
+
+    def put_y(a, z, b):
+        mm(bank(b, z - a), w("qv", 0, 128), w("svv", 0, 128), w("qx3", a, z), w("sx3", a, z))
+        act(w("yo", a, z), bank(b, z - a))
+        for s, e, o in runs(a, z):
+            dma("s", T.y[:, o:o + e - s], ap(w("yo", s, e)), "st", [w("yo", s, e)], [])
 
     for k in range(3):
         h, last = H[k], k == 2
-        e = "ext%d" % (k + 1)
+        e, n = "ext%d" % (k + 1), 16 * h
+        own, whole = w(e, n, n + 192), w(e, 0, 2 * n + 192)
         lu, sv = w("lu", 0, 24), w("sv", 0, 8)
-        sh = w("sh", 2 * k, 2 * k + 2)
+        a1, a2 = 16 - 2 * h, 16 + 2 * h
+        mid = 16 * a1
 
         def unpack_b(b):
             mm(bank(4 + b, 256), *ceb(b), w("bc%d" % k, 0, 256), w("bs%d" % k, 0, 256))
@@ -456,14 +493,13 @@ def rank_program(g, core, T, topo):
                 act(gz, bwin(b), ind=lu)
                 tt(z, gz, bank(b, C), A.subtract)
 
+        unpack_f(k, (2, 3))
         unpack_b(0)
-        z_of(0)
         unpack_b(2)
         unpack_b(1)
-        unpack_f(k, (2,))
+        z_of(0)
         z_of(2)
         unpack_b(3)
-        unpack_f(k, (3,))
         z_of(1)
         z_of(3)
         for t in range(3):
@@ -471,128 +507,93 @@ def rank_program(g, core, T, topo):
             quant(qz, sz, w("zt", 512 * t, 512 * t + 512))
             mm(bank(4 + t, 128), qz, sz, w("qua", 0, 128), w("sua", 0, 128))
             act(w("sc", 64 * t, 64 * t + 64), bank(4 + t, 128, 64))
+        if k == 0:
+            lin(w("gk", 0, 192), w("gk", 0, 192), 1, GF)
+            quant(w("qe", 0, 200), w("se", 0, 200), w("et", 0, 800))
         for t in range(3):
-            tt(w("fl", t, 192, 3), bank(4 + t, 64), w("sc", 64 * t, 64 * t + 64), A.is_gt)
-        tt(w("f1", 0, 96), w("fl", 0, 96), w("fl", 96, 192), A.add)
-        tt(w("f2", 0, 96), w("f1", 0, 96), w("sgn", 0, 96), A.mult)
-        tt(w("f3", 0, 48), w("f2", 0, 48), w("f2", 48, 96), A.add)
-        tt(w("rk", 0, 24), w("f3", 0, 24), w("f3", 24, 48), A.add)
-        copy(w("et", 0, 768, 4), w("rk", 0, 32), w("el", 0, 12))
-        act(w("et", 1, 768, 4), w("rk", 0, 32), ind=w("el", 12, 24))
-        quant(w("qe", 0, 192), w("se", 0, 192), w("et", 0, 768))
-        mm(bank(7, 192), w("cc", 128 * k, 128 * k + 128), w("ccs", 128 * k, 128 * k + 128), w("qe", 0, 192), w("se", 0, 192))
+            tt(w("fl", 64 * t, 64 * t + 64), bank(4 + t, 64), w("sc", 64 * t, 64 * t + 64), A.is_gt)
+        scan(w("rk", 0, 192), w("sc1", 0, 192), w("fl", 0, 192))
+        src, et = w("rk", 7, 256, 8), w("et", 0, 1056)
+        op("v", lambda: vec.tensor_copy(ap(et).indirect(ap(L("spread"))), ap(src)), [src, L("spread")], [et])
+        quant(w("qe", 8, 192), w("se", 8, 192), w("et", 32, 768))
+        mm(bank(7, 192), *ccw(k, 0), w("qe", 8, 200), w("se", 8, 200), True, False)
+        mm(bank(7, 192), *ccw(k, 1), w("qe", 0, 192), w("se", 0, 192), False, True)
         for b in (2, 3):
             act(fpw(b), bank(b, C))
+        row_lists(k)
         tt(w("eq", 0, 192), bank(7, 192), w("gk", 0, 192), A.is_equal)
-        tt(w("pr", 0, 192), w("eq", 0, 192), w("lsh", 0, 192), A.mult)
-        tt(w("p1", 0, 96), w("pr", 0, 96), w("pr", 96, 192), A.add)
-        tt(w("p2", 0, 48), w("p1", 0, 48), w("p1", 48, 96), A.add)
-        tt(w(e, 8, 32), w("p2", 0, 24), w("p2", 24, 48), A.add)
-        halo(k + 1)
-        if last:
-            turn(k, -h, 8, 32)
-            for b in range(4):
-                act(w("fh", 64 * b, 64 * b + 32), fpw(b, 0, 32))
-                act(w("fh", 64 * b + 32, 64 * b + 64), fpw(b, 352, 384))
+        tt(w("pr", 0, 192), w("lsh", 0, 192), w("eq", 0, 192), A.mult, ind=L("cand"))
+        scan(own, w("c8", 0, 192), w("pr", 0, 192))
+        halo(k + 1, n, 192)
+        add_f(k, 0, mid, 4)
+        copy(w("mi", 0, 32), own, L("own%d" % k))
+        gather("mi", 0, a1, (0, 1), "v")
+        gather("mi", 0, a1, (2, 3), "s")
+        if a2 < 24:
+            gather("mi", a2, 24, range(4), "s")
+        layer(k, 0, mid, 4)
         if k == 0:
-            fill(w("exo", 0, 48), 0.0)
-            weave(c_seeds)
-            for i in range(1, 4):
-                fill(w("ext%d" % i, 40, 48), 0.0)
-            fill(w("exr", 40, 48), 0.0)
-            for i in (1, 2):
-                ts(w("sh", 2 * i, 2 * i + 2), i2, fc(20 + i), A.add)
-            fill(w("xsd", 256, 512), 0.0)
-        tt(w("exo", 8, 32), w("p2", 0, 24), w("p2", 24, 48), A.add)
-        copy(w("mi", 0, 32), w("exo", 0, 48), sh)
-        a, z = 32 * h, C - 32 * h
-        for b in (0, 2, 1, 3):
-            gather(w("yt", 4 * a + b, 4 * z, 4), b, w("mi", a // 16, z // 16))
-        if k == 0:
-            turner(1)
+            ts(w("d3", 0, 24), w("d24", 0, 24), G16, A.add, 0.33333334, A.mult)
+            ts(L("nat"), io2(4), 8.0, A.mult, HL, A.add)
+            ts(w("d4", 0, 24), w("d3", 0, 24), 3.0, A.mult, G16, A.subtract)
+            tt(w("dm", 0, 24), w("d4", 0, 24), w("d24", 0, 24), A.is_equal)
+        new_x(k, 0, mid, 4)
         if not last:
-            turn(k, H[k + 1] - h, 0, 40)
-            copy(w("sg", 0, 32), w(e, 0, 48), w("sd", 2 * k, 2 * k + 2))
-            tt(w("sm", 0, 24), w("sg", 0, 24), w("dm", 0, 24), A.mult)
-            tt(w("s1", 0, 8), w("sm", 0, 8), w("sm", 8, 16), A.add)
-            tt(w("s2", 0, 8), w("s1", 0, 8), w("sm", 16, 24), A.add)
-            copy(sv, w("s2", 0, 8))
-            for b in (0, 2, 1, 3):
-                gather(w("ys", b, 512, 4), b, sv)
+            rows(k + 1, whole, "s")
+            fan_out(k + 1)
+            tt(w("sm", 0, 32), whole, w("dm", 0, 32), A.mult, ind=L("all%d" % k, 2, 4))
+            scan(w("sn", 0, 24), w("c3", 0, 24), w("sm", 0, 24))
+            copy(sv, w("sn", 2, 24, 3))
+            copy(w("mu", 0, 32), whole, L("all%d" % k, 0, 2))
+            for b in (2, 0, 3, 1):
+                if b < 2:
+                    copy(w("ys", b, 512, 4), bwin(b), sv)
+                else:
+                    act(w("ys", b, 512, 4), bwin(b), ind=sv)
             quant(w("qys", 0, 128), w("sys0", 0, 128), w("ys", 0, 512))
+            gather("mu", a1, a2, (0,), "s")
             for b in range(4):
                 mm(bank(b, 128), *wb(b), w("qys", 0, 128), w("sys0", 0, 128))
-                act(w("rs", 64 * b, 64 * b + 64), bank(b, 128, 0, 2), F.Relu)
-            copy(w("mu", 0, 32), w(e, 0, 48), sh)
+                act(w("rs", 64 * b, 64 * b + 64), bank(b, 128, 0, 2), F.Relu, 0.015625)
+            add_f(k, mid, C, 4)
             for b in range(4):
-                tt(w("xsd", b, 256, 4), w("rs", 64 * b, 64 * b + 64), w("bp", 256 * b + 64 * rank, 256 * b + 64 * rank + 64), A.add)
+                tt(w("xsd", b, 256, 4), w("rs", 64 * b, 64 * b + 64), w("bp", 256 * b + 64 * rank, 256 * b + 64 * rank + 64), A.add, ind=L("nat"))
             quant(w("qs%d" % (k + 1), 0, 128), w("ss%d" % (k + 1), 0, 128), w("xsd", 0, 512))
             seeds(k + 1)
-            for b in (0, 2, 1, 3):
-                gather(w("yt", b, 4 * a, 4), b, w("mu", 0, a // 16))
-                gather(w("yt", 4 * z + b, 4 * C, 4), b, w("mu", z // 16, 24))
-            a, z = 0, C
-        xn, n = "xt%d" % (k + 1), z - a
-        qy, sy = w("qy", a, z), w("sy", a, z)
-        quant(qy, sy, w("yt", 4 * a, 4 * z))
-        for b in range(4):
-            mm(bank(4 + b, n), *ceb(b), w("qx%d" % k, a, z), w("sx%d" % k, a, z), True, False)
-        for b in range(4):
-            mm(bank(4 + b, n), *wb(b), qy, sy, False, True)
-            tt(w(xn, 4 * a + b, 4 * z, 4), bank(4 + b, n), fpw(b, a, z), A.max)
-        if not last:
-            lists(k + 1, "exr")
-        quant(w("qx%d" % (k + 1), a, z), w("sx%d" % (k + 1), a, z), w(xn, 4 * a, 4 * z))
-        if not last:
+            fan_in(k + 1)
+            gather("mu", a1, a2, (1, 2), "s")
+            gather("mu", a1, a2, (3,), "v")
+            turn(k + 1, "s")
+            layer(k, mid, C, 4)
+            turn_back()
+            new_x(k, mid, C, 4)
+            quant_x(k + 1, 0, C)
             unpack_f(k + 1, (0, 1))
-            fan(k + 1)
-        if k == 0:
-            fill(w("yh", 256, 512), 0.0)
-        if k == 1:
-            quant(w("qv", 0, 128), w("svv", 0, 128), w("vt", 0, 512))
-            ts(it(15, 1), it(0, 1), 2, A.is_ge, 20, A.mult)
-            tt(it(15, 1), it(15, 1), it(0, 1), A.add)
-            ts(w("shh", 0, 1), it(15, 1), fc(22), A.add)
-            turner(2)
-
-    qv, svv = w("qv", 0, 128), w("svv", 0, 128)
-    x3, s3 = w("qx3", 32, 352), w("sx3", 32, 352)
-    mm(bank(4, 320), qv, svv, x3, s3)
-    act(w("yo", 32, 352), bank(4, 320))
-
-    def out_scales(c0, c1, name, a, b):
-        for i in range(4):
-            dma("y", T.osc[4 * i:4 * i + 4, c0:c1], ap(w(name, a, b, 1, 32 * i, 32 * i + 4)), "st", [w(name, a, b)], [])
-
-    copy(w("mh", 0, 16), w("ext3", 0, 48), w("shh", 0, 1))
-    for b in (0, 2, 1, 3):
-        gather(w("yh", b, 256, 4), b, w("mh", 0, 4))
-    quant(w("qys", 0, 128), w("sys0", 0, 128), w("yh", 0, 512))
-    for b in range(4):
-        mm(bank(b, 128), *wb(b), w("qys", 0, 128), w("sys0", 0, 128))
-        act(w("rs", 64 * b, 64 * b + 64), bank(b, 64), F.Relu)
-    for b in range(4):
-        tt(w("xsd", b, 256, 4), w("rs", 64 * b, 64 * b + 64), w("fh", 64 * b, 64 * b + 64), A.add)
-    quant(w("qh", 0, 128), w("sh0", 0, 128), w("xsd", 0, 512))
-    mm(bank(7, 128), qv, svv, w("qh", 0, 128), w("sh0", 0, 128))
-    act(w("yo2", 0, 64), bank(7, 64))
-    pn = w("pi", 0, 24)
-    fill(w("on", 24, 32), 0.0)
-    copy(pn, w("exr", 8, 32))
-    relabel(w("on", 0, 24), pn, 24)
-    op("v", lambda: vec.transpose(ap(w("ot", 0, 32)), ap(w("on", 0, 32))), [w("on", 0, 32)], [w("ot", 0, 32)])
-    dma("y", T.oc[:, 128:1408], ap(x3).bitcast(dt.uint8), "st", [x3], [])
-    out_scales(32, 352, "sx3", 32, 352)
-    dma("y", T.y[:, 32:352], ap(w("yo", 32, 352)), "st", [w("yo", 32, 352)], [])
-    for a, b in ((0, 0), (32, 352)):
-        v = w("qh", a, a + 32)
-        dma("y", T.oc[:, 4 * b:4 * b + 128], ap(v).bitcast(dt.uint8), "st", [v], [])
-        out_scales(b, b + 32, "sh0", a, a + 32)
-        v = w("yo2", a, a + 32)
-        dma("s", T.y[:, b:b + 32], ap(v), "st", [v], [])
-    for m in range(8):
-        v = w("ot", 16 * (m % 2), 16 * (m % 2) + 16, 1, 32 * (m // 2), 32 * (m // 2) + 24)
-        dma("y", T.op[m:m + 1, :], ap(v), "st", [v], [])
+            if k == 0:
+                ts(L("tn2"), DROW, float(H[2]), A.mult, Q16, A.add)
+                turner_q(1)
+                turner(2)
+            else:
+                turner_q(2)
+                quant(w("qv", 0, 128), w("svv", 0, 128), w("vt", 0, 512))
+        else:
+            add_f(k, mid, C, 0)
+            copy(w("mu", 0, 32), whole, L("all%d" % k, 0, 2))
+            quant_x(3, 0, mid)
+            gather("mu", a1, a2, (2, 3), "s")
+            gather("mu", a1, a2, (0, 1), "v")
+            put_codes(0, mid)
+            layer(k, mid, C, 0)
+            rows(3, own, "s")
+            put_y(0, mid, 4)
+            turn(3, "s")
+            new_x(k, mid, C, 0)
+            for m in range(8):
+                v = w("ot", 16 * (m % 2), 16 * (m % 2) + 16, 1, 32 * (m // 2), 32 * (m // 2) + 24)
+                dma("y", T.op[m:m + 1, :], ap(v), "st", [v], [])
+            quant_x(3, mid, C)
+            put_codes(mid, C)
+            put_y(mid, C, 5)
     for sem in SEMAPHORES:
         if total.get(sem, 0):
             wait("g", sem, total[sem])

@@ -38,15 +38,15 @@ for _n, _c, _t in (("fp", 4 * C, BF), ("bp", 1024, BF), ("gz", 2 * C, BF), ("zt"
                    ("wq", 512, X4), ("wsc", 512, U8), ("wd", 528, BF), ("ce", 512, X4), ("cs", 512, U8), ("ct", 528, BF), ("cc", 768, X4), ("ccs", 768, U8),
                    ("ci", 8, I32), ("cf", 40, F32), ("dd", 16, F32), ("da", 16, F32), ("io2", 12, F32), ("ib", 4, F32), ("bt", 16, F32), ("tw", 32, F32), ("sw", 12, F32),
                    ("i64", 64, F32), ("i128", 128, F32), ("eye", 64, BF), ("d24", 24, F32), ("d3", 24, I32), ("d4", 24, F32), ("dm", 32, BF), ("c3", 24, BF),
-                   ("gk", 192, BF), ("sc1", 192, BF), ("c8", 192, BF), ("ls", 96, U16)):
+                   ("gk", 192, BF), ("sc1", 192, BF), ("c8", 192, BF), ("ls", 100, U16)):
     _b(_n, _c, _t)
 SEMAPHORES = ["kv", "ks", "kt", "kg", "lx", "lp", "lu", "lw", "lv", "st", "loc", "ha0", "ha1", "ha2", "ha3"]
 for _r in range(3):
-    SEMAPHORES += ["se%d" % _r, "ow%d" % _r, "fw%d" % _r, "fr%d" % _r]
+    SEMAPHORES += ["se%d" % _r, "fw%d" % _r, "fr%d" % _r]
 
 LISTS, _at = {}, 0
 for _n, _c in (("rows0", 4), ("rows1", 4), ("rows2", 4), ("rows3", 4), ("turn", 6), ("rot", 2), ("seed", 4), ("nat", 4), ("pair", 8), ("spread", 2), ("cand", 12),
-               ("tn0", 8), ("tn1", 8), ("tn2", 8), ("all0", 4), ("all1", 4), ("all2", 4), ("own0", 2), ("own1", 2), ("own2", 2)):
+               ("tn0", 8), ("tn1", 8), ("tn2", 8), ("all0", 4), ("all1", 4), ("all2", 4), ("own0", 2), ("own1", 2), ("own2", 2), ("same", 4)):
     LISTS[_n] = (_at, _at + _c)
     _at += _c
 
@@ -188,7 +188,7 @@ def rank_program(g, core, T, topo):
         return w("ls", s + a, e if b is None else s + b)
 
     up, down = (rank - 1) % N, (rank + 1) % N
-    others = [r for r in range(N) if r != rank]
+    others = [(rank + i) % N for i in range(1, N)]
 
     def dst(r):
         rid, pid, _ = topo.addr(T.cores[r])
@@ -219,9 +219,6 @@ def rank_program(g, core, T, topo):
         q, s = (bq, bs) if k == 0 else (w("qs%d" % k, 0, 64), w("ss%d" % k, 0, 64))
         fused([(ids, m, "se%d" % k, ap(q).bitcast(dt.uint8), [ap(bq).bitcast(dt.uint8) for r in others])], [q])
         fused([(ids, m, "se%d" % k, ap(s), [ap(bs) for r in others])], [s])
-        if k:
-            dma("y", ap(bq).bitcast(dt.uint8), ap(q).bitcast(dt.uint8), "ow%d" % k, [q], [bq])
-            dma("y", ap(bs), ap(s), "ow%d" % k, [s], [bs])
         n = 2 * len(others) * bin(m).count("1")
         for r in others:
             arrive(w("bc%d" % k, 64 * r, 64 * r + 64), "se%d" % k, n)
@@ -231,6 +228,7 @@ def rank_program(g, core, T, topo):
     dma("s", ap(w("ext0", 8, 32)), T.p[:, :], "lp", [], [w("ext0", 8, 32)])
     dma("y", ap(w("xt0", 0, cut)), T.x[:, 4 * ROT:4 * C], "lx", [], [w("xt0", 0, cut)])
     dma("y", ap(w("xt0", cut, 4 * C)), T.x[:, 0:4 * ROT], "lx", [], [w("xt0", cut, 4 * C)])
+    dma("y", ap(w("ut", 0, 512)), T.u[:, :], "lu", [], [w("ut", 0, 512)])
 
     def fc(i, n=1):
         return w("cf", i, i + n)
@@ -246,6 +244,8 @@ def rank_program(g, core, T, topo):
     iota(w("ib", 0, 4), [[-8, 2], [16, 2]], 8, 1)
     iota(w("i128", 0, 128), [[1, 128]], 0, 0)
     iota(w("i64", 0, 64), [[0, 2], [-16, 2], [1, 16]], 16, 0)
+    iota(w("d24", 0, 24), [[0, 8], [1, 3]], 0, 1)
+    iota(w("rk", 192, 256), [[0, 64]], 0, 0)
     halo(0, 8, 24)
 
     fill(w("wd", 0, 516), 0.0)
@@ -288,24 +288,36 @@ def rank_program(g, core, T, topo):
     def ceb(b):
         return w("ce", 128 * b, 128 * b + 128), w("cs", 128 * b, 128 * b + 128)
 
-    quant(*ceb(0), w("wd", 3, 515))
+    def turner(i):
+        for e in range(2):
+            act(w("ct", 2 * (i % 2) + e, 512, 4), w("eye", 16 * e, 16 * e + 48), ind=L("tn%d" % i))
+
     ts(L("tn0"), DROW, float(H[0]), A.mult, Q16, A.add)
     ts(L("tn1"), DROW, float(H[1]), A.mult, Q16, A.add)
+    lin(TMP, B32, 2, 32)
+    lin(LH, H8, 0.125, 0)
+    lin(E0, LO, 4, TMP)
+    lin(LH, LO, 24, LH)
+    turner(0)
+    turner(1)
+    for b in range(4):
+        quant(*ceb(b), w("wd", 3 - b, 515 - b))
+    ts(w("tw", 8, 14), w("tw", 0, 6), 0.0, A.is_lt, 48.0, A.mult)
+    ts(w("tw", 16, 22), w("tw", 0, 6), 16.0, A.is_ge, 16.0, A.mult)
+    ts(L("rows0"), w("bt", 2, 6), X64, A.add, 0.125, A.mult)
+    tt(w("tw", 8, 14), w("tw", 8, 14), w("tw", 16, 22), A.add)
+    ts(L("rot"), w("bt", 0, 2), 0.125, A.mult)
+    tt(w("tw", 24, 30), w("tw", 8, 14), w("tw", 0, 6), A.add)
 
     quant(w("qx0", 0, C), w("sx0", 0, C), w("xt0", 0, 4 * C))
     pick(w("bc0", 64 * rank, 64 * rank + 64), w("bs0", 64 * rank, 64 * rank + 64), w("qx0", 0, C), w("sx0", 0, C), L("seed"))
     seeds(0)
-    dma("y", ap(w("ut", 0, 512)), T.u[:, :], "lu", [], [w("ut", 0, 512)], ["lx"])
-    dma("y", ap(w("wq", 0, 512)).bitcast(dt.uint8), T.wc[:, :], "lw", [], [w("wq", 0, 512)])
-    dma("y", ap(w("wsc", 0, 512)), T.ws[:, :], "lw", [], [w("wsc", 0, 512)])
     iota(w("et", 0, 800), [[0, 800]], 0, 0)
-    iota(w("rk", 192, 256), [[0, 64]], 0, 0)
     iota(w("c8", 0, 192), [[0, 192]], 1, 0)
     keep_if(w("sc1", 0, 192), [[0, 3], [1, 8], [-1, 8]], A.not_equal, -1.0, w("c8", 0, 192))
     keep_if(w("sc1", 0, 192), [[0, 24], [1, 8]], A.is_gt, 0.0)
     keep_if(w("c8", 0, 192), [[0, 24], [1, 8]], A.is_gt, 0.0)
     iota(w("gk", 0, 192), [[0, 24], [-1, 8]], 0, 0)
-    iota(w("d24", 0, 24), [[0, 8], [1, 3]], 0, 1)
     iota(w("c3", 0, 24), [[0, 24]], 1, 0)
     keep_if(w("c3", 0, 24), [[0, 8], [1, 3]], A.is_gt, 0.0)
     iota(w("dm", 24, 32), [[0, 8]], 0, 0)
@@ -323,10 +335,6 @@ def rank_program(g, core, T, topo):
             if b < 2:
                 act(fpw(b), bank(b, C))
 
-    def turner(i):
-        for e in range(2):
-            act(w("ct", 2 * (i % 2) + e, 512, 4), w("eye", 16 * e, 16 * e + 48), ind=L("tn%d" % i))
-
     def ccw(i, e):
         a = 256 * i + 128 * e
         return w("cc", a, a + 128), w("ccs", a, a + 128)
@@ -336,22 +344,28 @@ def rank_program(g, core, T, topo):
             o = 2 * (i % 2) + e
             quant(*ccw(i, e), w("ct", o, o + 512))
 
-    ts(w("tw", 8, 14), w("tw", 0, 6), 0.0, A.is_lt, 48.0, A.mult)
-    ts(w("tw", 16, 22), w("tw", 0, 6), 16.0, A.is_ge, 16.0, A.mult)
-    ts(L("rows0"), w("bt", 2, 6), X64, A.add, 0.125, A.mult)
-    tt(w("tw", 8, 14), w("tw", 8, 14), w("tw", 16, 22), A.add)
-    ts(L("rot"), w("bt", 0, 2), 0.125, A.mult)
-    tt(w("tw", 24, 30), w("tw", 8, 14), w("tw", 0, 6), A.add)
-    for b in (1, 2, 3):
-        quant(*ceb(b), w("wd", 3 - b, 515 - b))
     t0 = LISTS["turn"][0]
     copy(w("ls", t0, t0 + 6, 2), w("tw", 24, 30, 2))
     ts(w("ls", t0 + 1, t0 + 6, 2), w("tw", 25, 30, 2), 16.0, A.add)
     unpack_f(0, (0, 1))
-    turner(0)
-    turner(1)
     ts(L("pair", 0, 4), w("sw", 0, 4), LO16, A.max)
     ts(L("pair", 4, 8), w("sw", 0, 4), LO16, A.min)
+    quant(w("qu", 0, 128), w("suu", 0, 128), w("ut", 0, 512))
+    turner_q(0)
+    pick(w("qua", 0, 128), w("sua", 0, 128), w("qu", 0, 128), w("suu", 0, 128), L("pair"))
+    lin(fc(25), H8, 96, E0)
+    lin(TMP, E0, 1, 256)
+    lin(GF, G16, -0.0625, 0)
+    lin(fc(24), H8, 32, TMP)
+    lin(HL, H8, 1, L3)
+    for i, h in enumerate(H):
+        lin(fc(20 + i), DR, 16 * h, 7)
+    ts(w("d3", 0, 24), w("d24", 0, 24), G16, A.add, 0.33333334, A.mult)
+    ts(L("cand"), io2(12), LH, A.add)
+    ts(w("d4", 0, 24), w("d3", 0, 24), 3.0, A.mult, G16, A.subtract)
+    ts(L("same"), io2(4), 8.0, A.mult, Q, A.add)
+    tt(w("dm", 0, 24), w("d4", 0, 24), w("d24", 0, 24), A.is_equal)
+    turner_q(1)
 
     def rows(k, src, on):
         if on == "v":
@@ -392,25 +406,15 @@ def rank_program(g, core, T, topo):
     rows(0, w("ext0", 0, 40), "v")
     fan_out(0)
     fan_in(0)
+    dma("y", ap(w("wq", 0, 512)).bitcast(dt.uint8), T.wc[:, :], "lw", [], [w("wq", 0, 512)])
+    dma("y", ap(w("wsc", 0, 512)), T.ws[:, :], "lw", [], [w("wsc", 0, 512)])
     dma("y", ap(w("vt", 0, 512)), T.v[:, :], "lv", [], [w("vt", 0, 512)])
     turn(0, "v")
     turn_back()
-    quant(w("qu", 0, 128), w("suu", 0, 128), w("ut", 0, 512))
-    pick(w("qua", 0, 128), w("sua", 0, 128), w("qu", 0, 128), w("suu", 0, 128), L("pair"))
-    lin(TMP, B32, 2, 32)
-    lin(LH, H8, 0.125, 0)
-    lin(E0, LO, 4, TMP)
-    lin(LH, LO, 24, LH)
-    lin(fc(25), H8, 96, E0)
-    lin(TMP, E0, 1, 256)
-    lin(GF, G16, -0.0625, 0)
-    lin(fc(24), H8, 32, TMP)
-    lin(HL, H8, 1, L3)
-    for i, h in enumerate(H):
-        lin(fc(20 + i), DR, 16 * h, 7)
-    turner_q(0)
     copy(L("spread"), EL)
-    ts(L("cand"), io2(12), LH, A.add)
+    ts(L("nat"), io2(4), 8.0, A.mult, HL, A.add)
+    ts(L("tn2"), DROW, float(H[2]), A.mult, Q16, A.add)
+    quant(w("qe", 0, 200), w("se", 0, 200), w("et", 0, 800))
 
     def row_lists(i):
         h = H[i]
@@ -457,12 +461,13 @@ def rank_program(g, core, T, topo):
             if max(a, lo) < min(z, hi):
                 yield max(a, lo), min(z, hi), max(a, lo) + d
 
-    def put_codes(a, z):
+    def put_codes(a, z, qs):
         for s, e, o in runs(a, z):
             v = w("qx3", s, e)
             dma("y", T.oc[:, 4 * o:4 * (o + e - s)], ap(v).bitcast(dt.uint8), "st", [v], [])
+        for s, e, o in runs(a, z):
             for i in range(4):
-                dma("y", T.osc[4 * i:4 * i + 4, o:o + e - s], ap(w("sx3", s, e, 1, 32 * i, 32 * i + 4)), "st", [w("sx3", s, e)], [])
+                dma(qs[i], T.osc[4 * i:4 * i + 4, o:o + e - s], ap(w("sx3", s, e, 1, 32 * i, 32 * i + 4)), "st", [w("sx3", s, e)], [])
 
     def put_y(a, z, b):
         mm(bank(b, z - a), w("qv", 0, 128), w("svv", 0, 128), w("qx3", a, z), w("sx3", a, z))
@@ -480,36 +485,41 @@ def rank_program(g, core, T, topo):
 
         def unpack_b(b):
             mm(bank(4 + b, 256), *ceb(b), w("bc%d" % k, 0, 256), w("bs%d" % k, 0, 256))
-            if b < 2:
+            if b == 0:
                 copy(bwin(b), bank(4 + b, 256))
             else:
                 act(bwin(b), bank(4 + b, 256))
 
-        def z_of(b):
-            z, gz = w("zt", b, 4 * C, 4), w("gz", C * (b % 2), C * (b % 2) + C)
-            if b < 2:
-                tt(z, bwin(b), fpw(b), A.subtract, ind=lu)
-            else:
-                act(gz, bwin(b), ind=lu)
-                tt(z, gz, bank(b, C), A.subtract)
+        def z_last(t):
+            a, z = 128 * t, 128 * t + 128
+            tt(w("zt", 4 * a + 3, 4 * z, 4), w("gz", C + a, C + z), bank(3, z, a), A.subtract)
 
-        unpack_f(k, (2, 3))
-        unpack_b(0)
-        unpack_b(2)
-        unpack_b(1)
-        z_of(0)
-        z_of(2)
-        unpack_b(3)
-        z_of(1)
-        z_of(3)
-        for t in range(3):
+        def scores(t):
             qz, sz = w("qz", 128 * t, 128 * t + 128), w("sz", 128 * t, 128 * t + 128)
             quant(qz, sz, w("zt", 512 * t, 512 * t + 512))
             mm(bank(4 + t, 128), qz, sz, w("qua", 0, 128), w("sua", 0, 128))
             act(w("sc", 64 * t, 64 * t + 64), bank(4 + t, 128, 64))
+
+        unpack_b(0)
+        unpack_b(2)
+        unpack_b(1)
+        unpack_f(k, (2,))
+        tt(w("zt", 0, 4 * C, 4), bwin(0), fpw(0), A.subtract, ind=lu)
+        act(w("gz", 0, C), bwin(2), ind=lu)
+        tt(w("zt", 1, 4 * C, 4), bwin(1), fpw(1), A.subtract, ind=lu)
+        unpack_b(3)
+        unpack_f(k, (3,))
+        tt(w("zt", 2, 4 * C, 4), w("gz", 0, C), bank(2, C), A.subtract)
+        for t in range(3):
+            act(w("gz", C + 128 * t, C + 128 * t + 128), bwin(3), ind=w("lu", 8 * t, 8 * t + 8))
+        z_last(0)
+        z_last(1)
+        scores(0)
+        z_last(2)
+        scores(1)
+        scores(2)
         if k == 0:
             lin(w("gk", 0, 192), w("gk", 0, 192), 1, GF)
-            quant(w("qe", 0, 200), w("se", 0, 200), w("et", 0, 800))
         for t in range(3):
             tt(w("fl", 64 * t, 64 * t + 64), bank(4 + t, 64), w("sc", 64 * t, 64 * t + 64), A.is_gt)
         scan(w("rk", 0, 192), w("sc1", 0, 192), w("fl", 0, 192))
@@ -526,25 +536,31 @@ def rank_program(g, core, T, topo):
         scan(own, w("c8", 0, 192), w("pr", 0, 192))
         halo(k + 1, n, 192)
         add_f(k, 0, mid, 4)
+        if last:
+            rows(3, own, "s")
         copy(w("mi", 0, 32), own, L("own%d" % k))
         gather("mi", 0, a1, (0, 1), "v")
         gather("mi", 0, a1, (2, 3), "s")
-        if a2 < 24:
+        if k == 0:
+            turner(2)
+        else:
             gather("mi", a2, 24, range(4), "s")
         layer(k, 0, mid, 4)
-        if k == 0:
-            ts(w("d3", 0, 24), w("d24", 0, 24), G16, A.add, 0.33333334, A.mult)
-            ts(L("nat"), io2(4), 8.0, A.mult, HL, A.add)
-            ts(w("d4", 0, 24), w("d3", 0, 24), 3.0, A.mult, G16, A.subtract)
-            tt(w("dm", 0, 24), w("d4", 0, 24), w("d24", 0, 24), A.is_equal)
+        if last:
+            turn(3, "s")
+            for m in range(8):
+                v = w("ot", 16 * (m % 2), 16 * (m % 2) + 16, 1, 32 * (m // 2), 32 * (m // 2) + 24)
+                dma("y", T.op[m:m + 1, :], ap(v), "st", [v], [])
         new_x(k, 0, mid, 4)
         if not last:
+            if k == 0:
+                quant_x(1, 0, mid)
             rows(k + 1, whole, "s")
             fan_out(k + 1)
             tt(w("sm", 0, 32), whole, w("dm", 0, 32), A.mult, ind=L("all%d" % k, 2, 4))
+            copy(w("mu", 0, 32), whole, L("all%d" % k, 0, 2))
             scan(w("sn", 0, 24), w("c3", 0, 24), w("sm", 0, 24))
             copy(sv, w("sn", 2, 24, 3))
-            copy(w("mu", 0, 32), whole, L("all%d" % k, 0, 2))
             for b in (2, 0, 3, 1):
                 if b < 2:
                     copy(w("ys", b, 512, 4), bwin(b), sv)
@@ -552,47 +568,42 @@ def rank_program(g, core, T, topo):
                     act(w("ys", b, 512, 4), bwin(b), ind=sv)
             quant(w("qys", 0, 128), w("sys0", 0, 128), w("ys", 0, 512))
             gather("mu", a1, a2, (0,), "s")
+            if k == 1:
+                quant_x(2, 0, mid)
             for b in range(4):
                 mm(bank(b, 128), *wb(b), w("qys", 0, 128), w("sys0", 0, 128))
                 act(w("rs", 64 * b, 64 * b + 64), bank(b, 128, 0, 2), F.Relu, 0.015625)
             add_f(k, mid, C, 4)
+            gather("mu", a1, a2, (1, 2), "s")
             for b in range(4):
                 tt(w("xsd", b, 256, 4), w("rs", 64 * b, 64 * b + 64), w("bp", 256 * b + 64 * rank, 256 * b + 64 * rank + 64), A.add, ind=L("nat"))
-            quant(w("qs%d" % (k + 1), 0, 128), w("ss%d" % (k + 1), 0, 128), w("xsd", 0, 512))
+            q, s = w("qs%d" % (k + 1), 0, 128), w("ss%d" % (k + 1), 0, 128)
+            quant(q, s, w("xsd", 0, 512))
             seeds(k + 1)
             fan_in(k + 1)
-            gather("mu", a1, a2, (1, 2), "s")
             gather("mu", a1, a2, (3,), "v")
-            turn(k + 1, "s")
             layer(k, mid, C, 4)
-            turn_back()
+            pick(w("bc%d" % (k + 1), 64 * rank, 64 * rank + 64), w("bs%d" % (k + 1), 64 * rank, 64 * rank + 64), q, s, L("same"))
             new_x(k, mid, C, 4)
-            quant_x(k + 1, 0, C)
+            quant_x(k + 1, mid, C)
             unpack_f(k + 1, (0, 1))
-            if k == 0:
-                ts(L("tn2"), DROW, float(H[2]), A.mult, Q16, A.add)
-                turner_q(1)
-                turner(2)
-            else:
+            turn(k + 1, "v")
+            turn_back()
+            if k == 1:
                 turner_q(2)
                 quant(w("qv", 0, 128), w("svv", 0, 128), w("vt", 0, 512))
         else:
             add_f(k, mid, C, 0)
             copy(w("mu", 0, 32), whole, L("all%d" % k, 0, 2))
-            quant_x(3, 0, mid)
             gather("mu", a1, a2, (2, 3), "s")
             gather("mu", a1, a2, (0, 1), "v")
-            put_codes(0, mid)
             layer(k, mid, C, 0)
-            rows(3, own, "s")
+            quant_x(3, 0, mid)
+            put_codes(0, mid, "yyyy")
             put_y(0, mid, 4)
-            turn(3, "s")
             new_x(k, mid, C, 0)
-            for m in range(8):
-                v = w("ot", 16 * (m % 2), 16 * (m % 2) + 16, 1, 32 * (m // 2), 32 * (m // 2) + 24)
-                dma("y", T.op[m:m + 1, :], ap(v), "st", [v], [])
             quant_x(3, mid, C)
-            put_codes(mid, C)
+            put_codes(mid, C, "syyy")
             put_y(mid, C, 5)
     for sem in SEMAPHORES:
         if total.get(sem, 0):

@@ -4,6 +4,8 @@ from concourse.mybir import dt, AluOpType, ActivationFunctionType
 C = 384
 H = [4, 2, 1]
 DC = [0, 1, 1, 1, 0, -1, -1, -1]
+EARLY = [2, 2]
+FS = 5
 ROT = 128
 
 SCRATCH = {}
@@ -21,6 +23,7 @@ for _r in range(4):
     _b("qx%d" % _r, C, X4)
     _b("sx%d" % _r, C, U8)
 _b("ext0", 40, I32)
+SCRATCH["eq"] = ("sbuf", [128, 12, 16], BF)
 for _r in range(3):
     _b("ext%d" % (_r + 1), 192 + 32 * H[_r], BF)
     _b("bc%d" % _r, 256, X4)
@@ -30,15 +33,15 @@ for _r in (1, 2):
     _b("qs%d" % _r, 128, X4)
     _b("ss%d" % _r, 128, U8)
 for _n, _c, _t in (("fp", 4 * C, BF), ("bp", 1024, BF), ("gz", 2 * C, BF), ("zt", 4 * C, BF), ("yt", 4 * C, BF), ("ys", 512, BF), ("xsd", 512, BF),
-                   ("lfw", 64, BF), ("tl", 64, BF), ("tg", 32, BF), ("lf", 32, BF), ("lu", 32, U16), ("mi", 32, U16), ("mu", 32, U16), ("sv", 8, U16), ("lsh", 192, BF),
+                   ("lfw", 64, BF), ("tl", 64, BF), ("tg", 32, BF), ("lf", 32, BF), ("lu", 32, U16), ("mi", 32, U16), ("mu", 32, U16), ("sv", 8, U16), ("lsh", 192, BF), ("lsr", 192, BF),
                    ("qz", C, X4), ("sz", C, U8), ("qy", C, X4), ("sy", C, U8), ("qys", 128, X4), ("sys0", 128, U8),
-                   ("sc", 192, F32), ("fl", 192, BF), ("rk", 256, BF), ("et", 1056, BF), ("qe", 200, X4), ("se", 200, U8), ("eq", 192, BF), ("pr", 192, BF),
+                   ("sc", 192, F32), ("fl", 192, BF), ("rk", 256, BF), ("et", 512, BF), ("qe", 128, X4), ("se", 128, U8), ("pr", 192, BF),
                    ("sm", 32, BF), ("sn", 24, BF), ("rs", 256, F32), ("yo", C, F32), ("ot", 32, F32),
                    ("ut", 512, BF), ("vt", 512, BF), ("qu", 128, X4), ("suu", 128, U8), ("qua", 128, X4), ("sua", 128, U8), ("qv", 128, X4), ("svv", 128, U8),
                    ("wq", 512, X4), ("wsc", 512, U8), ("wd", 528, BF), ("ce", 512, X4), ("cs", 512, U8), ("ct", 528, BF), ("cc", 768, X4), ("ccs", 768, U8),
                    ("ci", 8, I32), ("cf", 40, F32), ("dd", 16, F32), ("da", 16, F32), ("io2", 12, F32), ("ib", 4, F32), ("bt", 16, F32), ("tw", 32, F32), ("sw", 12, F32),
                    ("i64", 64, F32), ("i128", 128, F32), ("eye", 64, BF), ("d24", 24, F32), ("d3", 24, I32), ("d4", 24, F32), ("dm", 32, BF), ("c3", 24, BF),
-                   ("gk", 192, BF), ("sc1", 192, BF), ("c8", 192, BF), ("ls", 100, U16)):
+                   ("gk", 96, BF), ("sc1", 192, BF), ("c8", 192, BF), ("ls", 100, U16)):
     _b(_n, _c, _t)
 SEMAPHORES = ["kv", "ks", "kt", "kg", "lx", "lp", "lu", "lw", "lv", "st", "loc", "ha0", "ha1", "ha2", "ha3"]
 for _r in range(3):
@@ -229,6 +232,8 @@ def rank_program(g, core, T, topo):
     dma("y", ap(w("xt0", 0, cut)), T.x[:, 4 * ROT:4 * C], "lx", [], [w("xt0", 0, cut)])
     dma("y", ap(w("xt0", cut, 4 * C)), T.x[:, 0:4 * ROT], "lx", [], [w("xt0", cut, 4 * C)])
     dma("y", ap(w("ut", 0, 512)), T.u[:, :], "lu", [], [w("ut", 0, 512)])
+    dma("y", ap(w("wq", 0, 512)).bitcast(dt.uint8), T.wc[:, :], "lw", [], [w("wq", 0, 512)])
+    dma("y", ap(w("wsc", 0, 512)), T.ws[:, :], "lw", [], [w("wsc", 0, 512)])
 
     def fc(i, n=1):
         return w("cf", i, i + n)
@@ -241,11 +246,9 @@ def rank_program(g, core, T, topo):
     iota(w("ci", 5, 6), [[0, 1]], 0, 1)
     iota(w("ci", 6, 7), [[0, 1]], 0, 3)
     iota(io2(12), [[2, 12]], 0, 0)
-    iota(w("ib", 0, 4), [[-8, 2], [16, 2]], 8, 1)
     iota(w("i128", 0, 128), [[1, 128]], 0, 0)
+    iota(w("ib", 0, 4), [[-8, 2], [16, 2]], 8, 1)
     iota(w("i64", 0, 64), [[0, 2], [-16, 2], [1, 16]], 16, 0)
-    iota(w("d24", 0, 24), [[0, 8], [1, 3]], 0, 1)
-    iota(w("rk", 192, 256), [[0, 64]], 0, 0)
     halo(0, 8, 24)
 
     fill(w("wd", 0, 516), 0.0)
@@ -265,8 +268,8 @@ def rank_program(g, core, T, topo):
     lin(PM8, O1, -16, 8)
     lin(Q16, Q, 1, 16)
 
-    ts(w("sw", 0, 4), io2(4), 48.0, A.mult, Q6, A.add)
     ts(w("wd", 3, 515, 4), w("i128", 0, 128), P, A.is_equal)
+    ts(w("sw", 0, 4), io2(4), 48.0, A.mult, Q6, A.add)
     ts(w("sw", 4, 8), w("sw", 0, 4), float(ROT), A.is_lt, float(C), A.mult)
     ts(w("bt", 8, 12), w("ib", 0, 4), G16, A.add, 8.0, A.mult)
     tt(w("sw", 8, 12), w("sw", 0, 4), w("sw", 4, 8), A.add)
@@ -274,12 +277,11 @@ def rank_program(g, core, T, topo):
     ts(L("seed"), w("sw", 8, 12), -float(ROT), A.add)
     tt(w("bt", 0, 4), w("bt", 8, 12), w("bt", 12, 16), A.add)
     ts(w("da", 0, 11), w("da", 0, 11), -1.0, A.mult, 2.0, A.add)
-    ts(w("eye", 0, 64), w("i64", 0, 64), C31, A.is_equal)
+    fill(w("ct", 0, 516), 0.0)
     ts(w("dd", 0, 11), w("da", 0, 11), -1.0, A.max, 1.0, A.min)
-    fill(w("ct", 512, 516), 0.0)
-    lin(w("bt", 4, 6), w("bt", 2, 4), 1, PM8)
     lin(HI, H8, 2, 0)
     lin(LO16, LO, 16, 0)
+    lin(w("bt", 4, 6), w("bt", 2, 4), 1, PM8)
     lin(w("sw", 0, 4), io2(4), 16, HI)
     lin(X64, DR, 64, 64)
     for i, s in enumerate((H[0], H[1] - H[0], -1)):
@@ -292,32 +294,34 @@ def rank_program(g, core, T, topo):
         for e in range(2):
             act(w("ct", 2 * (i % 2) + e, 512, 4), w("eye", 16 * e, 16 * e + 48), ind=L("tn%d" % i))
 
-    ts(L("tn0"), DROW, float(H[0]), A.mult, Q16, A.add)
-    ts(L("tn1"), DROW, float(H[1]), A.mult, Q16, A.add)
-    lin(TMP, B32, 2, 32)
     lin(LH, H8, 0.125, 0)
-    lin(E0, LO, 4, TMP)
+    lin(E0, LO, 4, B32)
     lin(LH, LO, 24, LH)
-    turner(0)
-    turner(1)
+    lin(TMP, E0, 1, 128)
+    lin(fc(25), H8, 48, E0)
+    lin(fc(24), H8, 16, TMP)
     for b in range(4):
         quant(*ceb(b), w("wd", 3 - b, 515 - b))
+
+    quant(w("qx0", 0, C), w("sx0", 0, C), w("xt0", 0, 4 * C))
+    pick(w("bc0", 64 * rank, 64 * rank + 64), w("bs0", 64 * rank, 64 * rank + 64), w("qx0", 0, C), w("sx0", 0, C), L("seed"))
+    seeds(0)
+    ts(w("eye", 0, 64), w("i64", 0, 64), C31, A.is_equal)
+    ts(L("tn0"), DROW, float(H[0]), A.mult, Q16, A.add)
     ts(w("tw", 8, 14), w("tw", 0, 6), 0.0, A.is_lt, 48.0, A.mult)
     ts(w("tw", 16, 22), w("tw", 0, 6), 16.0, A.is_ge, 16.0, A.mult)
     ts(L("rows0"), w("bt", 2, 6), X64, A.add, 0.125, A.mult)
     tt(w("tw", 8, 14), w("tw", 8, 14), w("tw", 16, 22), A.add)
     ts(L("rot"), w("bt", 0, 2), 0.125, A.mult)
     tt(w("tw", 24, 30), w("tw", 8, 14), w("tw", 0, 6), A.add)
-
-    quant(w("qx0", 0, C), w("sx0", 0, C), w("xt0", 0, 4 * C))
-    pick(w("bc0", 64 * rank, 64 * rank + 64), w("bs0", 64 * rank, 64 * rank + 64), w("qx0", 0, C), w("sx0", 0, C), L("seed"))
-    seeds(0)
-    iota(w("et", 0, 800), [[0, 800]], 0, 0)
+    iota(w("et", 0, 512), [[0, 512]], 0, 0)
+    iota(w("rk", 192, 256), [[0, 64]], 0, 0)
+    iota(w("d24", 0, 24), [[0, 8], [1, 3]], 0, 1)
     iota(w("c8", 0, 192), [[0, 192]], 1, 0)
     keep_if(w("sc1", 0, 192), [[0, 3], [1, 8], [-1, 8]], A.not_equal, -1.0, w("c8", 0, 192))
     keep_if(w("sc1", 0, 192), [[0, 24], [1, 8]], A.is_gt, 0.0)
     keep_if(w("c8", 0, 192), [[0, 24], [1, 8]], A.is_gt, 0.0)
-    iota(w("gk", 0, 192), [[0, 24], [-1, 8]], 0, 0)
+    iota(w("gk", 0, 96), [[0, 12], [-1, 8]], 0, 0)
     iota(w("c3", 0, 24), [[0, 24]], 1, 0)
     keep_if(w("c3", 0, 24), [[0, 8], [1, 3]], A.is_gt, 0.0)
     iota(w("dm", 24, 32), [[0, 8]], 0, 0)
@@ -339,33 +343,24 @@ def rank_program(g, core, T, topo):
         a = 256 * i + 128 * e
         return w("cc", a, a + 128), w("ccs", a, a + 128)
 
-    def turner_q(i):
-        for e in range(2):
+    def turner_q(i, es=(0, 1)):
+        for e in es:
             o = 2 * (i % 2) + e
             quant(*ccw(i, e), w("ct", o, o + 512))
 
     t0 = LISTS["turn"][0]
+    ts(L("pair", 0, 4), w("sw", 0, 4), LO16, A.max)
     copy(w("ls", t0, t0 + 6, 2), w("tw", 24, 30, 2))
     ts(w("ls", t0 + 1, t0 + 6, 2), w("tw", 25, 30, 2), 16.0, A.add)
     unpack_f(0, (0, 1))
-    ts(L("pair", 0, 4), w("sw", 0, 4), LO16, A.max)
+    turner(0)
     ts(L("pair", 4, 8), w("sw", 0, 4), LO16, A.min)
     quant(w("qu", 0, 128), w("suu", 0, 128), w("ut", 0, 512))
-    turner_q(0)
     pick(w("qua", 0, 128), w("sua", 0, 128), w("qu", 0, 128), w("suu", 0, 128), L("pair"))
-    lin(fc(25), H8, 96, E0)
-    lin(TMP, E0, 1, 256)
     lin(GF, G16, -0.0625, 0)
-    lin(fc(24), H8, 32, TMP)
     lin(HL, H8, 1, L3)
     for i, h in enumerate(H):
         lin(fc(20 + i), DR, 16 * h, 7)
-    ts(w("d3", 0, 24), w("d24", 0, 24), G16, A.add, 0.33333334, A.mult)
-    ts(L("cand"), io2(12), LH, A.add)
-    ts(w("d4", 0, 24), w("d3", 0, 24), 3.0, A.mult, G16, A.subtract)
-    ts(L("same"), io2(4), 8.0, A.mult, Q, A.add)
-    tt(w("dm", 0, 24), w("d4", 0, 24), w("d24", 0, 24), A.is_equal)
-    turner_q(1)
 
     def rows(k, src, on):
         if on == "v":
@@ -373,18 +368,20 @@ def rank_program(g, core, T, topo):
         else:
             act(w("lfw", 0, 64), src, ind=L("rows%d" % k))
 
-    def turn(k, on):
+    def turn(k, step, on="v"):
         j = min(k, 2)
-        flip(w("tl", 0, 64), w("lfw", 0, 64))
-        out = w("ot" if k == 3 else "tg", 0, 32)
-        if on == "v":
-            copy(out, w("tl", 0, 64), L("turn", 2 * j, 2 * j + 2))
+        if step == 0:
+            flip(w("tl", 0, 64), w("lfw", 0, 64))
+        elif step == 1:
+            out = w("ot" if k == 3 else "tg", 0, 32)
+            if on == "v":
+                copy(out, w("tl", 0, 64), L("turn", 2 * j, 2 * j + 2))
+            else:
+                act(out, w("tl", 0, 64), ind=L("turn", 2 * j, 2 * j + 2))
+        elif step == 2:
+            flip(w("lf", 0, 32), w("tg", 0, 32))
         else:
-            act(out, w("tl", 0, 64), ind=L("turn", 2 * j, 2 * j + 2))
-
-    def turn_back():
-        flip(w("lf", 0, 32), w("tg", 0, 32))
-        copy(w("lu", 0, 32), w("lf", 0, 32), L("rot"))
+            copy(w("lu", 0, 32), w("lf", 0, 32), L("rot"))
 
     def fan_out(k):
         t, h = T["fan%d" % k], H[k]
@@ -394,7 +391,7 @@ def rank_program(g, core, T, topo):
                 a, b = max(lo, d - h), min(hi, 16 + d + h)
                 if a < b:
                     v = w("lfw", col, col + 24, 1, 16 * m + a - lo, 16 * m + b - lo)
-                    dma("y", t[a - d + h:b - d + h, m, :], ap(v), "fw%d" % k, [v], [])
+                    dma("s" if k == 0 and m >= FS else "y", t[a - d + h:b - d + h, m, :], ap(v), "fw%d" % k, [v], [])
 
     def fan_in(k):
         t, h = T["fan%d" % k], H[k]
@@ -406,21 +403,23 @@ def rank_program(g, core, T, topo):
     rows(0, w("ext0", 0, 40), "v")
     fan_out(0)
     fan_in(0)
-    dma("y", ap(w("wq", 0, 512)).bitcast(dt.uint8), T.wc[:, :], "lw", [], [w("wq", 0, 512)])
-    dma("y", ap(w("wsc", 0, 512)), T.ws[:, :], "lw", [], [w("wsc", 0, 512)])
     dma("y", ap(w("vt", 0, 512)), T.v[:, :], "lv", [], [w("vt", 0, 512)])
-    turn(0, "v")
-    turn_back()
     copy(L("spread"), EL)
-    ts(L("nat"), io2(4), 8.0, A.mult, HL, A.add)
-    ts(L("tn2"), DROW, float(H[2]), A.mult, Q16, A.add)
-    quant(w("qe", 0, 200), w("se", 0, 200), w("et", 0, 800))
+    turn(0, 0)
+    ts(L("cand"), io2(12), LH, A.add)
+    turn(0, 1)
+    turner_q(0, (0,))
+    turn(0, 2)
+    turner_q(0, (1,))
+    turn(0, 3)
 
-    def row_lists(i):
+    def row_lists(i, j):
         h = H[i]
-        ts(L("own%d" % i), w("bt", 0, 2), fc(20 + i), A.add, 191.0, A.min)
-        ts(L("all%d" % i), w("bt", 0, 4), fc(20 + i), A.add, 16.0 * h, A.add)
-        if i < 2:
+        if j == 0:
+            ts(L("own%d" % i), w("bt", 0, 2), fc(20 + i), A.add, 191.0, A.min)
+        elif j == 1:
+            ts(L("all%d" % i), w("bt", 0, 4), fc(20 + i), A.add, 16.0 * h, A.add)
+        elif i < 2:
             ts(L("rows%d" % (i + 1)), w("bt", 2, 6), fc(21 + i), A.add, 16.0 * h, A.add)
         else:
             ts(L("rows3"), w("bt", 2, 6), 7.0, A.add)
@@ -449,8 +448,8 @@ def rank_program(g, core, T, topo):
         for b in range(4):
             mm(bank(b0 + b, z - a), *wb(b), qy, sy, False, True)
 
-    def new_x(k, a, z, b0):
-        for b in range(4):
+    def new_x(k, a, z, b0, bs=range(4)):
+        for b in bs:
             tt(w("xt%d" % (k + 1), 4 * a + b, 4 * z, 4), bank(b0 + b, z - a), fpw(b, a, z), A.max)
 
     def quant_x(k, a, z):
@@ -461,13 +460,15 @@ def rank_program(g, core, T, topo):
             if max(a, lo) < min(z, hi):
                 yield max(a, lo), min(z, hi), max(a, lo) + d
 
-    def put_codes(a, z, qs):
+    def put_codes(a, z):
         for s, e, o in runs(a, z):
             v = w("qx3", s, e)
             dma("y", T.oc[:, 4 * o:4 * (o + e - s)], ap(v).bitcast(dt.uint8), "st", [v], [])
+
+    def put_scales(a, z, q, quarters):
         for s, e, o in runs(a, z):
-            for i in range(4):
-                dma(qs[i], T.osc[4 * i:4 * i + 4, o:o + e - s], ap(w("sx3", s, e, 1, 32 * i, 32 * i + 4)), "st", [w("sx3", s, e)], [])
+            for i in quarters:
+                dma(q, T.osc[4 * i:4 * i + 4, o:o + e - s], ap(w("sx3", s, e, 1, 32 * i, 32 * i + 4)), "st", [w("sx3", s, e)], [])
 
     def put_y(a, z, b):
         mm(bank(b, z - a), w("qv", 0, 128), w("svv", 0, 128), w("qx3", a, z), w("sx3", a, z))
@@ -519,20 +520,30 @@ def rank_program(g, core, T, topo):
         scores(1)
         scores(2)
         if k == 0:
-            lin(w("gk", 0, 192), w("gk", 0, 192), 1, GF)
+            lin(w("gk", 0, 96), w("gk", 0, 96), 1, GF)
         for t in range(3):
             tt(w("fl", 64 * t, 64 * t + 64), bank(4 + t, 64), w("sc", 64 * t, 64 * t + 64), A.is_gt)
+            if t == 1:
+                row_lists(k, 0)
         scan(w("rk", 0, 192), w("sc1", 0, 192), w("fl", 0, 192))
-        src, et = w("rk", 7, 256, 8), w("et", 0, 1056)
+        src, et, eq = w("rk", 7, 256, 8), w("et", 0, 512), w("eq", 0, 12)
         op("v", lambda: vec.tensor_copy(ap(et).indirect(ap(L("spread"))), ap(src)), [src, L("spread")], [et])
-        quant(w("qe", 8, 192), w("se", 8, 192), w("et", 32, 768))
-        mm(bank(7, 192), *ccw(k, 0), w("qe", 8, 200), w("se", 8, 200), True, False)
-        mm(bank(7, 192), *ccw(k, 1), w("qe", 0, 192), w("se", 0, 192), False, True)
-        for b in (2, 3):
-            act(fpw(b), bank(b, C))
-        row_lists(k)
-        tt(w("eq", 0, 192), bank(7, 192), w("gk", 0, 192), A.is_equal)
-        tt(w("pr", 0, 192), w("lsh", 0, 192), w("eq", 0, 192), A.mult, ind=L("cand"))
+        quant(w("qe", 0, 128), w("se", 0, 128), et)
+        for j in range(2):
+            mm(bank(6 + j, 128), *ccw(k, j), w("qe", 0, 128), w("se", 0, 128))
+        act(fpw(2), bank(2, C))
+        act(w("lsr", 0, 192), w("lsh", 0, 192), ind=L("cand"))
+        act(fpw(3), bank(3, C))
+        row_lists(k, 1)
+        row_lists(k, 2)
+        if not last:
+            ts(L("tn%d" % (k + 1)), DROW, float(H[k + 1]), A.mult, Q16, A.add)
+            turner(k + 1)
+        for j in range(2):
+            a, b = bank(6 + j, 96), w("gk", 0, 96)
+            op("v", lambda: vec.tensor_tensor(T.eq[:, :, 8 * j:8 * j + 8], ap(a), ap(b), A.is_equal), [a, b], [w("eq", j, 12, 2)])
+        a, b = w("pr", 0, 192), w("lsr", 0, 192)
+        op("v", lambda: vec.tensor_tensor(ap(a), ap(b), T.eq[:, :, :], A.mult), [b, eq], [a])
         scan(own, w("c8", 0, 192), w("pr", 0, 192))
         halo(k + 1, n, 192)
         add_f(k, 0, mid, 4)
@@ -541,20 +552,23 @@ def rank_program(g, core, T, topo):
         copy(w("mi", 0, 32), own, L("own%d" % k))
         gather("mi", 0, a1, (0, 1), "v")
         gather("mi", 0, a1, (2, 3), "s")
-        if k == 0:
-            turner(2)
-        else:
+        if k:
             gather("mi", a2, 24, range(4), "s")
+        if k == 0:
+            ts(w("d3", 0, 24), w("d24", 0, 24), G16, A.add, 0.33333334, A.mult)
         layer(k, 0, mid, 4)
+        if k == 0:
+            ts(w("d4", 0, 24), w("d3", 0, 24), 3.0, A.mult, G16, A.subtract)
+            ts(L("nat"), io2(4), 8.0, A.mult, HL, A.add)
+            tt(w("dm", 0, 24), w("d4", 0, 24), w("d24", 0, 24), A.is_equal)
         if last:
-            turn(3, "s")
+            turn(3, 0)
+            turn(3, 1, "s")
             for m in range(8):
                 v = w("ot", 16 * (m % 2), 16 * (m % 2) + 16, 1, 32 * (m // 2), 32 * (m // 2) + 24)
                 dma("y", T.op[m:m + 1, :], ap(v), "st", [v], [])
-        new_x(k, 0, mid, 4)
+        new_x(k, 0, mid, 4, range(4) if last else range(EARLY[k]))
         if not last:
-            if k == 0:
-                quant_x(1, 0, mid)
             rows(k + 1, whole, "s")
             fan_out(k + 1)
             tt(w("sm", 0, 32), whole, w("dm", 0, 32), A.mult, ind=L("all%d" % k, 2, 4))
@@ -568,8 +582,7 @@ def rank_program(g, core, T, topo):
                     act(w("ys", b, 512, 4), bwin(b), ind=sv)
             quant(w("qys", 0, 128), w("sys0", 0, 128), w("ys", 0, 512))
             gather("mu", a1, a2, (0,), "s")
-            if k == 1:
-                quant_x(2, 0, mid)
+            new_x(k, 0, mid, 4, range(EARLY[k], 4))
             for b in range(4):
                 mm(bank(b, 128), *wb(b), w("qys", 0, 128), w("sys0", 0, 128))
                 act(w("rs", 64 * b, 64 * b + 64), bank(b, 128, 0, 2), F.Relu, 0.015625)
@@ -583,14 +596,19 @@ def rank_program(g, core, T, topo):
             fan_in(k + 1)
             gather("mu", a1, a2, (3,), "v")
             layer(k, mid, C, 4)
+            if k == 0:
+                ts(L("same"), io2(4), 8.0, A.mult, Q, A.add)
+            turn(k + 1, 0)
             pick(w("bc%d" % (k + 1), 64 * rank, 64 * rank + 64), w("bs%d" % (k + 1), 64 * rank, 64 * rank + 64), q, s, L("same"))
+            turn(k + 1, 1, "s")
             new_x(k, mid, C, 4)
-            quant_x(k + 1, mid, C)
+            quant_x(k + 1, 0, C)
             unpack_f(k + 1, (0, 1))
-            turn(k + 1, "v")
-            turn_back()
+            turn(k + 1, 2)
+            turner_q(k + 1, (0,))
+            turn(k + 1, 3)
+            turner_q(k + 1, (1,))
             if k == 1:
-                turner_q(2)
                 quant(w("qv", 0, 128), w("svv", 0, 128), w("vt", 0, 512))
         else:
             add_f(k, mid, C, 0)
@@ -599,12 +617,16 @@ def rank_program(g, core, T, topo):
             gather("mu", a1, a2, (0, 1), "v")
             layer(k, mid, C, 0)
             quant_x(3, 0, mid)
-            put_codes(0, mid, "yyyy")
+            put_codes(0, mid)
+            put_scales(0, mid, "y", range(4))
             put_y(0, mid, 4)
             new_x(k, mid, C, 0)
             quant_x(3, mid, C)
-            put_codes(mid, C, "syyy")
+            put_codes(mid, C)
+            put_scales(mid, C, "y", (0, 1))
+            put_scales(mid, C, "s", (2,))
             put_y(mid, C, 5)
+            put_scales(mid, C, "s", (3,))
     for sem in SEMAPHORES:
         if total.get(sem, 0):
             wait("g", sem, total[sem])

@@ -6,6 +6,7 @@ H = [4, 2, 1]
 DC = [0, 1, 1, 1, 0, -1, -1, -1]
 EARLY = [2, 2]
 FS = 5
+OPT = {"g0": 0, "c1": [0, 0, 0], "dk": [2, 1, 1]}
 ROT = 128
 
 SCRATCH = {}
@@ -23,25 +24,24 @@ for _r in range(4):
     _b("qx%d" % _r, C, X4)
     _b("sx%d" % _r, C, U8)
 _b("ext0", 40, I32)
-SCRATCH["eq"] = ("sbuf", [128, 12, 16], BF)
 for _r in range(3):
     _b("ext%d" % (_r + 1), 192 + 32 * H[_r], BF)
     _b("bc%d" % _r, 256, X4)
     _b("bs%d" % _r, 256, U8)
     SCRATCH["fan%d" % _r] = ("dram", [16 + 2 * H[_r], 8, 24], BF)
-for _r in (1, 2):
+for _r in range(3):
     _b("qs%d" % _r, 128, X4)
     _b("ss%d" % _r, 128, U8)
 for _n, _c, _t in (("fp", 4 * C, BF), ("bp", 1024, BF), ("gz", 2 * C, BF), ("zt", 4 * C, BF), ("yt", 4 * C, BF), ("ys", 512, BF), ("xsd", 512, BF),
-                   ("lfw", 64, BF), ("tl", 64, BF), ("tg", 32, BF), ("lf", 32, BF), ("lu", 32, U16), ("mi", 32, U16), ("mu", 32, U16), ("sv", 8, U16), ("lsh", 192, BF), ("lsr", 192, BF),
+                   ("lfw", 64, BF), ("tl", 64, BF), ("tg", 32, BF), ("lf", 32, BF), ("lu", 32, U16), ("mi", 32, U16), ("mu", 32, U16), ("sv", 8, U16), ("lsh", 384, BF), ("lsr", 192, BF),
                    ("qz", C, X4), ("sz", C, U8), ("qy", C, X4), ("sy", C, U8), ("qys", 128, X4), ("sys0", 128, U8),
-                   ("sc", 192, F32), ("fl", 192, BF), ("rk", 256, BF), ("et", 512, BF), ("qe", 128, X4), ("se", 128, U8), ("pr", 192, BF),
-                   ("sm", 32, BF), ("sn", 24, BF), ("rs", 256, F32), ("yo", C, F32), ("ot", 32, F32),
+                   ("sc", 192, F32), ("fl", 192, BF), ("rk", 256, BF), ("et", 512, BF), ("qe", 128, X4), ("se", 128, U8), ("ne", 192, BF),
+                   ("sm", 32, BF), ("sn", 24, BF), ("fs", 256, BF), ("i16", 16, F32), ("yo", C, F32), ("ot", 32, F32),
                    ("ut", 512, BF), ("vt", 512, BF), ("qu", 128, X4), ("suu", 128, U8), ("qua", 128, X4), ("sua", 128, U8), ("qv", 128, X4), ("svv", 128, U8),
                    ("wq", 512, X4), ("wsc", 512, U8), ("wd", 528, BF), ("ce", 512, X4), ("cs", 512, U8), ("ct", 528, BF), ("cc", 768, X4), ("ccs", 768, U8),
                    ("ci", 8, I32), ("cf", 40, F32), ("dd", 16, F32), ("da", 16, F32), ("io2", 12, F32), ("ib", 4, F32), ("bt", 16, F32), ("tw", 32, F32), ("sw", 12, F32),
                    ("i64", 64, F32), ("i128", 128, F32), ("eye", 64, BF), ("d24", 24, F32), ("d3", 24, I32), ("d4", 24, F32), ("dm", 32, BF), ("c3", 24, BF),
-                   ("gk", 96, BF), ("sc1", 192, BF), ("c8", 192, BF), ("ls", 100, U16)):
+                   ("gk", 96, BF), ("sc1", 192, BF), ("i12", 12, F32), ("ls", 120, U16)):
     _b(_n, _c, _t)
 SEMAPHORES = ["kv", "ks", "kt", "kg", "lx", "lp", "lu", "lw", "lv", "st", "loc", "ha0", "ha1", "ha2", "ha3"]
 for _r in range(3):
@@ -49,7 +49,7 @@ for _r in range(3):
 
 LISTS, _at = {}, 0
 for _n, _c in (("rows0", 4), ("rows1", 4), ("rows2", 4), ("rows3", 4), ("turn", 6), ("rot", 2), ("seed", 4), ("nat", 4), ("pair", 8), ("spread", 2), ("cand", 12),
-               ("tn0", 8), ("tn1", 8), ("tn2", 8), ("all0", 4), ("all1", 4), ("all2", 4), ("own0", 2), ("own1", 2), ("own2", 2), ("same", 4)):
+               ("tn0", 8), ("tn1", 8), ("tn2", 8), ("all0", 4), ("all1", 4), ("all2", 4), ("own0", 2), ("own1", 2), ("own2", 2), ("wide", 8), ("slot", 16)):
     LISTS[_n] = (_at, _at + _c)
     _at += _c
 
@@ -62,7 +62,7 @@ def rank_program(g, core, T, topo):
     N = len(T.cores)
     vec, sca, ten, syn = g.vector, g.scalar, g.tensor, g.sync
     queue = {"v": vec, "s": sca, "t": ten, "g": g, "y": syn}
-    total, seen, log = {}, {q: {} for q in queue}, {}
+    total, seen, log, behind = {}, {q: {} for q in queue}, {}, {}
 
     def w(name, a, b, step=1, p0=0, p1=128):
         return (name, a, b, step, p0, p1)
@@ -83,6 +83,8 @@ def rank_program(g, core, T, topo):
         if seen[q].get(sem, 0) < val:
             queue[q].wait_ge(T.sem[sem], int(val))
             seen[q][sem] = val
+            for s, n in behind.get((sem, val), {}).items():
+                seen[q][s] = max(seen[q].get(s, 0), n)
 
     def order(q, reads, writes, acc, dma):
         for vs, wr in ((reads, False), (writes, True)):
@@ -93,9 +95,8 @@ def rank_program(g, core, T, topo):
                         continue
                     if not (wr or owr or (bank and oq != q)):
                         continue
-                    if oq == q and not odma and not dma:
-                        if (acc and wr) or not owr:
-                            continue
+                    if oq == q and acc and wr and owr:
+                        continue
                     wait(q, osem, total[osem] if odma else oval)
 
     def note(q, reads, writes, sem, val, dma):
@@ -111,6 +112,7 @@ def rank_program(g, core, T, topo):
         sem = "k" + q
         total[sem] = total.get(sem, 0) + 1
         call().then_inc(T.sem[sem], 1)
+        behind[(sem, total[sem])] = dict(seen[q])
         note(q, reads, writes, sem, total[sem], False)
 
     def dma(q, out, in_, sem, reads, writes, after=()):
@@ -214,14 +216,15 @@ def rank_program(g, core, T, topo):
         arrive(top, s, len(hu) + len(hd))
         arrive(low, s, len(hu) + len(hd))
 
+    def mine(k):
+        return w("bc%d" % k, 64 * rank, 64 * rank + 64), w("bs%d" % k, 64 * rank, 64 * rank + 64)
+
     def seeds(k):
         m = bits(topo.engines(core, T.cores[others[0]]))
         ids = [dst(r) for r in others]
-        a, b = 64 * rank, 64 * rank + 64
-        bq, bs = w("bc%d" % k, a, b), w("bs%d" % k, a, b)
-        q, s = (bq, bs) if k == 0 else (w("qs%d" % k, 0, 64), w("ss%d" % k, 0, 64))
-        fused([(ids, m, "se%d" % k, ap(q).bitcast(dt.uint8), [ap(bq).bitcast(dt.uint8) for r in others])], [q])
-        fused([(ids, m, "se%d" % k, ap(s), [ap(bs) for r in others])], [s])
+        q, s = mine(k)
+        fused([(ids, m, "se%d" % k, ap(q).bitcast(dt.uint8), [ap(q).bitcast(dt.uint8) for r in others])], [q])
+        fused([(ids, m, "se%d" % k, ap(s), [ap(s) for r in others])], [s])
         n = 2 * len(others) * bin(m).count("1")
         for r in others:
             arrive(w("bc%d" % k, 64 * r, 64 * r + 64), "se%d" % k, n)
@@ -238,13 +241,14 @@ def rank_program(g, core, T, topo):
     def fc(i, n=1):
         return w("cf", i, i + n)
 
-    Q, LO, L3, C31, O1, P, G16, H8, B32, X64, PM8, Q6, HL, HI, LO16, E0, LH, Q16, GF, TMP = [fc(i) for i in range(20)]
+    Q, LO, L3, C31, O1, P, L3H, H8, B32, X64, PM8, Q6, HL, HI, LO16, E0, LH, Q16, GF, TMP = [fc(i) for i in range(20)]
+    G16, HL2 = fc(26), fc(27)
     X7, EL = fc(20, 3), fc(24, 2)
     DR, D2, DROW = w("dd", 0, 1), w("dd", 1, 3), w("dd", 3, 11)
     io2 = lambda n: w("io2", 0, n)
 
     iota(w("ci", 5, 6), [[0, 1]], 0, 1)
-    iota(w("ci", 6, 7), [[0, 1]], 0, 3)
+    iota(w("ci", 7, 8), [[0, 1]], 0, 3)
     iota(io2(12), [[2, 12]], 0, 0)
     iota(w("i128", 0, 128), [[1, 128]], 0, 0)
     iota(w("ib", 0, 4), [[-8, 2], [16, 2]], 8, 1)
@@ -255,8 +259,9 @@ def rank_program(g, core, T, topo):
     ts(w("ci", 0, 1), w("ci", 5, 6), 15, A.bitwise_and)
     ts(w("ci", 3, 4), w("ci", 5, 6), 31, A.bitwise_and)
     ts(w("ci", 4, 5), w("ci", 5, 6), 1, A.bitwise_and)
-    ts(w("ci", 1, 3), w("ci", 5, 7), 7, A.bitwise_and)
-    copy(fc(0, 6), w("ci", 0, 6))
+    ts(w("ci", 1, 3), w("ci", 5, 8, 2), 7, A.bitwise_and)
+    ts(w("ci", 6, 7), w("ci", 7, 8), 1, A.arith_shift_right, 7, A.bitwise_and)
+    copy(fc(0, 7), w("ci", 0, 7))
     lin(w("da", 3, 11), io2(8), 0.5, -2, F.Abs)
     lin(Q6, Q, 6, 0)
     lin(G16, P, -1, Q)
@@ -294,9 +299,8 @@ def rank_program(g, core, T, topo):
         for e in range(2):
             act(w("ct", 2 * (i % 2) + e, 512, 4), w("eye", 16 * e, 16 * e + 48), ind=L("tn%d" % i))
 
-    lin(LH, H8, 0.125, 0)
     lin(E0, LO, 4, B32)
-    lin(LH, LO, 24, LH)
+    lin(HL, H8, 1, L3)
     lin(TMP, E0, 1, 128)
     lin(fc(25), H8, 48, E0)
     lin(fc(24), H8, 16, TMP)
@@ -304,8 +308,9 @@ def rank_program(g, core, T, topo):
         quant(*ceb(b), w("wd", 3 - b, 515 - b))
 
     quant(w("qx0", 0, C), w("sx0", 0, C), w("xt0", 0, 4 * C))
-    pick(w("bc0", 64 * rank, 64 * rank + 64), w("bs0", 64 * rank, 64 * rank + 64), w("qx0", 0, C), w("sx0", 0, C), L("seed"))
+    pick(*mine(0), w("qx0", 0, C), w("sx0", 0, C), L("seed"))
     seeds(0)
+    iota(w("i16", 0, 16), [[256, 4], [16, 4]], 64 * rank, 0)
     ts(w("eye", 0, 64), w("i64", 0, 64), C31, A.is_equal)
     ts(L("tn0"), DROW, float(H[0]), A.mult, Q16, A.add)
     ts(w("tw", 8, 14), w("tw", 0, 6), 0.0, A.is_lt, 48.0, A.mult)
@@ -316,16 +321,17 @@ def rank_program(g, core, T, topo):
     tt(w("tw", 24, 30), w("tw", 8, 14), w("tw", 0, 6), A.add)
     iota(w("et", 0, 512), [[0, 512]], 0, 0)
     iota(w("rk", 192, 256), [[0, 64]], 0, 0)
+    iota(w("lsh", 168, 192), [[0, 24]], 0, 0)
     iota(w("d24", 0, 24), [[0, 8], [1, 3]], 0, 1)
-    iota(w("c8", 0, 192), [[0, 192]], 1, 0)
-    keep_if(w("sc1", 0, 192), [[0, 3], [1, 8], [-1, 8]], A.not_equal, -1.0, w("c8", 0, 192))
+    iota(w("i12", 0, 12), [[1, 2], [4, 6]], 0, 0)
+    iota(w("sc1", 0, 192), [[0, 192]], 1, 0)
+    keep_if(w("sc1", 0, 192), [[0, 3], [1, 8], [-1, 8]], A.not_equal, -1.0)
     keep_if(w("sc1", 0, 192), [[0, 24], [1, 8]], A.is_gt, 0.0)
-    keep_if(w("c8", 0, 192), [[0, 24], [1, 8]], A.is_gt, 0.0)
     iota(w("gk", 0, 96), [[0, 12], [-1, 8]], 0, 0)
     iota(w("c3", 0, 24), [[0, 24]], 1, 0)
     keep_if(w("c3", 0, 24), [[0, 8], [1, 3]], A.is_gt, 0.0)
     iota(w("dm", 24, 32), [[0, 8]], 0, 0)
-    iota(w("xsd", 256, 512), [[0, 256]], 0, 0)
+    iota(w("xsd", 0, 512), [[0, 512]], 0, 0)
 
     def bank(b, n, a=0, step=1):
         return w("ps%d" % b, a, n, step)
@@ -333,11 +339,11 @@ def rank_program(g, core, T, topo):
     def fpw(b, a=0, e=C):
         return w("fp", C * b + a, C * b + e)
 
-    def unpack_f(k, bs):
+    def unpack_f(k, bs, a=0, z=C, b0=0):
         for b in bs:
-            mm(bank(b, C), *ceb(b), w("qx%d" % k, 0, C), w("sx%d" % k, 0, C))
+            mm(bank(b0 + b, z - a), *ceb(b), w("qx%d" % k, a, z), w("sx%d" % k, a, z))
             if b < 2:
-                act(fpw(b), bank(b, C))
+                act(fpw(b, a, z), bank(b0 + b, z - a))
 
     def ccw(i, e):
         a = 256 * i + 128 * e
@@ -357,10 +363,15 @@ def rank_program(g, core, T, topo):
     ts(L("pair", 4, 8), w("sw", 0, 4), LO16, A.min)
     quant(w("qu", 0, 128), w("suu", 0, 128), w("ut", 0, 512))
     pick(w("qua", 0, 128), w("sua", 0, 128), w("qu", 0, 128), w("suu", 0, 128), L("pair"))
-    lin(GF, G16, -0.0625, 0)
-    lin(HL, H8, 1, L3)
-    for i, h in enumerate(H):
-        lin(fc(20 + i), DR, 16 * h, 7)
+
+    def later_columns():
+        lin(w("gk", 0, 96), w("gk", 0, 96), 1, GF)
+        lin(TMP, O1, -7, 0)
+        lin(PM8, O1, 7, -7)
+        lin(w("bt", 8, 12), w("bt", 0, 4), 1, TMP)
+        lin(w("bt", 12, 14), w("bt", 4, 6), 1, PM8)
+        for i, h in enumerate(H):
+            lin(fc(20 + i), DR, 16 * h, 14)
 
     def rows(k, src, on):
         if on == "v":
@@ -396,7 +407,7 @@ def rank_program(g, core, T, topo):
     def fan_in(k):
         t, h = T["fan%d" % k], H[k]
         for m in range(8):
-            o = w("lsh", 0, 192, 1, 16 * m, 16 * m + 16)
+            o = w("lsh", 192, 384, 1, 16 * m, 16 * m + 16)
             a = h + h * DC[m]
             dma("y", ap(o), t[a:a + 16, :, :], "fr%d" % k, [], [o], ["fw%d" % k])
 
@@ -404,9 +415,15 @@ def rank_program(g, core, T, topo):
     fan_out(0)
     fan_in(0)
     dma("y", ap(w("vt", 0, 512)), T.v[:, :], "lv", [], [w("vt", 0, 512)])
+    lin(LH, H8, 0.25, 0)
+    lin(fc(28), LO, 192, -6 * 192, F.Relu)
+    lin(LH, LO, 24, LH)
+    lin(HL2, HL, 2, 0)
+    lin(GF, G16, -0.0625, 0)
+    lin(LH, fc(28), 1, LH)
     copy(L("spread"), EL)
     turn(0, 0)
-    ts(L("cand"), io2(12), LH, A.add)
+    ts(L("wide"), io2(8), 4.0, A.mult, L3H, A.add)
     turn(0, 1)
     turner_q(0, (0,))
     turn(0, 2)
@@ -416,13 +433,13 @@ def rank_program(g, core, T, topo):
     def row_lists(i, j):
         h = H[i]
         if j == 0:
-            ts(L("own%d" % i), w("bt", 0, 2), fc(20 + i), A.add, 191.0, A.min)
+            ts(L("own%d" % i), w("bt", 8, 10), fc(20 + i), A.add, 191.0, A.min)
         elif j == 1:
-            ts(L("all%d" % i), w("bt", 0, 4), fc(20 + i), A.add, 16.0 * h, A.add)
+            ts(L("all%d" % i), w("bt", 8, 12), fc(20 + i), A.add, 16.0 * h, A.add)
         elif i < 2:
-            ts(L("rows%d" % (i + 1)), w("bt", 2, 6), fc(21 + i), A.add, 16.0 * h, A.add)
+            ts(L("rows%d" % (i + 1)), w("bt", 10, 14), fc(21 + i), A.add, 16.0 * h, A.add)
         else:
-            ts(L("rows3"), w("bt", 2, 6), 7.0, A.add)
+            ts(L("rows3"), w("bt", 10, 14), 14.0, A.add)
 
     def bwin(b):
         return w("bp", 256 * b, 256 * b + 256)
@@ -486,7 +503,7 @@ def rank_program(g, core, T, topo):
 
         def unpack_b(b):
             mm(bank(4 + b, 256), *ceb(b), w("bc%d" % k, 0, 256), w("bs%d" % k, 0, 256))
-            if b == 0:
+            if b == 0 or (b == 1 and OPT["c1"][k]):
                 copy(bwin(b), bank(4 + b, 256))
             else:
                 act(bwin(b), bank(4 + b, 256))
@@ -501,11 +518,19 @@ def rank_program(g, core, T, topo):
             mm(bank(4 + t, 128), qz, sz, w("qua", 0, 128), w("sua", 0, 128))
             act(w("sc", 64 * t, 64 * t + 64), bank(4 + t, 128, 64))
 
+        def steps():
+            tt(w("lsh", 0, 168), w("lsh", 192, 360), w("lsh", 216, 384), A.subtract)
+
+        if OPT["dk"][k] == 0:
+            steps()
         unpack_b(0)
         unpack_b(2)
-        unpack_b(1)
-        unpack_f(k, (2,))
+        if not OPT["c1"][k]:
+            unpack_b(1)
         tt(w("zt", 0, 4 * C, 4), bwin(0), fpw(0), A.subtract, ind=lu)
+        if OPT["c1"][k]:
+            unpack_b(1)
+        unpack_f(k, (2,))
         act(w("gz", 0, C), bwin(2), ind=lu)
         tt(w("zt", 1, 4 * C, 4), bwin(1), fpw(1), A.subtract, ind=lu)
         unpack_b(3)
@@ -520,31 +545,36 @@ def rank_program(g, core, T, topo):
         scores(1)
         scores(2)
         if k == 0:
-            lin(w("gk", 0, 96), w("gk", 0, 96), 1, GF)
+            later_columns()
+            ts(L("cand"), w("i12", 0, 12), LH, A.add)
         for t in range(3):
             tt(w("fl", 64 * t, 64 * t + 64), bank(4 + t, 64), w("sc", 64 * t, 64 * t + 64), A.is_gt)
-            if t == 1:
-                row_lists(k, 0)
+            if t == 0 and OPT["dk"][k] == 1:
+                steps()
+            if t == 0 and k == 0:
+                ts(L("slot"), w("i16", 0, 16), HL, A.add)
+                ts(L("nat"), io2(4), 16.0, A.mult, HL2, A.add)
         scan(w("rk", 0, 192), w("sc1", 0, 192), w("fl", 0, 192))
-        src, et, eq = w("rk", 7, 256, 8), w("et", 0, 512), w("eq", 0, 12)
+        src, et = w("rk", 7, 256, 8), w("et", 0, 512)
         op("v", lambda: vec.tensor_copy(ap(et).indirect(ap(L("spread"))), ap(src)), [src, L("spread")], [et])
         quant(w("qe", 0, 128), w("se", 0, 128), et)
         for j in range(2):
             mm(bank(6 + j, 128), *ccw(k, j), w("qe", 0, 128), w("se", 0, 128))
-        act(fpw(2), bank(2, C))
-        act(w("lsr", 0, 192), w("lsh", 0, 192), ind=L("cand"))
+        if OPT["dk"][k] == 2:
+            act(fpw(2), bank(2, C))
+            steps()
+        act(w("lsr", 0, 192), w("lsh", 0, 384), ind=L("cand"))
+        if OPT["dk"][k] != 2:
+            act(fpw(2), bank(2, C))
         act(fpw(3), bank(3, C))
-        row_lists(k, 1)
-        row_lists(k, 2)
-        if not last:
-            ts(L("tn%d" % (k + 1)), DROW, float(H[k + 1]), A.mult, Q16, A.add)
-            turner(k + 1)
+        if k:
+            row_lists(k, 1)
+            row_lists(k, 2)
+        row_lists(k, 0)
         for j in range(2):
-            a, b = bank(6 + j, 96), w("gk", 0, 96)
-            op("v", lambda: vec.tensor_tensor(T.eq[:, :, 8 * j:8 * j + 8], ap(a), ap(b), A.is_equal), [a, b], [w("eq", j, 12, 2)])
-        a, b = w("pr", 0, 192), w("lsr", 0, 192)
-        op("v", lambda: vec.tensor_tensor(ap(a), ap(b), T.eq[:, :, :], A.mult), [b, eq], [a])
-        scan(own, w("c8", 0, 192), w("pr", 0, 192))
+            tt(w("ne", 96 * j, 96 * j + 96), bank(6 + j, 96), w("gk", 0, 96), A.not_equal)
+        for j in range(2):
+            scan(w(e, n + j, n + 192, 2), w("ne", 96 * j, 96 * j + 96), w("lsr", 96 * j, 96 * j + 96))
         halo(k + 1, n, 192)
         add_f(k, 0, mid, 4)
         if last:
@@ -554,13 +584,21 @@ def rank_program(g, core, T, topo):
         gather("mi", 0, a1, (2, 3), "s")
         if k:
             gather("mi", a2, 24, range(4), "s")
+        if not last:
+            act(w("fs", 0, 256), w("bp", 0, 1024), ind=L("slot"))
         if k == 0:
             ts(w("d3", 0, 24), w("d24", 0, 24), G16, A.add, 0.33333334, A.mult)
         layer(k, 0, mid, 4)
         if k == 0:
+            pick(w("qs0", 0, 128), w("ss0", 0, 128), *mine(0), L("wide"))
+        if not last:
+            for b in range(4):
+                mm(bank(b, 128), *ceb(b), w("qs%d" % k, 0, 128), w("ss%d" % k, 0, 128), True, False)
+        if k == 0:
             ts(w("d4", 0, 24), w("d3", 0, 24), 3.0, A.mult, G16, A.subtract)
-            ts(L("nat"), io2(4), 8.0, A.mult, HL, A.add)
+            row_lists(k, 1)
             tt(w("dm", 0, 24), w("d4", 0, 24), w("d24", 0, 24), A.is_equal)
+            row_lists(k, 2)
         if last:
             turn(3, 0)
             turn(3, 1, "s")
@@ -575,35 +613,37 @@ def rank_program(g, core, T, topo):
             copy(w("mu", 0, 32), whole, L("all%d" % k, 0, 2))
             scan(w("sn", 0, 24), w("c3", 0, 24), w("sm", 0, 24))
             copy(sv, w("sn", 2, 24, 3))
+            gather("mu", a1, a2, range(OPT["g0"]), "s")
             for b in (2, 0, 3, 1):
                 if b < 2:
-                    copy(w("ys", b, 512, 4), bwin(b), sv)
+                    ts(w("ys", b, 512, 4), bwin(b), 0.015625, A.mult, ind=sv)
                 else:
-                    act(w("ys", b, 512, 4), bwin(b), ind=sv)
+                    act(w("ys", b, 512, 4), bwin(b), scale=0.015625, ind=sv)
             quant(w("qys", 0, 128), w("sys0", 0, 128), w("ys", 0, 512))
-            gather("mu", a1, a2, (0,), "s")
-            new_x(k, 0, mid, 4, range(EARLY[k], 4))
+            gather("mu", a1, a2, range(OPT["g0"], 3), "s")
+            gather("mu", a1, a2, (3,), "v")
             for b in range(4):
-                mm(bank(b, 128), *wb(b), w("qys", 0, 128), w("sys0", 0, 128))
-                act(w("rs", 64 * b, 64 * b + 64), bank(b, 128, 0, 2), F.Relu, 0.015625)
-            add_f(k, mid, C, 4)
-            gather("mu", a1, a2, (1, 2), "s")
+                mm(bank(b, 128), *wb(b), w("qys", 0, 128), w("sys0", 0, 128), False, True)
             for b in range(4):
-                tt(w("xsd", b, 256, 4), w("rs", 64 * b, 64 * b + 64), w("bp", 256 * b + 64 * rank, 256 * b + 64 * rank + 64), A.add, ind=L("nat"))
+                tt(w("xsd", b, 512, 8), bank(b, 128, 0, 2), w("fs", 64 * b, 64 * b + 64), A.max)
             q, s = w("qs%d" % (k + 1), 0, 128), w("ss%d" % (k + 1), 0, 128)
             quant(q, s, w("xsd", 0, 512))
+            pick(*mine(k + 1), q, s, L("nat"))
             seeds(k + 1)
             fan_in(k + 1)
-            gather("mu", a1, a2, (3,), "v")
-            layer(k, mid, C, 4)
-            if k == 0:
-                ts(L("same"), io2(4), 8.0, A.mult, Q, A.add)
+            add_f(k, mid, C, 0)
+            layer(k, mid, C, 0)
+            new_x(k, 0, mid, 4, range(EARLY[k], 4))
+            ts(L("tn%d" % (k + 1)), DROW, float(H[k + 1]), A.mult, Q16, A.add)
+            quant_x(k + 1, 0, mid)
+            turner(k + 1)
+            new_x(k, mid, C, 0, (0,))
             turn(k + 1, 0)
-            pick(w("bc%d" % (k + 1), 64 * rank, 64 * rank + 64), w("bs%d" % (k + 1), 64 * rank, 64 * rank + 64), q, s, L("same"))
+            unpack_f(k + 1, (0, 1), 0, mid, 4)
             turn(k + 1, 1, "s")
-            new_x(k, mid, C, 4)
-            quant_x(k + 1, 0, C)
-            unpack_f(k + 1, (0, 1))
+            new_x(k, mid, C, 0, (1, 2, 3))
+            quant_x(k + 1, mid, C)
+            unpack_f(k + 1, (0, 1), mid, C)
             turn(k + 1, 2)
             turner_q(k + 1, (0,))
             turn(k + 1, 3)

@@ -4,9 +4,9 @@ from concourse.mybir import dt, AluOpType, ActivationFunctionType
 C = 384
 H = [4, 2, 1]
 DC = [0, 1, 1, 1, 0, -1, -1, -1]
-EARLY = [2, 2]
-FS = 5
-OPT = {"g0": 0, "c1": [0, 0, 0], "dk": [2, 1, 1]}
+EARLY = [[0, 0, 3, 6], [0, 3, 6, 6], [0, 1, 1, 2]]
+OPT = {"c3": [1, 1, 1], "zo": "01a2bc", "ce": 2, "tg": 1, "mu": [2, 2], "tt": [2, 2]}
+OWN = 384
 ROT = 128
 
 SCRATCH = {}
@@ -25,31 +25,33 @@ for _r in range(4):
     _b("sx%d" % _r, C, U8)
 _b("ext0", 40, I32)
 for _r in range(3):
-    _b("ext%d" % (_r + 1), 192 + 32 * H[_r], BF)
+    _b("ext%d" % (_r + 1), OWN + 64 * H[_r], BF)
     _b("bc%d" % _r, 256, X4)
     _b("bs%d" % _r, 256, U8)
-    SCRATCH["fan%d" % _r] = ("dram", [16 + 2 * H[_r], 8, 24], BF)
+    if _r:
+        SCRATCH["fan%d" % _r] = ("dram", [16 + 2 * H[_r], 8, 24], BF)
 for _r in range(3):
     _b("qs%d" % _r, 128, X4)
     _b("ss%d" % _r, 128, U8)
 for _n, _c, _t in (("fp", 4 * C, BF), ("bp", 1024, BF), ("gz", 2 * C, BF), ("zt", 4 * C, BF), ("yt", 4 * C, BF), ("ys", 512, BF), ("xsd", 512, BF),
-                   ("lfw", 64, BF), ("tl", 64, BF), ("tg", 32, BF), ("lf", 32, BF), ("lu", 32, U16), ("mi", 32, U16), ("mu", 32, U16), ("sv", 8, U16), ("lsh", 384, BF), ("lsr", 192, BF),
+                   ("lfw", 64, BF), ("tl", 448, BF), ("tg", 32, BF), ("lf", 32, BF), ("lu", 32, U16), ("mi", 32, U16), ("mu", 32, U16), ("sv", 8, U16), ("lsh", 288, BF), ("lsr", 384, BF),
                    ("qz", C, X4), ("sz", C, U8), ("qy", C, X4), ("sy", C, U8), ("qys", 128, X4), ("sys0", 128, U8),
-                   ("sc", 192, F32), ("fl", 192, BF), ("rk", 256, BF), ("et", 512, BF), ("qe", 128, X4), ("se", 128, U8), ("ne", 192, BF),
+                   ("sc", 192, F32), ("fl", 192, BF), ("rk", 256, BF), ("et", 512, BF), ("qe", 128, X4), ("se", 128, U8), ("ne", 384, BF),
                    ("sm", 32, BF), ("sn", 24, BF), ("fs", 256, BF), ("i16", 16, F32), ("yo", C, F32), ("ot", 32, F32),
                    ("ut", 512, BF), ("vt", 512, BF), ("qu", 128, X4), ("suu", 128, U8), ("qua", 128, X4), ("sua", 128, U8), ("qv", 128, X4), ("svv", 128, U8),
-                   ("wq", 512, X4), ("wsc", 512, U8), ("wd", 528, BF), ("ce", 512, X4), ("cs", 512, U8), ("ct", 528, BF), ("cc", 768, X4), ("ccs", 768, U8),
-                   ("ci", 8, I32), ("cf", 40, F32), ("dd", 16, F32), ("da", 16, F32), ("io2", 12, F32), ("ib", 4, F32), ("bt", 16, F32), ("tw", 32, F32), ("sw", 12, F32),
+                   ("wq", 512, X4), ("wsc", 512, U8), ("wd", 528, BF), ("ce", 512, X4), ("cs", 512, U8), ("cc", 768, X4), ("ccs", 768, U8),
+                   ("ci", 8, I32), ("cf", 40, F32), ("dd", 16, F32), ("da", 16, F32), ("io2", 12, F32), ("ib", 4, F32), ("bt", 16, F32), ("tw", 72, F32), ("sw", 12, F32),
                    ("i64", 64, F32), ("i128", 128, F32), ("eye", 64, BF), ("d24", 24, F32), ("d3", 24, I32), ("d4", 24, F32), ("dm", 32, BF), ("c3", 24, BF),
-                   ("gk", 96, BF), ("sc1", 192, BF), ("i12", 12, F32), ("ls", 120, U16)):
+                   ("gk", 96, BF), ("sc1", 192, BF), ("i12", 48, F32), ("lz", 46, F32), ("tb", 22, F32), ("gb", 256, BF), ("ls", 172, U16)):
     _b(_n, _c, _t)
-SEMAPHORES = ["kv", "ks", "kt", "kg", "lx", "lp", "lu", "lw", "lv", "st", "loc", "ha0", "ha1", "ha2", "ha3"]
+SEMAPHORES = ["kv", "ks", "kt", "kg", "lx", "lx2", "lp", "lu", "lw", "lv", "st", "loc", "ha0", "ha1", "ha2", "ha3"]
 for _r in range(3):
     SEMAPHORES += ["se%d" % _r, "fw%d" % _r, "fr%d" % _r]
 
 LISTS, _at = {}, 0
-for _n, _c in (("rows0", 4), ("rows1", 4), ("rows2", 4), ("rows3", 4), ("turn", 6), ("rot", 2), ("seed", 4), ("nat", 4), ("pair", 8), ("spread", 2), ("cand", 12),
-               ("tn0", 8), ("tn1", 8), ("tn2", 8), ("all0", 4), ("all1", 4), ("all2", 4), ("own0", 2), ("own1", 2), ("own2", 2), ("wide", 8), ("slot", 16)):
+for _n, _c in (("rows0", 4), ("turn", 6), ("both", 16), ("rot", 2), ("spread", 2), ("wide", 8), ("tn0", 8),
+               ("cand0", 24), ("rows1", 4), ("rows2", 4), ("rows3", 4), ("seed", 4), ("nat", 4), ("pair", 8), ("cand", 24),
+               ("tn1", 8), ("tn2", 8), ("all0", 4), ("all1", 4), ("all2", 4), ("own0", 2), ("own1", 2), ("own2", 2), ("slot", 16)):
     LISTS[_n] = (_at, _at + _c)
     _at += _c
 
@@ -87,6 +89,7 @@ def rank_program(g, core, T, topo):
                 seen[q][s] = max(seen[q].get(s, 0), n)
 
     def order(q, reads, writes, acc, dma):
+        need = {}
         for vs, wr in ((reads, False), (writes, True)):
             for v in vs:
                 bank = v[0][:2] == "ps"
@@ -97,7 +100,10 @@ def rank_program(g, core, T, topo):
                         continue
                     if oq == q and acc and wr and owr:
                         continue
-                    wait(q, osem, total[osem] if odma else oval)
+                    need[osem] = max(need.get(osem, 0), total[osem] if odma else oval)
+        for sem, val in need.items():
+            if not any(behind.get((s, n), {}).get(sem, 0) >= val for s, n in need.items() if s != sem):
+                wait(q, sem, val)
 
     def note(q, reads, writes, sem, val, dma):
         for v in writes:
@@ -233,10 +239,8 @@ def rank_program(g, core, T, topo):
     cut = 4 * (C - ROT)
     dma("s", ap(w("ext0", 8, 32)), T.p[:, :], "lp", [], [w("ext0", 8, 32)])
     dma("y", ap(w("xt0", 0, cut)), T.x[:, 4 * ROT:4 * C], "lx", [], [w("xt0", 0, cut)])
-    dma("y", ap(w("xt0", cut, 4 * C)), T.x[:, 0:4 * ROT], "lx", [], [w("xt0", cut, 4 * C)])
+    dma("y", ap(w("xt0", cut, 4 * C)), T.x[:, 0:4 * ROT], "lx2", [], [w("xt0", cut, 4 * C)])
     dma("y", ap(w("ut", 0, 512)), T.u[:, :], "lu", [], [w("ut", 0, 512)])
-    dma("y", ap(w("wq", 0, 512)).bitcast(dt.uint8), T.wc[:, :], "lw", [], [w("wq", 0, 512)])
-    dma("y", ap(w("wsc", 0, 512)), T.ws[:, :], "lw", [], [w("wsc", 0, 512)])
 
     def fc(i, n=1):
         return w("cf", i, i + n)
@@ -253,6 +257,8 @@ def rank_program(g, core, T, topo):
     iota(w("i128", 0, 128), [[1, 128]], 0, 0)
     iota(w("ib", 0, 4), [[-8, 2], [16, 2]], 8, 1)
     iota(w("i64", 0, 64), [[0, 2], [-16, 2], [1, 16]], 16, 0)
+    iota(w("tb", 0, 6), [[0, 3], [16, 2]], 0, 0)
+    iota(w("tb", 6, 22), [[64, 4], [16, 2], [0, 2]], 0, 0)
     halo(0, 8, 24)
 
     fill(w("wd", 0, 516), 0.0)
@@ -282,13 +288,12 @@ def rank_program(g, core, T, topo):
     ts(L("seed"), w("sw", 8, 12), -float(ROT), A.add)
     tt(w("bt", 0, 4), w("bt", 8, 12), w("bt", 12, 16), A.add)
     ts(w("da", 0, 11), w("da", 0, 11), -1.0, A.mult, 2.0, A.add)
-    fill(w("ct", 0, 516), 0.0)
     ts(w("dd", 0, 11), w("da", 0, 11), -1.0, A.max, 1.0, A.min)
     lin(HI, H8, 2, 0)
     lin(LO16, LO, 16, 0)
     lin(w("bt", 4, 6), w("bt", 2, 4), 1, PM8)
     lin(w("sw", 0, 4), io2(4), 16, HI)
-    lin(X64, DR, 64, 64)
+    lin(X64, DR, 8, 8)
     for i, s in enumerate((H[0], H[1] - H[0], -1)):
         lin(w("tw", 2 * i, 2 * i + 2), D2, s, Q)
 
@@ -297,41 +302,58 @@ def rank_program(g, core, T, topo):
 
     def turner(i):
         for e in range(2):
-            act(w("ct", 2 * (i % 2) + e, 512, 4), w("eye", 16 * e, 16 * e + 48), ind=L("tn%d" % i))
+            act(w("wd", 2 * (i % 2) + e, 512, 4), w("eye", 16 * e, 16 * e + 48), ind=L("tn%d" % i))
 
+    def Z(name, a=0, b=None):
+        return ("lz",) + L(name, a, b)[1:]
+
+    for j in range(2):
+        lin(w("tw", 6 + j, 22, 2), DROW, H[0], w("tw", j, j + 1))
+    lin(Z("rows0"), w("bt", 2, 6), 0.125, X64)
+    lin(Z("tn0"), DROW, H[0], Q16)
     lin(E0, LO, 4, B32)
-    lin(HL, H8, 1, L3)
-    lin(TMP, E0, 1, 128)
-    lin(fc(25), H8, 48, E0)
-    lin(fc(24), H8, 16, TMP)
-    for b in range(4):
+    for b in range(2):
         quant(*ceb(b), w("wd", 3 - b, 515 - b))
 
-    quant(w("qx0", 0, C), w("sx0", 0, C), w("xt0", 0, 4 * C))
+    quant(w("qx0", 0, C - ROT), w("sx0", 0, C - ROT), w("xt0", 0, cut))
+    quant(w("qx0", C - ROT, C), w("sx0", C - ROT, C), w("xt0", cut, 4 * C))
     pick(*mine(0), w("qx0", 0, C), w("sx0", 0, C), L("seed"))
     seeds(0)
     iota(w("i16", 0, 16), [[256, 4], [16, 4]], 64 * rank, 0)
+    ts(w("tw", 24, 46), w("tw", 0, 22), 0.0, A.is_lt, 48.0, A.mult)
+    ts(w("tw", 48, 70), w("tw", 0, 22), 16.0, A.is_ge, 16.0, A.mult)
+    lin(fc(29), B32, -2, 192)
+    lin(TMP, E0, 1, 128)
+    lin(w("tb", 6, 22), w("tb", 6, 22), 1, fc(29))
+    lin(Z("spread", 1, 2), H8, 48, E0)
+    lin(Z("rot"), w("bt", 0, 2), 0.125, 0)
+    lin(Z("spread", 0, 1), H8, 16, TMP)
+    lin(Z("wide"), io2(8), 4, L3H)
+    lin(HL, H8, 1, L3)
     ts(w("eye", 0, 64), w("i64", 0, 64), C31, A.is_equal)
-    ts(L("tn0"), DROW, float(H[0]), A.mult, Q16, A.add)
-    ts(w("tw", 8, 14), w("tw", 0, 6), 0.0, A.is_lt, 48.0, A.mult)
-    ts(w("tw", 16, 22), w("tw", 0, 6), 16.0, A.is_ge, 16.0, A.mult)
-    ts(L("rows0"), w("bt", 2, 6), X64, A.add, 0.125, A.mult)
-    tt(w("tw", 8, 14), w("tw", 8, 14), w("tw", 16, 22), A.add)
-    ts(L("rot"), w("bt", 0, 2), 0.125, A.mult)
-    tt(w("tw", 24, 30), w("tw", 8, 14), w("tw", 0, 6), A.add)
-    iota(w("et", 0, 512), [[0, 512]], 0, 0)
-    iota(w("rk", 192, 256), [[0, 64]], 0, 0)
-    iota(w("lsh", 168, 192), [[0, 24]], 0, 0)
+    quant(*ceb(2), w("wd", 1, 513))
+    tt(w("tw", 24, 46), w("tw", 24, 46), w("tw", 48, 70), A.add)
+    quant(*ceb(3), w("wd", 0, 512))
+    tt(w("tb", 0, 22), w("tb", 0, 22), w("tw", 0, 22), A.add)
+    ts(L("pair", 0, 4), w("sw", 0, 4), LO16, A.max)
+    tt(Z("turn", 0, 22), w("tw", 24, 46), w("tb", 0, 22), A.add)
+    ts(L("pair", 4, 8), w("sw", 0, 4), LO16, A.min)
+    copy(w("ls", 0, 46), w("lz", 0, 46))
+    quant(w("qu", 0, 128), w("suu", 0, 128), w("ut", 0, 512))
     iota(w("d24", 0, 24), [[0, 8], [1, 3]], 0, 1)
-    iota(w("i12", 0, 12), [[1, 2], [4, 6]], 0, 0)
+    iota(w("tl", 0, 192), [[0, 192]], 0, 0)
+    iota(w("tl", 256, 448), [[0, 192]], 0, 0)
+    iota(w("gk", 0, 96), [[0, 12], [-1, 8]], 0, 0)
+    iota(w("lsh", 256, 288), [[0, 32]], 0, 0)
+    iota(w("i12", 24, 48), [[32, 2], [1, 2], [4, 6]], 0, 0)
     iota(w("sc1", 0, 192), [[0, 192]], 1, 0)
     keep_if(w("sc1", 0, 192), [[0, 3], [1, 8], [-1, 8]], A.not_equal, -1.0)
     keep_if(w("sc1", 0, 192), [[0, 24], [1, 8]], A.is_gt, 0.0)
-    iota(w("gk", 0, 96), [[0, 12], [-1, 8]], 0, 0)
-    iota(w("c3", 0, 24), [[0, 24]], 1, 0)
-    keep_if(w("c3", 0, 24), [[0, 8], [1, 3]], A.is_gt, 0.0)
+    iota(w("rk", 192, 256), [[0, 64]], 0, 0)
+    iota(w("et", 0, 512), [[0, 512]], 0, 0)
+    iota(w("ne", 1, 384, 2), [[0, 192]], 1, 0)
     iota(w("dm", 24, 32), [[0, 8]], 0, 0)
-    iota(w("xsd", 0, 512), [[0, 512]], 0, 0)
+    iota(w("c3", 0, 24), [[0, 24]], 1, 0)
 
     def bank(b, n, a=0, step=1):
         return w("ps%d" % b, a, n, step)
@@ -352,26 +374,26 @@ def rank_program(g, core, T, topo):
     def turner_q(i, es=(0, 1)):
         for e in es:
             o = 2 * (i % 2) + e
-            quant(*ccw(i, e), w("ct", o, o + 512))
+            quant(*ccw(i, e), w("wd", o, o + 512))
 
-    t0 = LISTS["turn"][0]
-    ts(L("pair", 0, 4), w("sw", 0, 4), LO16, A.max)
-    copy(w("ls", t0, t0 + 6, 2), w("tw", 24, 30, 2))
-    ts(w("ls", t0 + 1, t0 + 6, 2), w("tw", 25, 30, 2), 16.0, A.add)
-    unpack_f(0, (0, 1))
+    unpack_f(0, (0,))
     turner(0)
-    ts(L("pair", 4, 8), w("sw", 0, 4), LO16, A.min)
-    quant(w("qu", 0, 128), w("suu", 0, 128), w("ut", 0, 512))
-    pick(w("qua", 0, 128), w("sua", 0, 128), w("qu", 0, 128), w("suu", 0, 128), L("pair"))
 
-    def later_columns():
-        lin(w("gk", 0, 96), w("gk", 0, 96), 1, GF)
-        lin(TMP, O1, -7, 0)
-        lin(PM8, O1, 7, -7)
-        lin(w("bt", 8, 12), w("bt", 0, 4), 1, TMP)
-        lin(w("bt", 12, 14), w("bt", 4, 6), 1, PM8)
-        for i, h in enumerate(H):
-            lin(fc(20 + i), DR, 16 * h, 14)
+    def later_columns(part):
+        if part == 0:
+            lin(Q6, H8, 0.25, 0)
+            lin(fc(28), LO, 32, Q6)
+        elif part == 1:
+            lin(GF, G16, -0.0625, 0)
+            lin(TMP, O1, -15, 0)
+        else:
+            lin(w("gk", 0, 96), w("gk", 0, 96), 1, GF)
+            lin(fc(20), DR, 32 * H[0], 28)
+            lin(w("bt", 8, 12), w("bt", 0, 4), 2, TMP)
+            lin(PM8, O1, 15, -15)
+            lin(fc(21), DR, 32 * H[1], 28)
+            lin(w("bt", 12, 14), w("bt", 4, 6), 2, PM8)
+            lin(HL2, HL, 2, 0)
 
     def rows(k, src, on):
         if on == "v":
@@ -382,13 +404,13 @@ def rank_program(g, core, T, topo):
     def turn(k, step, on="v"):
         j = min(k, 2)
         if step == 0:
-            flip(w("tl", 0, 64), w("lfw", 0, 64))
+            flip(w("tl", 192, 256), w("lfw", 0, 64))
         elif step == 1:
             out = w("ot" if k == 3 else "tg", 0, 32)
             if on == "v":
-                copy(out, w("tl", 0, 64), L("turn", 2 * j, 2 * j + 2))
+                copy(out, w("tl", 192, 256), L("turn", 2 * j, 2 * j + 2))
             else:
-                act(out, w("tl", 0, 64), ind=L("turn", 2 * j, 2 * j + 2))
+                act(out, w("tl", 192, 256), ind=L("turn", 2 * j, 2 * j + 2))
         elif step == 2:
             flip(w("lf", 0, 32), w("tg", 0, 32))
         else:
@@ -397,49 +419,52 @@ def rank_program(g, core, T, topo):
     def fan_out(k):
         t, h = T["fan%d" % k], H[k]
         for m in range(8):
-            d = (h - (H[k - 1] if k else 0)) * DC[m]
+            d = (h - H[k - 1]) * DC[m]
             for lo, hi, col in ((-16, 0, 32), (0, 16, 0), (16, 32, 32)):
                 a, b = max(lo, d - h), min(hi, 16 + d + h)
                 if a < b:
                     v = w("lfw", col, col + 24, 1, 16 * m + a - lo, 16 * m + b - lo)
-                    dma("s" if k == 0 and m >= FS else "y", t[a - d + h:b - d + h, m, :], ap(v), "fw%d" % k, [v], [])
+                    dma("y", t[a - d + h:b - d + h, m, :], ap(v), "fw%d" % k, [v], [])
 
     def fan_in(k):
         t, h = T["fan%d" % k], H[k]
         for m in range(8):
-            o = w("lsh", 192, 384, 1, 16 * m, 16 * m + 16)
+            o = w("lsh", 0, 192, 1, 16 * m, 16 * m + 16)
             a = h + h * DC[m]
-            dma("y", ap(o), t[a:a + 16, :, :], "fr%d" % k, [], [o], ["fw%d" % k])
+            dma("y", ap(o), t[a:a + 16, :, :], "fr%d" % k, [], [o], ["fw%d" % k, "se%d" % k])
 
+    pick(w("qua", 0, 128), w("sua", 0, 128), w("qu", 0, 128), w("suu", 0, 128), L("pair"))
+    unpack_f(0, (1,))
+    later_columns(0)
+    ts(L("slot"), w("i16", 0, 16), HL, A.add)
     rows(0, w("ext0", 0, 40), "v")
-    fan_out(0)
-    fan_in(0)
-    dma("y", ap(w("vt", 0, 512)), T.v[:, :], "lv", [], [w("vt", 0, 512)])
-    lin(LH, H8, 0.25, 0)
-    lin(fc(28), LO, 192, -6 * 192, F.Relu)
-    lin(LH, LO, 24, LH)
-    lin(HL2, HL, 2, 0)
-    lin(GF, G16, -0.0625, 0)
-    lin(LH, fc(28), 1, LH)
-    copy(L("spread"), EL)
+    ts(w("d3", 0, 24), w("d24", 0, 24), G16, A.add, 0.33333334, A.mult)
     turn(0, 0)
-    ts(L("wide"), io2(8), 4.0, A.mult, L3H, A.add)
-    turn(0, 1)
+    for i in range(4):
+        for j in range(4):
+            if i != j:
+                a = 192 + 64 * (i - j)
+                v, o = w("tl", 192, 256, 1, 32 * i, 32 * i + 32), w("tl", a, a + 64, 1, 32 * j, 32 * j + 32)
+                dma("y", ap(o), ap(v), "fr0", [v], [o])
+    dma("y", ap(w("wq", 0, 512)).bitcast(dt.uint8), T.wc[:, :], "lw", [], [w("wq", 0, 512)], ["se0"])
+    dma("y", ap(w("wsc", 0, 512)), T.ws[:, :], "lw", [], [w("wsc", 0, 512)])
     turner_q(0, (0,))
-    turn(0, 2)
+    turn(0, 1)
     turner_q(0, (1,))
+    turn(0, 2)
+    ts(w("d4", 0, 24), w("d3", 0, 24), 3.0, A.mult, G16, A.subtract)
     turn(0, 3)
 
     def row_lists(i, j):
         h = H[i]
         if j == 0:
-            ts(L("own%d" % i), w("bt", 8, 10), fc(20 + i), A.add, 191.0, A.min)
+            ts(L("own%d" % i), w("bt", 8, 10), fc(20 + i), A.add, OWN - 1.0, A.min)
         elif j == 1:
-            ts(L("all%d" % i), w("bt", 8, 12), fc(20 + i), A.add, 16.0 * h, A.add)
+            ts(L("all%d" % i), w("bt", 8, 12), fc(20 + i), A.add, 32.0 * h, A.add)
         elif i < 2:
-            ts(L("rows%d" % (i + 1)), w("bt", 10, 14), fc(21 + i), A.add, 16.0 * h, A.add)
+            ts(L("rows%d" % (i + 1)), w("bt", 10, 14), fc(21 + i), A.add, 32.0 * h, A.add)
         else:
-            ts(L("rows3"), w("bt", 10, 14), 14.0, A.add)
+            ts(L("rows3"), w("bt", 10, 14), 28.0, A.add)
 
     def bwin(b):
         return w("bp", 256 * b, 256 * b + 256)
@@ -487,23 +512,24 @@ def rank_program(g, core, T, topo):
             for i in quarters:
                 dma(q, T.osc[4 * i:4 * i + 4, o:o + e - s], ap(w("sx3", s, e, 1, 32 * i, 32 * i + 4)), "st", [w("sx3", s, e)], [])
 
-    def put_y(a, z, b):
-        mm(bank(b, z - a), w("qv", 0, 128), w("svv", 0, 128), w("qx3", a, z), w("sx3", a, z))
-        act(w("yo", a, z), bank(b, z - a))
+    def put_y(a, z, b, on="s"):
+        n = max(z - a, 128)
+        mm(bank(b, n), w("qv", 0, 128), w("svv", 0, 128), w("qx3", a, a + n), w("sx3", a, a + n))
+        (act if on == "s" else copy)(w("yo", a, z), bank(b, z - a))
         for s, e, o in runs(a, z):
-            dma("s", T.y[:, o:o + e - s], ap(w("yo", s, e)), "st", [w("yo", s, e)], [])
+            dma("s" if on == "s" else "y", T.y[:, o:o + e - s], ap(w("yo", s, e)), "st", [w("yo", s, e)], [])
 
     for k in range(3):
         h, last = H[k], k == 2
-        e, n = "ext%d" % (k + 1), 16 * h
-        own, whole = w(e, n, n + 192), w(e, 0, 2 * n + 192)
+        e, n = "ext%d" % (k + 1), 32 * h
+        own, whole = w(e, n, n + OWN), w(e, 0, 2 * n + OWN)
         lu, sv = w("lu", 0, 24), w("sv", 0, 8)
         a1, a2 = 16 - 2 * h, 16 + 2 * h
         mid = 16 * a1
 
         def unpack_b(b):
             mm(bank(4 + b, 256), *ceb(b), w("bc%d" % k, 0, 256), w("bs%d" % k, 0, 256))
-            if b == 0 or (b == 1 and OPT["c1"][k]):
+            if b == 0:
                 copy(bwin(b), bank(4 + b, 256))
             else:
                 act(bwin(b), bank(4 + b, 256))
@@ -518,143 +544,184 @@ def rank_program(g, core, T, topo):
             mm(bank(4 + t, 128), qz, sz, w("qua", 0, 128), w("sua", 0, 128))
             act(w("sc", 64 * t, 64 * t + 64), bank(4 + t, 128, 64))
 
-        def steps():
-            tt(w("lsh", 0, 168), w("lsh", 192, 360), w("lsh", 216, 384), A.subtract)
-
-        if OPT["dk"][k] == 0:
-            steps()
         unpack_b(0)
         unpack_b(2)
-        if not OPT["c1"][k]:
-            unpack_b(1)
+        unpack_b(1)
+        if OPT["c3"][k]:
+            unpack_b(3)
         tt(w("zt", 0, 4 * C, 4), bwin(0), fpw(0), A.subtract, ind=lu)
-        if OPT["c1"][k]:
-            unpack_b(1)
         unpack_f(k, (2,))
         act(w("gz", 0, C), bwin(2), ind=lu)
         tt(w("zt", 1, 4 * C, 4), bwin(1), fpw(1), A.subtract, ind=lu)
-        unpack_b(3)
+        if not OPT["c3"][k]:
+            unpack_b(3)
         unpack_f(k, (3,))
         tt(w("zt", 2, 4 * C, 4), w("gz", 0, C), bank(2, C), A.subtract)
         for t in range(3):
             act(w("gz", C + 128 * t, C + 128 * t + 128), bwin(3), ind=w("lu", 8 * t, 8 * t + 8))
+        if k == 0:
+            act(w("gb", 0, 256), w("tl", 0, 448), ind=L("both"))
         z_last(0)
         z_last(1)
         scores(0)
+        if k == 0:
+            later_columns(1)
         z_last(2)
         scores(1)
         scores(2)
         if k == 0:
-            later_columns()
-            ts(L("cand"), w("i12", 0, 12), LH, A.add)
+            ts(L("cand0"), w("i12", 24, 48), fc(28), A.add)
+            flip(w("lsh", 0, 256), w("gb", 0, 256))
+        elif k == 1:
+            turner_q(1, (1,))
+            row_lists(k, 0)
+        else:
+            turner_q(2)
+        cand = "cand" if k else "cand0"
+        act(w("lsr", 0, 384, 2), w("lsh", 0, 288), ind=L(cand, 0, 12))
+        act(w("lsr", 1, 384, 2), w("lsh", 0, 288), scale=-1.0, ind=L(cand, 12, 24))
         for t in range(3):
             tt(w("fl", 64 * t, 64 * t + 64), bank(4 + t, 64), w("sc", 64 * t, 64 * t + 64), A.is_gt)
-            if t == 0 and OPT["dk"][k] == 1:
-                steps()
-            if t == 0 and k == 0:
-                ts(L("slot"), w("i16", 0, 16), HL, A.add)
-                ts(L("nat"), io2(4), 16.0, A.mult, HL2, A.add)
         scan(w("rk", 0, 192), w("sc1", 0, 192), w("fl", 0, 192))
         src, et = w("rk", 7, 256, 8), w("et", 0, 512)
         op("v", lambda: vec.tensor_copy(ap(et).indirect(ap(L("spread"))), ap(src)), [src, L("spread")], [et])
         quant(w("qe", 0, 128), w("se", 0, 128), et)
         for j in range(2):
             mm(bank(6 + j, 128), *ccw(k, j), w("qe", 0, 128), w("se", 0, 128))
-        if OPT["dk"][k] == 2:
+        if k == 0:
+            later_columns(2)
+            pick(w("qs0", 0, 128), w("ss0", 0, 128), *mine(0), L("wide"))
+        else:
             act(fpw(2), bank(2, C))
-            steps()
-        act(w("lsr", 0, 192), w("lsh", 0, 384), ind=L("cand"))
-        if OPT["dk"][k] != 2:
-            act(fpw(2), bank(2, C))
-        act(fpw(3), bank(3, C))
-        if k:
+            act(fpw(3), bank(3, C))
+        if k == 1:
             row_lists(k, 1)
             row_lists(k, 2)
-        row_lists(k, 0)
+            ts(L("tn2"), DROW, float(H[2]), A.mult, Q16, A.add)
+        if last:
+            quant(w("qv", 0, 128), w("svv", 0, 128), w("vt", 0, 512))
         for j in range(2):
-            tt(w("ne", 96 * j, 96 * j + 96), bank(6 + j, 96), w("gk", 0, 96), A.not_equal)
+            tt(w("ne", 192 * j, 192 * j + 192, 2), bank(6 + j, 96), w("gk", 0, 96), A.not_equal)
         for j in range(2):
-            scan(w(e, n + j, n + 192, 2), w("ne", 96 * j, 96 * j + 96), w("lsr", 96 * j, 96 * j + 96))
-        halo(k + 1, n, 192)
+            scan(w(e, n + j, n + OWN, 2), w("ne", 192 * j, 192 * j + 192), w("lsr", 192 * j, 192 * j + 192))
+        halo(k + 1, n, OWN)
+        if k == 0:
+            keep_if(w("c3", 0, 24), [[0, 8], [1, 3]], A.is_gt, 0.0)
+            iota(w("xsd", 0, 512), [[0, 512]], 0, 0)
+            iota(w("i12", 0, 24), [[24, 2], [1, 2], [4, 6]], 0, 0)
         add_f(k, 0, mid, 4)
         if last:
             rows(3, own, "s")
+        if k == 0:
+            row_lists(k, 0)
         copy(w("mi", 0, 32), own, L("own%d" % k))
+        if k == 0:
+            row_lists(k, 1)
         gather("mi", 0, a1, (0, 1), "v")
         gather("mi", 0, a1, (2, 3), "s")
         if k:
             gather("mi", a2, 24, range(4), "s")
-        if not last:
-            act(w("fs", 0, 256), w("bp", 0, 1024), ind=L("slot"))
-        if k == 0:
-            ts(w("d3", 0, 24), w("d24", 0, 24), G16, A.add, 0.33333334, A.mult)
+        else:
+            act(fpw(2), bank(2, C))
+            act(fpw(3), bank(3, C))
+            row_lists(k, 2)
         layer(k, 0, mid, 4)
         if k == 0:
-            pick(w("qs0", 0, 128), w("ss0", 0, 128), *mine(0), L("wide"))
+            tt(w("dm", 0, 24), w("d4", 0, 24), w("d24", 0, 24), A.is_equal)
+            ts(L("nat"), io2(4), 16.0, A.mult, HL2, A.add)
+            ts(L("tn1"), DROW, float(H[1]), A.mult, Q16, A.add)
         if not last:
+            act(w("fs", 0, 256), w("bp", 0, 1024), ind=L("slot"))
             for b in range(4):
                 mm(bank(b, 128), *ceb(b), w("qs%d" % k, 0, 128), w("ss%d" % k, 0, 128), True, False)
-        if k == 0:
-            ts(w("d4", 0, 24), w("d3", 0, 24), 3.0, A.mult, G16, A.subtract)
-            row_lists(k, 1)
-            tt(w("dm", 0, 24), w("d4", 0, 24), w("d24", 0, 24), A.is_equal)
-            row_lists(k, 2)
+
+        if k == 1:
+            for j in range(3):
+                row_lists(2, j)
+
+        def inner(at):
+            new_x(k, 0, mid, 4, [b for b in range(4) if EARLY[k][b] == at])
+
         if last:
             turn(3, 0)
             turn(3, 1, "s")
             for m in range(8):
                 v = w("ot", 16 * (m % 2), 16 * (m % 2) + 16, 1, 32 * (m // 2), 32 * (m // 2) + 24)
                 dma("y", T.op[m:m + 1, :], ap(v), "st", [v], [])
-        new_x(k, 0, mid, 4, range(4) if last else range(EARLY[k]))
+        inner(0)
         if not last:
             rows(k + 1, whole, "s")
             fan_out(k + 1)
             tt(w("sm", 0, 32), whole, w("dm", 0, 32), A.mult, ind=L("all%d" % k, 2, 4))
-            copy(w("mu", 0, 32), whole, L("all%d" % k, 0, 2))
+            def edge_list(at):
+                if OPT["mu"][k] == at:
+                    copy(w("mu", 0, 32), whole, L("all%d" % k, 0, 2))
+
+            edge_list(0)
+            inner(1)
             scan(w("sn", 0, 24), w("c3", 0, 24), w("sm", 0, 24))
+            edge_list(1)
+            inner(2)
             copy(sv, w("sn", 2, 24, 3))
-            gather("mu", a1, a2, range(OPT["g0"]), "s")
+            edge_list(2)
             for b in (2, 0, 3, 1):
                 if b < 2:
                     ts(w("ys", b, 512, 4), bwin(b), 0.015625, A.mult, ind=sv)
                 else:
                     act(w("ys", b, 512, 4), bwin(b), scale=0.015625, ind=sv)
+            edge_list(3)
+            inner(3)
             quant(w("qys", 0, 128), w("sys0", 0, 128), w("ys", 0, 512))
-            gather("mu", a1, a2, range(OPT["g0"], 3), "s")
+            gather("mu", a1, a2, range(3), "s")
             gather("mu", a1, a2, (3,), "v")
             for b in range(4):
                 mm(bank(b, 128), *wb(b), w("qys", 0, 128), w("sys0", 0, 128), False, True)
             for b in range(4):
                 tt(w("xsd", b, 512, 8), bank(b, 128, 0, 2), w("fs", 64 * b, 64 * b + 64), A.max)
+            inner(4)
             q, s = w("qs%d" % (k + 1), 0, 128), w("ss%d" % (k + 1), 0, 128)
             quant(q, s, w("xsd", 0, 512))
+            inner(5)
             pick(*mine(k + 1), q, s, L("nat"))
             seeds(k + 1)
             fan_in(k + 1)
+            if k == 0:
+                dma("y", ap(w("vt", 0, 512)), T.v[:, :], "lv", [], [w("vt", 0, 512)])
             add_f(k, mid, C, 0)
             layer(k, mid, C, 0)
-            new_x(k, 0, mid, 4, range(EARLY[k], 4))
-            ts(L("tn%d" % (k + 1)), DROW, float(H[k + 1]), A.mult, Q16, A.add)
-            quant_x(k + 1, 0, mid)
+            if k == 0:
+                lin(LH, LO, 24, Q6)
+                lin(fc(22), DR, 32 * H[2], 28)
             turner(k + 1)
-            new_x(k, mid, C, 0, (0,))
-            turn(k + 1, 0)
+            inner(6)
+            if OPT["tt"][k] == 0:
+                turn(k + 1, 0)
+            quant_x(k + 1, 0, mid)
+            if OPT["tt"][k] == 0:
+                turn(k + 1, 1, "s")
             unpack_f(k + 1, (0, 1), 0, mid, 4)
-            turn(k + 1, 1, "s")
-            new_x(k, mid, C, 0, (1, 2, 3))
+            new_x(k, mid, C, 0)
+            if OPT["tt"][k] == 1:
+                turn(k + 1, 0)
+                turn(k + 1, 1, "s")
             quant_x(k + 1, mid, C)
             unpack_f(k + 1, (0, 1), mid, C)
+            if OPT["tt"][k] == 2:
+                turn(k + 1, 0)
+                turn(k + 1, 1)
             turn(k + 1, 2)
-            turner_q(k + 1, (0,))
+            if k == 0:
+                turner_q(1, (0,))
             turn(k + 1, 3)
-            turner_q(k + 1, (1,))
-            if k == 1:
-                quant(w("qv", 0, 128), w("svv", 0, 128), w("vt", 0, 512))
+            if k == 0:
+                ts(L("cand"), w("i12", 0, 24), LH, A.add)
         else:
             add_f(k, mid, C, 0)
             copy(w("mu", 0, 32), whole, L("all%d" % k, 0, 2))
-            gather("mu", a1, a2, (2, 3), "s")
-            gather("mu", a1, a2, (0, 1), "v")
+            gather("mu", a1, a2, range(OPT["tg"], 4), "s")
+            inner(1)
+            gather("mu", a1, a2, range(OPT["tg"]), "v")
+            inner(2)
             layer(k, mid, C, 0)
             quant_x(3, 0, mid)
             put_codes(0, mid)
@@ -665,8 +732,9 @@ def rank_program(g, core, T, topo):
             put_codes(mid, C)
             put_scales(mid, C, "y", (0, 1))
             put_scales(mid, C, "s", (2,))
-            put_y(mid, C, 5)
+            put_y(C - ROT, C, 5)
+            put_y(mid, C - ROT, 6, "v")
             put_scales(mid, C, "s", (3,))
-    for sem in SEMAPHORES:
+    for sem in [s for s in SEMAPHORES if s != "st"] + ["st"]:
         if total.get(sem, 0):
             wait("g", sem, total[sem])

@@ -4,8 +4,6 @@ from concourse.mybir import dt, AluOpType, ActivationFunctionType
 C = 384
 H = [4, 2, 1]
 DC = [0, 1, 1, 1, 0, -1, -1, -1]
-EARLY = [[0, 0, 3, 6], [0, 3, 6, 6], [0, 1, 1, 2]]
-OPT = {"c3": [1, 1, 1], "zo": "01a2bc", "ce": 2, "tg": 1, "mu": [2, 2], "tt": [2, 2]}
 OWN = 384
 ROT = 128
 
@@ -30,30 +28,29 @@ for _r in range(3):
     _b("bs%d" % _r, 256, U8)
     if _r:
         SCRATCH["fan%d" % _r] = ("dram", [16 + 2 * H[_r], 8, 24], BF)
-for _r in range(3):
-    _b("qs%d" % _r, 128, X4)
-    _b("ss%d" % _r, 128, U8)
-for _n, _c, _t in (("fp", 4 * C, BF), ("bp", 1024, BF), ("gz", 2 * C, BF), ("zt", 4 * C, BF), ("yt", 4 * C, BF), ("ys", 512, BF), ("xsd", 512, BF),
-                   ("lfw", 64, BF), ("tl", 448, BF), ("tg", 32, BF), ("lf", 32, BF), ("lu", 32, U16), ("mi", 32, U16), ("mu", 32, U16), ("sv", 8, U16), ("lsh", 288, BF), ("lsr", 384, BF),
-                   ("qz", C, X4), ("sz", C, U8), ("qy", C, X4), ("sy", C, U8), ("qys", 128, X4), ("sys0", 128, U8),
-                   ("sc", 192, F32), ("fl", 192, BF), ("rk", 256, BF), ("et", 512, BF), ("qe", 128, X4), ("se", 128, U8), ("ne", 384, BF),
-                   ("sm", 32, BF), ("sn", 24, BF), ("fs", 256, BF), ("i16", 16, F32), ("yo", C, F32), ("ot", 32, F32),
-                   ("ut", 512, BF), ("vt", 512, BF), ("qu", 128, X4), ("suu", 128, U8), ("qua", 128, X4), ("sua", 128, U8), ("qv", 128, X4), ("svv", 128, U8),
-                   ("wq", 512, X4), ("wsc", 512, U8), ("wd", 528, BF), ("ce", 512, X4), ("cs", 512, U8), ("cc", 768, X4), ("ccs", 768, U8),
-                   ("ci", 8, I32), ("cf", 40, F32), ("dd", 16, F32), ("da", 16, F32), ("io2", 12, F32), ("ib", 4, F32), ("bt", 16, F32), ("tw", 72, F32), ("sw", 12, F32),
-                   ("i64", 64, F32), ("i128", 128, F32), ("eye", 64, BF), ("d24", 24, F32), ("d3", 24, I32), ("d4", 24, F32), ("dm", 32, BF), ("c3", 24, BF),
-                   ("gk", 96, BF), ("sc1", 192, BF), ("i12", 48, F32), ("lz", 46, F32), ("tb", 22, F32), ("gb", 256, BF), ("ls", 172, U16)):
-    _b(_n, _c, _t)
-SEMAPHORES = ["kv", "ks", "kt", "kg", "lx", "lx2", "lp", "lu", "lw", "lv", "st", "loc", "ha0", "ha1", "ha2", "ha3"]
-for _r in range(3):
-    SEMAPHORES += ["se%d" % _r, "fw%d" % _r, "fr%d" % _r]
 
 LISTS, _at = {}, 0
-for _n, _c in (("rows0", 4), ("turn", 6), ("both", 16), ("rot", 2), ("spread", 2), ("wide", 8), ("tn0", 8),
-               ("cand0", 24), ("rows1", 4), ("rows2", 4), ("rows3", 4), ("seed", 4), ("nat", 4), ("pair", 8), ("cand", 24),
-               ("tn1", 8), ("tn2", 8), ("all0", 4), ("all1", 4), ("all2", 4), ("own0", 2), ("own1", 2), ("own2", 2), ("slot", 16)):
+for _n, _c in (("rows0", 4), ("turn", 6), ("both", 16), ("rot", 2), ("spread", 2), ("tn0", 8),
+               ("cand0", 24), ("cand", 24), ("seed", 4), ("pair", 8), ("tn1", 8), ("tn2", 8), ("rows1", 4), ("rows2", 4), ("rows3", 4),
+               ("all0", 2), ("all1", 2), ("all2", 2), ("own0", 2), ("own1", 2), ("own2", 2)):
     LISTS[_n] = (_at, _at + _c)
     _at += _c
+CAST = LISTS["tn0"][1]
+
+for _n, _c, _t in (("fp", 4 * C, BF), ("bp", 1024, BF), ("gz", 2 * C, BF), ("zt", 4 * C, BF), ("yt", 4 * C, BF),
+                   ("lfw", 64, BF), ("tl", 448, BF), ("tg", 32, BF), ("lf", 32, BF), ("lu", 32, U16), ("mi", 32, U16), ("mu", 32, U16), ("lsh", 288, BF), ("lsr", 384, BF),
+                   ("qz", C, X4), ("sz", C, U8), ("qy", C, X4), ("sy", C, U8),
+                   ("sc", 192, F32), ("fl", 192, BF), ("rk", 256, BF), ("et", 512, BF), ("qe", 128, X4), ("se", 128, U8), ("ne", 384, BF), ("yo", C, F32), ("ot", 32, F32),
+                   ("ut", 512, BF), ("vt", 512, BF), ("qu", 128, X4), ("suu", 128, U8), ("qua", 128, X4), ("sua", 128, U8), ("qv", 128, X4), ("svv", 128, U8),
+                   ("wq", 512, X4), ("wsc", 512, U8), ("wd", 528, BF), ("ce", 512, X4), ("cs", 512, U8), ("cc", 768, X4), ("ccs", 768, U8),
+                   ("ci", 8, I32), ("cf", 32, F32), ("dd", 16, F32), ("da", 16, F32), ("io2", 12, F32), ("ib", 4, F32), ("bt", 16, F32), ("tw", 72, F32), ("sw", 12, F32),
+                   ("i64", 64, F32), ("i128", 128, F32), ("eye", 64, BF), ("gk", 96, BF), ("sc1", 192, BF), ("i12", 48, F32), ("tb", 22, F32), ("gb", 256, BF),
+                   ("lz", CAST, F32), ("ls", _at, U16)):
+    _b(_n, _c, _t)
+SEMAPHORES = ["kv", "ks", "kt", "kg", "lx", "lx2", "lp", "lu", "lw", "lv", "loc", "ha0", "ha1", "ha2", "ha3"]
+for _r in range(3):
+    SEMAPHORES += ["se%d" % _r, "fw%d" % _r, "fr%d" % _r]
+SEMAPHORES += ["st"]
 
 
 def rank_program(g, core, T, topo):
@@ -142,6 +139,9 @@ def rank_program(g, core, T, topo):
     def copy(out, in_, ind=None):
         op("v", lambda: vec.tensor_copy(ap(out), at(in_, ind)), rd(in_, ind), [out])
 
+    def scatter(out, ind, in_):
+        op("v", lambda: vec.tensor_copy(at(out, ind), ap(in_)), [in_, ind], [out])
+
     def tt(out, a, b, o, ind=None):
         op("v", lambda: vec.tensor_tensor(ap(out), at(a, ind), ap(b), o), rd(a, ind) + [b], [out])
 
@@ -162,12 +162,11 @@ def rank_program(g, core, T, topo):
     def fill(out, val):
         op("v", lambda: vec.memset(ap(out), val), [], [out])
 
-    def act(out, in_, func=None, scale=1.0, ind=None):
-        f = F.Copy if func is None else func
+    def act(out, in_, ind=None, scale=1.0):
         if scale == 1.0:
-            op("s", lambda: sca.activation(ap(out), at(in_, ind), f), rd(in_, ind), [out])
+            op("s", lambda: sca.activation(ap(out), at(in_, ind), F.Copy), rd(in_, ind), [out])
         else:
-            op("s", lambda: sca.activation(ap(out), at(in_, ind), f, scale=scale), rd(in_, ind), [out])
+            op("s", lambda: sca.activation(ap(out), at(in_, ind), F.Copy, scale=scale), rd(in_, ind), [out])
 
     def lin(out, in_, scale, bias, func=None):
         col = isinstance(bias, tuple)
@@ -186,17 +185,22 @@ def rank_program(g, core, T, topo):
         else:
             op("g", lambda: g.iota(ap(out), pat, base, cm), [], [out])
 
-    def keep_if(v, pat, cmp, other, src=None):
-        src = v if src is None else src
-        op("g", lambda: g.affine_select(ap(v), ap(src), pat, cmp, other, 0, 0), [src], [v])
+    def keep_if(v, pat, cmp, other):
+        op("g", lambda: g.affine_select(ap(v), ap(v), pat, cmp, other, 0, 0), [v], [v])
 
     def pick(qo, so, qi, si, ind):
         op("v", lambda: vec.tensor_copy(ap(qo).bitcast(dt.uint32), ap(qi).bitcast(dt.uint32).indirect(ap(ind))), [qi, ind], [qo])
-        act(so, si, ind=ind)
+        act(so, si, ind)
 
     def L(name, a=0, b=None):
         s, e = LISTS[name]
         return w("ls", s + a, e if b is None else s + b)
+
+    def Z(name, a=0, b=None):
+        return ("lz",) + L(name, a, b)[1:]
+
+    def bank(b, n, a=0):
+        return w("ps%d" % b, a, n)
 
     up, down = (rank - 1) % N, (rank + 1) % N
     others = [(rank + i) % N for i in range(1, N)]
@@ -222,13 +226,11 @@ def rank_program(g, core, T, topo):
         arrive(top, s, len(hu) + len(hd))
         arrive(low, s, len(hu) + len(hd))
 
-    def mine(k):
-        return w("bc%d" % k, 64 * rank, 64 * rank + 64), w("bs%d" % k, 64 * rank, 64 * rank + 64)
-
     def seeds(k):
+        q, s = w("bc%d" % k, 64 * rank, 64 * rank + 64), w("bs%d" % k, 64 * rank, 64 * rank + 64)
+        pick(q, s, w("qx%d" % k, 0, C), w("sx%d" % k, 0, C), L("seed"))
         m = bits(topo.engines(core, T.cores[others[0]]))
         ids = [dst(r) for r in others]
-        q, s = mine(k)
         fused([(ids, m, "se%d" % k, ap(q).bitcast(dt.uint8), [ap(q).bitcast(dt.uint8) for r in others])], [q])
         fused([(ids, m, "se%d" % k, ap(s), [ap(s) for r in others])], [s])
         n = 2 * len(others) * bin(m).count("1")
@@ -245,14 +247,30 @@ def rank_program(g, core, T, topo):
     def fc(i, n=1):
         return w("cf", i, i + n)
 
-    Q, LO, L3, C31, O1, P, L3H, H8, B32, X64, PM8, Q6, HL, HI, LO16, E0, LH, Q16, GF, TMP = [fc(i) for i in range(20)]
-    G16, HL2 = fc(26), fc(27)
-    X7, EL = fc(20, 3), fc(24, 2)
+    Q, LO, C31, O1, P, G16, H8, B32, X8, PM8, Q6, HI, LO16, E0, LH, LH0, Q16, GF, TMP, QB = [fc(i) for i in range(20)]
+    XR = [fc(20 + i) for i in range(3)]
     DR, D2, DROW = w("dd", 0, 1), w("dd", 1, 3), w("dd", 3, 11)
     io2 = lambda n: w("io2", 0, n)
 
-    iota(w("ci", 5, 6), [[0, 1]], 0, 1)
-    iota(w("ci", 7, 8), [[0, 1]], 0, 3)
+    def ceb(b):
+        return w("ce", 128 * b, 128 * b + 128), w("cs", 128 * b, 128 * b + 128)
+
+    def ccw(i, e):
+        a = 256 * i + 128 * e
+        return w("cc", a, a + 128), w("ccs", a, a + 128)
+
+    def turner(i):
+        for e in range(2):
+            act(w("wd", 2 * (i % 2) + e, 512, 4), w("eye", 16 * e, 16 * e + 48), L("tn%d" % i))
+
+    def turner_q(i, e):
+        o = 2 * (i % 2) + e
+        quant(*ccw(i, e), w("wd", o, o + 512))
+
+    def turner_list(i):
+        ts(L("tn%d" % i), DROW, float(H[i]), A.mult, Q16, A.add)
+
+    iota(w("ci", 4, 5), [[0, 1]], 0, 1)
     iota(io2(12), [[2, 12]], 0, 0)
     iota(w("i128", 0, 128), [[1, 128]], 0, 0)
     iota(w("ib", 0, 4), [[-8, 2], [16, 2]], 8, 1)
@@ -262,12 +280,9 @@ def rank_program(g, core, T, topo):
     halo(0, 8, 24)
 
     fill(w("wd", 0, 516), 0.0)
-    ts(w("ci", 0, 1), w("ci", 5, 6), 15, A.bitwise_and)
-    ts(w("ci", 3, 4), w("ci", 5, 6), 31, A.bitwise_and)
-    ts(w("ci", 4, 5), w("ci", 5, 6), 1, A.bitwise_and)
-    ts(w("ci", 1, 3), w("ci", 5, 8, 2), 7, A.bitwise_and)
-    ts(w("ci", 6, 7), w("ci", 7, 8), 1, A.arith_shift_right, 7, A.bitwise_and)
-    copy(fc(0, 7), w("ci", 0, 7))
+    for i, m in enumerate((15, 7, 31, 1)):
+        ts(w("ci", i, i + 1), w("ci", 4, 5), m, A.bitwise_and)
+    copy(fc(0, 5), w("ci", 0, 5))
     lin(w("da", 3, 11), io2(8), 0.5, -2, F.Abs)
     lin(Q6, Q, 6, 0)
     lin(G16, P, -1, Q)
@@ -278,69 +293,49 @@ def rank_program(g, core, T, topo):
     lin(w("da", 2, 3), B32, 0.0625, -1, F.Abs)
     lin(PM8, O1, -16, 8)
     lin(Q16, Q, 1, 16)
-
     ts(w("wd", 3, 515, 4), w("i128", 0, 128), P, A.is_equal)
     ts(w("sw", 0, 4), io2(4), 48.0, A.mult, Q6, A.add)
-    ts(w("sw", 4, 8), w("sw", 0, 4), float(ROT), A.is_lt, float(C), A.mult)
     ts(w("bt", 8, 12), w("ib", 0, 4), G16, A.add, 8.0, A.mult)
-    tt(w("sw", 8, 12), w("sw", 0, 4), w("sw", 4, 8), A.add)
+    ts(w("sw", 4, 8), w("sw", 0, 4), float(ROT), A.is_lt, float(C), A.mult)
     ts(w("bt", 12, 16), w("bt", 8, 12), 192.0, A.is_ge, -192.0, A.mult)
-    ts(L("seed"), w("sw", 8, 12), -float(ROT), A.add)
+    tt(w("sw", 8, 12), w("sw", 0, 4), w("sw", 4, 8), A.add)
     tt(w("bt", 0, 4), w("bt", 8, 12), w("bt", 12, 16), A.add)
     ts(w("da", 0, 11), w("da", 0, 11), -1.0, A.mult, 2.0, A.add)
+    ts(L("seed"), w("sw", 8, 12), -float(ROT), A.add)
     ts(w("dd", 0, 11), w("da", 0, 11), -1.0, A.max, 1.0, A.min)
     lin(HI, H8, 2, 0)
     lin(LO16, LO, 16, 0)
     lin(w("bt", 4, 6), w("bt", 2, 4), 1, PM8)
     lin(w("sw", 0, 4), io2(4), 16, HI)
-    lin(X64, DR, 8, 8)
+    lin(X8, DR, 8, 8)
     for i, s in enumerate((H[0], H[1] - H[0], -1)):
         lin(w("tw", 2 * i, 2 * i + 2), D2, s, Q)
-
-    def ceb(b):
-        return w("ce", 128 * b, 128 * b + 128), w("cs", 128 * b, 128 * b + 128)
-
-    def turner(i):
-        for e in range(2):
-            act(w("wd", 2 * (i % 2) + e, 512, 4), w("eye", 16 * e, 16 * e + 48), ind=L("tn%d" % i))
-
-    def Z(name, a=0, b=None):
-        return ("lz",) + L(name, a, b)[1:]
-
     for j in range(2):
         lin(w("tw", 6 + j, 22, 2), DROW, H[0], w("tw", j, j + 1))
-    lin(Z("rows0"), w("bt", 2, 6), 0.125, X64)
+    lin(Z("rows0"), w("bt", 2, 6), 0.125, X8)
     lin(Z("tn0"), DROW, H[0], Q16)
     lin(E0, LO, 4, B32)
+    lin(QB, B32, -2, 192)
     for b in range(2):
         quant(*ceb(b), w("wd", 3 - b, 515 - b))
 
     quant(w("qx0", 0, C - ROT), w("sx0", 0, C - ROT), w("xt0", 0, cut))
     quant(w("qx0", C - ROT, C), w("sx0", C - ROT, C), w("xt0", cut, 4 * C))
-    pick(*mine(0), w("qx0", 0, C), w("sx0", 0, C), L("seed"))
     seeds(0)
-    iota(w("i16", 0, 16), [[256, 4], [16, 4]], 64 * rank, 0)
     ts(w("tw", 24, 46), w("tw", 0, 22), 0.0, A.is_lt, 48.0, A.mult)
     ts(w("tw", 48, 70), w("tw", 0, 22), 16.0, A.is_ge, 16.0, A.mult)
-    lin(fc(29), B32, -2, 192)
+    lin(w("tb", 6, 22), w("tb", 6, 22), 1, QB)
     lin(TMP, E0, 1, 128)
-    lin(w("tb", 6, 22), w("tb", 6, 22), 1, fc(29))
     lin(Z("spread", 1, 2), H8, 48, E0)
     lin(Z("rot"), w("bt", 0, 2), 0.125, 0)
     lin(Z("spread", 0, 1), H8, 16, TMP)
-    lin(Z("wide"), io2(8), 4, L3H)
-    lin(HL, H8, 1, L3)
     ts(w("eye", 0, 64), w("i64", 0, 64), C31, A.is_equal)
-    quant(*ceb(2), w("wd", 1, 513))
     tt(w("tw", 24, 46), w("tw", 24, 46), w("tw", 48, 70), A.add)
-    quant(*ceb(3), w("wd", 0, 512))
     tt(w("tb", 0, 22), w("tb", 0, 22), w("tw", 0, 22), A.add)
-    ts(L("pair", 0, 4), w("sw", 0, 4), LO16, A.max)
+    quant(*ceb(2), w("wd", 1, 513))
     tt(Z("turn", 0, 22), w("tw", 24, 46), w("tb", 0, 22), A.add)
-    ts(L("pair", 4, 8), w("sw", 0, 4), LO16, A.min)
-    copy(w("ls", 0, 46), w("lz", 0, 46))
-    quant(w("qu", 0, 128), w("suu", 0, 128), w("ut", 0, 512))
-    iota(w("d24", 0, 24), [[0, 8], [1, 3]], 0, 1)
+    quant(*ceb(3), w("wd", 0, 512))
+    copy(w("ls", 0, CAST), w("lz", 0, CAST))
     iota(w("tl", 0, 192), [[0, 192]], 0, 0)
     iota(w("tl", 256, 448), [[0, 192]], 0, 0)
     iota(w("gk", 0, 96), [[0, 12], [-1, 8]], 0, 0)
@@ -352,65 +347,43 @@ def rank_program(g, core, T, topo):
     iota(w("rk", 192, 256), [[0, 64]], 0, 0)
     iota(w("et", 0, 512), [[0, 512]], 0, 0)
     iota(w("ne", 1, 384, 2), [[0, 192]], 1, 0)
-    iota(w("dm", 24, 32), [[0, 8]], 0, 0)
-    iota(w("c3", 0, 24), [[0, 24]], 1, 0)
-
-    def bank(b, n, a=0, step=1):
-        return w("ps%d" % b, a, n, step)
+    iota(w("i12", 0, 24), [[24, 2], [1, 2], [4, 6]], 0, 0)
 
     def fpw(b, a=0, e=C):
         return w("fp", C * b + a, C * b + e)
 
-    def unpack_f(k, bs, a=0, z=C, b0=0):
-        for b in bs:
-            mm(bank(b0 + b, z - a), *ceb(b), w("qx%d" % k, a, z), w("sx%d" % k, a, z))
-            if b < 2:
-                act(fpw(b, a, z), bank(b0 + b, z - a))
-
-    def ccw(i, e):
-        a = 256 * i + 128 * e
-        return w("cc", a, a + 128), w("ccs", a, a + 128)
-
-    def turner_q(i, es=(0, 1)):
-        for e in es:
-            o = 2 * (i % 2) + e
-            quant(*ccw(i, e), w("wd", o, o + 512))
-
-    unpack_f(0, (0,))
-    turner(0)
+    def unpack_f(k, b):
+        mm(bank(b, C), *ceb(b), w("qx%d" % k, 0, C), w("sx%d" % k, 0, C))
+        if b < 2:
+            act(fpw(b), bank(b, C))
 
     def later_columns(part):
         if part == 0:
             lin(Q6, H8, 0.25, 0)
-            lin(fc(28), LO, 32, Q6)
+            lin(TMP, O1, -15, 0)
+            lin(LH0, LO, 32, Q6)
+            lin(w("bt", 8, 12), w("bt", 0, 4), 2, TMP)
         elif part == 1:
             lin(GF, G16, -0.0625, 0)
-            lin(TMP, O1, -15, 0)
-        else:
+            lin(XR[0], DR, 32 * H[0], 28)
+        elif part == 2:
             lin(w("gk", 0, 96), w("gk", 0, 96), 1, GF)
-            lin(fc(20), DR, 32 * H[0], 28)
-            lin(w("bt", 8, 12), w("bt", 0, 4), 2, TMP)
             lin(PM8, O1, 15, -15)
-            lin(fc(21), DR, 32 * H[1], 28)
+            lin(XR[1], DR, 32 * H[1], 28)
             lin(w("bt", 12, 14), w("bt", 4, 6), 2, PM8)
-            lin(HL2, HL, 2, 0)
+        else:
+            lin(LH, LO, 24, Q6)
+            lin(XR[2], DR, 32 * H[2], 28)
 
     def rows(k, src, on):
-        if on == "v":
-            copy(w("lfw", 0, 64), src, L("rows%d" % k))
-        else:
-            act(w("lfw", 0, 64), src, ind=L("rows%d" % k))
+        (copy if on == "v" else act)(w("lfw", 0, 64), src, L("rows%d" % k))
 
     def turn(k, step, on="v"):
         j = min(k, 2)
         if step == 0:
             flip(w("tl", 192, 256), w("lfw", 0, 64))
         elif step == 1:
-            out = w("ot" if k == 3 else "tg", 0, 32)
-            if on == "v":
-                copy(out, w("tl", 192, 256), L("turn", 2 * j, 2 * j + 2))
-            else:
-                act(out, w("tl", 192, 256), ind=L("turn", 2 * j, 2 * j + 2))
+            (copy if on == "v" else act)(w("ot" if k == 3 else "tg", 0, 32), w("tl", 192, 256), L("turn", 2 * j, 2 * j + 2))
         elif step == 2:
             flip(w("lf", 0, 32), w("tg", 0, 32))
         else:
@@ -433,12 +406,21 @@ def rank_program(g, core, T, topo):
             a = h + h * DC[m]
             dma("y", ap(o), t[a:a + 16, :, :], "fr%d" % k, [], [o], ["fw%d" % k, "se%d" % k])
 
-    pick(w("qua", 0, 128), w("sua", 0, 128), w("qu", 0, 128), w("suu", 0, 128), L("pair"))
-    unpack_f(0, (1,))
-    later_columns(0)
-    ts(L("slot"), w("i16", 0, 16), HL, A.add)
+    def row_list(i, j):
+        h = H[i]
+        if j == 0:
+            ts(L("own%d" % i), w("bt", 8, 10), XR[i], A.add, OWN - 1.0, A.min)
+        elif j == 1:
+            ts(L("all%d" % i), w("bt", 8, 10), XR[i], A.add, 32.0 * h, A.add)
+        elif i < 2:
+            ts(L("rows%d" % (i + 1)), w("bt", 10, 14), XR[i + 1], A.add, 32.0 * h, A.add)
+        else:
+            ts(L("rows3"), w("bt", 10, 14), 28.0, A.add)
+
+    unpack_f(0, 0)
+    turner(0)
     rows(0, w("ext0", 0, 40), "v")
-    ts(w("d3", 0, 24), w("d24", 0, 24), G16, A.add, 0.33333334, A.mult)
+    ts(L("pair", 0, 4), w("sw", 0, 4), LO16, A.max)
     turn(0, 0)
     for i in range(4):
         for j in range(4):
@@ -448,23 +430,15 @@ def rank_program(g, core, T, topo):
                 dma("y", ap(o), ap(v), "fr0", [v], [o])
     dma("y", ap(w("wq", 0, 512)).bitcast(dt.uint8), T.wc[:, :], "lw", [], [w("wq", 0, 512)], ["se0"])
     dma("y", ap(w("wsc", 0, 512)), T.ws[:, :], "lw", [], [w("wsc", 0, 512)])
-    turner_q(0, (0,))
+    dma("y", ap(w("vt", 0, 512)), T.v[:, :], "lv", [], [w("vt", 0, 512)])
+    ts(L("pair", 4, 8), w("sw", 0, 4), LO16, A.min)
     turn(0, 1)
-    turner_q(0, (1,))
+    quant(w("qu", 0, 128), w("suu", 0, 128), w("ut", 0, 512))
     turn(0, 2)
-    ts(w("d4", 0, 24), w("d3", 0, 24), 3.0, A.mult, G16, A.subtract)
+    unpack_f(0, 1)
+    pick(w("qua", 0, 128), w("sua", 0, 128), w("qu", 0, 128), w("suu", 0, 128), L("pair"))
     turn(0, 3)
-
-    def row_lists(i, j):
-        h = H[i]
-        if j == 0:
-            ts(L("own%d" % i), w("bt", 8, 10), fc(20 + i), A.add, OWN - 1.0, A.min)
-        elif j == 1:
-            ts(L("all%d" % i), w("bt", 8, 12), fc(20 + i), A.add, 32.0 * h, A.add)
-        elif i < 2:
-            ts(L("rows%d" % (i + 1)), w("bt", 10, 14), fc(21 + i), A.add, 32.0 * h, A.add)
-        else:
-            ts(L("rows3"), w("bt", 10, 14), 28.0, A.add)
+    later_columns(0)
 
     def bwin(b):
         return w("bp", 256 * b, 256 * b + 256)
@@ -478,20 +452,20 @@ def rank_program(g, core, T, topo):
             if on == "v":
                 ts(out, bwin(b), 0.015625, A.mult, ind=ind)
             else:
-                act(out, bwin(b), scale=0.015625, ind=ind)
+                act(out, bwin(b), ind, 0.015625)
 
     def add_f(k, a, z, b0):
         for b in range(4):
             mm(bank(b0 + b, z - a), *ceb(b), w("qx%d" % k, a, z), w("sx%d" % k, a, z), True, False)
 
-    def layer(k, a, z, b0):
+    def layer(a, z, b0):
         qy, sy = w("qy", a, z), w("sy", a, z)
         quant(qy, sy, w("yt", 4 * a, 4 * z))
         for b in range(4):
             mm(bank(b0 + b, z - a), *wb(b), qy, sy, False, True)
 
-    def new_x(k, a, z, b0, bs=range(4)):
-        for b in bs:
+    def new_x(k, a, z, b0):
+        for b in range(4):
             tt(w("xt%d" % (k + 1), 4 * a + b, 4 * z, 4), bank(b0 + b, z - a), fpw(b, a, z), A.max)
 
     def quant_x(k, a, z):
@@ -523,16 +497,9 @@ def rank_program(g, core, T, topo):
         h, last = H[k], k == 2
         e, n = "ext%d" % (k + 1), 32 * h
         own, whole = w(e, n, n + OWN), w(e, 0, 2 * n + OWN)
-        lu, sv = w("lu", 0, 24), w("sv", 0, 8)
+        lu = w("lu", 0, 24)
         a1, a2 = 16 - 2 * h, 16 + 2 * h
         mid = 16 * a1
-
-        def unpack_b(b):
-            mm(bank(4 + b, 256), *ceb(b), w("bc%d" % k, 0, 256), w("bs%d" % k, 0, 256))
-            if b == 0:
-                copy(bwin(b), bank(4 + b, 256))
-            else:
-                act(bwin(b), bank(4 + b, 256))
 
         def z_last(t):
             a, z = 128 * t, 128 * t + 128
@@ -544,23 +511,21 @@ def rank_program(g, core, T, topo):
             mm(bank(4 + t, 128), qz, sz, w("qua", 0, 128), w("sua", 0, 128))
             act(w("sc", 64 * t, 64 * t + 64), bank(4 + t, 128, 64))
 
-        unpack_b(0)
-        unpack_b(2)
-        unpack_b(1)
-        if OPT["c3"][k]:
-            unpack_b(3)
+        for b in (0, 2, 1, 3):
+            mm(bank(4 + b, 256), *ceb(b), w("bc%d" % k, 0, 256), w("bs%d" % k, 0, 256))
+            (act if b else copy)(bwin(b), bank(4 + b, 256))
+        if k == 0:
+            turner_q(0, 0)
+            unpack_f(0, 2)
+            unpack_f(0, 3)
         tt(w("zt", 0, 4 * C, 4), bwin(0), fpw(0), A.subtract, ind=lu)
-        unpack_f(k, (2,))
-        act(w("gz", 0, C), bwin(2), ind=lu)
+        act(w("gz", 0, C), bwin(2), lu)
         tt(w("zt", 1, 4 * C, 4), bwin(1), fpw(1), A.subtract, ind=lu)
-        if not OPT["c3"][k]:
-            unpack_b(3)
-        unpack_f(k, (3,))
         tt(w("zt", 2, 4 * C, 4), w("gz", 0, C), bank(2, C), A.subtract)
         for t in range(3):
-            act(w("gz", C + 128 * t, C + 128 * t + 128), bwin(3), ind=w("lu", 8 * t, 8 * t + 8))
+            act(w("gz", C + 128 * t, C + 128 * t + 128), bwin(3), w("lu", 8 * t, 8 * t + 8))
         if k == 0:
-            act(w("gb", 0, 256), w("tl", 0, 448), ind=L("both"))
+            act(w("gb", 0, 256), w("tl", 0, 448), L("both"))
         z_last(0)
         z_last(1)
         scores(0)
@@ -570,171 +535,93 @@ def rank_program(g, core, T, topo):
         scores(1)
         scores(2)
         if k == 0:
-            ts(L("cand0"), w("i12", 24, 48), fc(28), A.add)
+            ts(L("cand0"), w("i12", 24, 48), LH0, A.add)
             flip(w("lsh", 0, 256), w("gb", 0, 256))
-        elif k == 1:
-            turner_q(1, (1,))
-            row_lists(k, 0)
-        else:
-            turner_q(2)
+            turner_q(0, 1)
         cand = "cand" if k else "cand0"
-        act(w("lsr", 0, 384, 2), w("lsh", 0, 288), ind=L(cand, 0, 12))
-        act(w("lsr", 1, 384, 2), w("lsh", 0, 288), scale=-1.0, ind=L(cand, 12, 24))
+        act(w("lsr", 0, 384, 2), w("lsh", 0, 288), L(cand, 0, 12))
+        act(w("lsr", 1, 384, 2), w("lsh", 0, 288), L(cand, 12, 24), -1.0)
         for t in range(3):
             tt(w("fl", 64 * t, 64 * t + 64), bank(4 + t, 64), w("sc", 64 * t, 64 * t + 64), A.is_gt)
         scan(w("rk", 0, 192), w("sc1", 0, 192), w("fl", 0, 192))
-        src, et = w("rk", 7, 256, 8), w("et", 0, 512)
-        op("v", lambda: vec.tensor_copy(ap(et).indirect(ap(L("spread"))), ap(src)), [src, L("spread")], [et])
-        quant(w("qe", 0, 128), w("se", 0, 128), et)
+        scatter(w("et", 0, 512), L("spread"), w("rk", 7, 256, 8))
+        quant(w("qe", 0, 128), w("se", 0, 128), w("et", 0, 512))
         for j in range(2):
             mm(bank(6 + j, 128), *ccw(k, j), w("qe", 0, 128), w("se", 0, 128))
         if k == 0:
             later_columns(2)
-            pick(w("qs0", 0, 128), w("ss0", 0, 128), *mine(0), L("wide"))
-        else:
-            act(fpw(2), bank(2, C))
-            act(fpw(3), bank(3, C))
-        if k == 1:
-            row_lists(k, 1)
-            row_lists(k, 2)
-            ts(L("tn2"), DROW, float(H[2]), A.mult, Q16, A.add)
-        if last:
-            quant(w("qv", 0, 128), w("svv", 0, 128), w("vt", 0, 512))
+            row_list(0, 0)
+            row_list(0, 1)
+        act(fpw(2), bank(2, C))
+        act(fpw(3), bank(3, C))
         for j in range(2):
             tt(w("ne", 192 * j, 192 * j + 192, 2), bank(6 + j, 96), w("gk", 0, 96), A.not_equal)
         for j in range(2):
             scan(w(e, n + j, n + OWN, 2), w("ne", 192 * j, 192 * j + 192), w("lsr", 192 * j, 192 * j + 192))
         halo(k + 1, n, OWN)
-        if k == 0:
-            keep_if(w("c3", 0, 24), [[0, 8], [1, 3]], A.is_gt, 0.0)
-            iota(w("xsd", 0, 512), [[0, 512]], 0, 0)
-            iota(w("i12", 0, 24), [[24, 2], [1, 2], [4, 6]], 0, 0)
         add_f(k, 0, mid, 4)
         if last:
             rows(3, own, "s")
-        if k == 0:
-            row_lists(k, 0)
         copy(w("mi", 0, 32), own, L("own%d" % k))
-        if k == 0:
-            row_lists(k, 1)
         gather("mi", 0, a1, (0, 1), "v")
         gather("mi", 0, a1, (2, 3), "s")
         if k:
             gather("mi", a2, 24, range(4), "s")
         else:
-            act(fpw(2), bank(2, C))
-            act(fpw(3), bank(3, C))
-            row_lists(k, 2)
-        layer(k, 0, mid, 4)
-        if k == 0:
-            tt(w("dm", 0, 24), w("d4", 0, 24), w("d24", 0, 24), A.is_equal)
-            ts(L("nat"), io2(4), 16.0, A.mult, HL2, A.add)
-            ts(L("tn1"), DROW, float(H[1]), A.mult, Q16, A.add)
-        if not last:
-            act(w("fs", 0, 256), w("bp", 0, 1024), ind=L("slot"))
-            for b in range(4):
-                mm(bank(b, 128), *ceb(b), w("qs%d" % k, 0, 128), w("ss%d" % k, 0, 128), True, False)
-
-        if k == 1:
-            for j in range(3):
-                row_lists(2, j)
-
-        def inner(at):
-            new_x(k, 0, mid, 4, [b for b in range(4) if EARLY[k][b] == at])
-
+            row_list(0, 2)
+        layer(0, mid, 4)
+        add_f(k, mid, C, 0)
         if last:
             turn(3, 0)
             turn(3, 1, "s")
             for m in range(8):
                 v = w("ot", 16 * (m % 2), 16 * (m % 2) + 16, 1, 32 * (m // 2), 32 * (m // 2) + 24)
                 dma("y", T.op[m:m + 1, :], ap(v), "st", [v], [])
-        inner(0)
+        copy(w("mu", 0, 32), whole, L("all%d" % k))
+        gather("mu", a1, a2, (1, 2, 3), "s")
         if not last:
             rows(k + 1, whole, "s")
             fan_out(k + 1)
-            tt(w("sm", 0, 32), whole, w("dm", 0, 32), A.mult, ind=L("all%d" % k, 2, 4))
-            def edge_list(at):
-                if OPT["mu"][k] == at:
-                    copy(w("mu", 0, 32), whole, L("all%d" % k, 0, 2))
-
-            edge_list(0)
-            inner(1)
-            scan(w("sn", 0, 24), w("c3", 0, 24), w("sm", 0, 24))
-            edge_list(1)
-            inner(2)
-            copy(sv, w("sn", 2, 24, 3))
-            edge_list(2)
-            for b in (2, 0, 3, 1):
-                if b < 2:
-                    ts(w("ys", b, 512, 4), bwin(b), 0.015625, A.mult, ind=sv)
-                else:
-                    act(w("ys", b, 512, 4), bwin(b), scale=0.015625, ind=sv)
-            edge_list(3)
-            inner(3)
-            quant(w("qys", 0, 128), w("sys0", 0, 128), w("ys", 0, 512))
-            gather("mu", a1, a2, range(3), "s")
-            gather("mu", a1, a2, (3,), "v")
-            for b in range(4):
-                mm(bank(b, 128), *wb(b), w("qys", 0, 128), w("sys0", 0, 128), False, True)
-            for b in range(4):
-                tt(w("xsd", b, 512, 8), bank(b, 128, 0, 2), w("fs", 64 * b, 64 * b + 64), A.max)
-            inner(4)
-            q, s = w("qs%d" % (k + 1), 0, 128), w("ss%d" % (k + 1), 0, 128)
-            quant(q, s, w("xsd", 0, 512))
-            inner(5)
-            pick(*mine(k + 1), q, s, L("nat"))
-            seeds(k + 1)
-            fan_in(k + 1)
-            if k == 0:
-                dma("y", ap(w("vt", 0, 512)), T.v[:, :], "lv", [], [w("vt", 0, 512)])
-            add_f(k, mid, C, 0)
-            layer(k, mid, C, 0)
-            if k == 0:
-                lin(LH, LO, 24, Q6)
-                lin(fc(22), DR, 32 * H[2], 28)
+        gather("mu", a1, a2, (0,), "v")
+        new_x(k, 0, mid, 4)
+        layer(mid, C, 0)
+        if k == 0:
+            turner_list(1)
+            later_columns(3)
+        if not last:
             turner(k + 1)
-            inner(6)
-            if OPT["tt"][k] == 0:
-                turn(k + 1, 0)
-            quant_x(k + 1, 0, mid)
-            if OPT["tt"][k] == 0:
-                turn(k + 1, 1, "s")
-            unpack_f(k + 1, (0, 1), 0, mid, 4)
-            new_x(k, mid, C, 0)
-            if OPT["tt"][k] == 1:
-                turn(k + 1, 0)
-                turn(k + 1, 1, "s")
-            quant_x(k + 1, mid, C)
-            unpack_f(k + 1, (0, 1), mid, C)
-            if OPT["tt"][k] == 2:
-                turn(k + 1, 0)
-                turn(k + 1, 1)
-            turn(k + 1, 2)
-            if k == 0:
-                turner_q(1, (0,))
-            turn(k + 1, 3)
-            if k == 0:
-                ts(L("cand"), w("i12", 0, 24), LH, A.add)
-        else:
-            add_f(k, mid, C, 0)
-            copy(w("mu", 0, 32), whole, L("all%d" % k, 0, 2))
-            gather("mu", a1, a2, range(OPT["tg"], 4), "s")
-            inner(1)
-            gather("mu", a1, a2, range(OPT["tg"]), "v")
-            inner(2)
-            layer(k, mid, C, 0)
-            quant_x(3, 0, mid)
+        quant_x(k + 1, 0, mid)
+        if last:
             put_codes(0, mid)
             put_scales(0, mid, "y", range(4))
             put_y(0, mid, 4)
-            new_x(k, mid, C, 0)
-            quant_x(3, mid, C)
+        new_x(k, mid, C, 0)
+        quant_x(k + 1, mid, C)
+        if last:
             put_codes(mid, C)
             put_scales(mid, C, "y", (0, 1))
             put_scales(mid, C, "s", (2,))
             put_y(C - ROT, C, 5)
             put_y(mid, C - ROT, 6, "v")
             put_scales(mid, C, "s", (3,))
-    for sem in [s for s in SEMAPHORES if s != "st"] + ["st"]:
+            break
+        seeds(k + 1)
+        fan_in(k + 1)
+        for b in range(4):
+            unpack_f(k + 1, b)
+        for step in range(4):
+            turn(k + 1, step)
+            if step < 2:
+                turner_q(k + 1, step)
+            if step == 2:
+                row_list(k + 1, 0)
+        row_list(k + 1, 1)
+        row_list(k + 1, 2)
+        if k == 0:
+            ts(L("cand"), w("i12", 0, 24), LH, A.add)
+            turner_list(2)
+        else:
+            quant(w("qv", 0, 128), w("svv", 0, 128), w("vt", 0, 512))
+    for sem in SEMAPHORES:
         if total.get(sem, 0):
             wait("g", sem, total[sem])

from concourse.bass import DstId, RemoteDMATransfer
from concourse.mybir import dt, AluOpType, ActivationFunctionType

C = 384
H = [4, 2, 1]
DC = [0, 1, 1, 1, 0, -1, -1, -1]
OWN = 384
ROT = 128

SCRATCH = {}


def _b(name, cols, dtype, where="sbuf"):
    SCRATCH[name] = (where, [128, cols], dtype)


X4, U8, BF, F32, I32, U16 = "float8_e4m3fn_x4", "uint8", "bfloat16", "float32", "int32", "uint16"
for _i in range(8):
    _b("ps%d" % _i, 512, F32, "psum")
for _r in range(4):
    _b("xt%d" % _r, 4 * C, BF)
    _b("qx%d" % _r, C, X4)
    _b("sx%d" % _r, C, U8)
_b("ext0", 40, I32)
for _r in range(3):
    _b("ext%d" % (_r + 1), OWN + 64 * H[_r], BF)
    _b("bc%d" % _r, 256, X4)
    _b("bs%d" % _r, 256, U8)
    if _r:
        SCRATCH["fan%d" % _r] = ("dram", [16 + 2 * H[_r], 8, 24], BF)

LISTS, _at = {}, 0
for _n, _c in (("rows0", 4), ("turn", 6), ("both", 16), ("rot", 2), ("spread", 2), ("tn0", 8),
               ("cand0", 24), ("cand", 24), ("seed", 4), ("pair", 8), ("tn1", 8), ("tn2", 8), ("rows1", 4), ("rows2", 4), ("rows3", 4),
               ("all0", 2), ("all1", 2), ("all2", 2), ("own0", 2), ("own1", 2), ("own2", 2)):
    LISTS[_n] = (_at, _at + _c)
    _at += _c
CAST = LISTS["tn0"][1]

for _n, _c, _t in (("fp", 4 * C, BF), ("bp", 1024, BF), ("gz", 2 * C, BF), ("zt", 4 * C, BF), ("yt", 4 * C, BF),
                   ("lfw", 64, BF), ("tl", 448, BF), ("tg", 32, BF), ("lf", 32, BF), ("lu", 32, U16), ("mi", 32, U16), ("mu", 32, U16), ("lsh", 288, BF), ("lsr", 384, BF),
                   ("qz", C, X4), ("sz", C, U8), ("qy", C, X4), ("sy", C, U8),
                   ("sc", 192, F32), ("fl", 192, BF), ("rk", 256, BF), ("et", 512, BF), ("qe", 128, X4), ("se", 128, U8), ("ne", 384, BF), ("yo", C, F32), ("ot", 32, F32),
                   ("ut", 512, BF), ("vt", 512, BF), ("qu", 128, X4), ("suu", 128, U8), ("qua", 128, X4), ("sua", 128, U8), ("qv", 128, X4), ("svv", 128, U8),
                   ("wq", 512, X4), ("wsc", 512, U8), ("wd", 528, BF), ("ce", 512, X4), ("cs", 512, U8), ("cc", 768, X4), ("ccs", 768, U8),
                   ("ci", 8, I32), ("cf", 32, F32), ("dd", 16, F32), ("da", 16, F32), ("io2", 12, F32), ("ib", 4, F32), ("bt", 16, F32), ("tw", 72, F32), ("sw", 12, F32),
                   ("i64", 64, F32), ("i128", 128, F32), ("eye", 64, BF), ("gk", 96, BF), ("sc1", 192, BF), ("i12", 48, F32), ("tb", 22, F32), ("gb", 256, BF),
                   ("lz", CAST, F32), ("ls", _at, U16)):
    _b(_n, _c, _t)
SEMAPHORES = ["kv", "ks", "kt", "kg", "lx", "lx2", "lp", "lu", "lw", "lv", "loc", "ha0", "ha1", "ha2", "ha3"]
for _r in range(3):
    SEMAPHORES += ["se%d" % _r, "fw%d" % _r, "fr%d" % _r]
SEMAPHORES += ["st"]


def rank_program(g, core, T, topo):
    rank = T.rank_of(core)
    if rank is None:
        return
    A, F = AluOpType, ActivationFunctionType
    N = len(T.cores)
    vec, sca, ten, syn = g.vector, g.scalar, g.tensor, g.sync
    queue = {"v": vec, "s": sca, "t": ten, "g": g, "y": syn}
    total, seen, log, behind = {}, {q: {} for q in queue}, {}, {}

    def w(name, a, b, step=1, p0=0, p1=128):
        return (name, a, b, step, p0, p1)

    def ap(v):
        name, a, b, step, p0, p1 = v
        t = T[name]
        if p0 == 0 and p1 == 128:
            return t[:, a:b] if step == 1 else t[:, a:b:step]
        return t[p0:p1, a:b] if step == 1 else t[p0:p1, a:b:step]

    def meet(x, y):
        if x[1] >= y[2] or y[1] >= x[2] or x[4] >= y[5] or y[4] >= x[5]:
            return False
        return not (x[3] == y[3] and x[3] > 1 and (x[1] - y[1]) % x[3])

    def wait(q, sem, val):
        if seen[q].get(sem, 0) < val:
            queue[q].wait_ge(T.sem[sem], int(val))
            seen[q][sem] = val
            for s, n in behind.get((sem, val), {}).items():
                seen[q][s] = max(seen[q].get(s, 0), n)

    def order(q, reads, writes, acc, dma):
        need = {}
        for vs, wr in ((reads, False), (writes, True)):
            for v in vs:
                bank = v[0][:2] == "ps"
                for (o, owr, oq, osem, oval, odma) in log.get(v[0], ()):
                    if not (bank or meet(v, o)):
                        continue
                    if not (wr or owr or (bank and oq != q)):
                        continue
                    if oq == q and acc and wr and owr:
                        continue
                    need[osem] = max(need.get(osem, 0), total[osem] if odma else oval)
        for sem, val in need.items():
            if not any(behind.get((s, n), {}).get(sem, 0) >= val for s, n in need.items() if s != sem):
                wait(q, sem, val)

    def note(q, reads, writes, sem, val, dma):
        for v in writes:
            old = log.get(v[0], [])
            log[v[0]] = [e for e in old if not (v[3] == 1 and v[1] <= e[0][1] and v[2] >= e[0][2] and v[4] <= e[0][4] and v[5] >= e[0][5])]
            log[v[0]].append((v, True, q, sem, val, dma))
        for v in reads:
            log.setdefault(v[0], []).append((v, False, q, sem, val, dma))

    def op(q, call, reads, writes, acc=False):
        order(q, reads, writes, acc, False)
        sem = "k" + q
        total[sem] = total.get(sem, 0) + 1
        call().then_inc(T.sem[sem], 1)
        behind[(sem, total[sem])] = dict(seen[q])
        note(q, reads, writes, sem, total[sem], False)

    def dma(q, out, in_, sem, reads, writes, after=()):
        order(q, reads, writes, False, True)
        for s in after:
            wait(q, s, total[s])
        total[sem] = total.get(sem, 0) + 16
        queue[q].dma_start(out, in_).then_inc(T.sem[sem], 16)
        note(q, reads, writes, sem, total[sem], True)

    def arrive(v, sem, val):
        total[sem] = val
        log.setdefault(v[0], []).append((v, True, "r", sem, val, True))

    def at(v, ind):
        return ap(v) if ind is None else ap(v).indirect(ap(ind))

    def rd(v, ind):
        return [v] if ind is None else [v, ind]

    def copy(out, in_, ind=None):
        op("v", lambda: vec.tensor_copy(ap(out), at(in_, ind)), rd(in_, ind), [out])

    def scatter(out, ind, in_):
        op("v", lambda: vec.tensor_copy(at(out, ind), ap(in_)), [in_, ind], [out])

    def tt(out, a, b, o, ind=None):
        op("v", lambda: vec.tensor_tensor(ap(out), at(a, ind), ap(b), o), rd(a, ind) + [b], [out])

    def ts(out, a, s1, o1, s2=None, o2=None, ind=None):
        more = [s for s in (s1, s2) if isinstance(s, tuple)]
        n1, n2 = [ap(s) if isinstance(s, tuple) else s for s in (s1, s2)]
        if o2 is None:
            op("v", lambda: vec.tensor_scalar(ap(out), at(a, ind), n1, None, o1), rd(a, ind) + more, [out])
        else:
            op("v", lambda: vec.tensor_scalar(ap(out), at(a, ind), n1, n2, o1, o2), rd(a, ind) + more, [out])

    def scan(out, keep, add):
        op("v", lambda: vec.tensor_tensor_scan(ap(out), ap(keep), ap(add), 0.0, A.mult, A.add), [keep, add], [out])

    def flip(out, in_):
        op("v", lambda: vec.transpose(ap(out), ap(in_)), [in_], [out])

    def fill(out, val):
        op("v", lambda: vec.memset(ap(out), val), [], [out])

    def act(out, in_, ind=None, scale=1.0):
        if scale == 1.0:
            op("s", lambda: sca.activation(ap(out), at(in_, ind), F.Copy), rd(in_, ind), [out])
        else:
            op("s", lambda: sca.activation(ap(out), at(in_, ind), F.Copy, scale=scale), rd(in_, ind), [out])

    def lin(out, in_, scale, bias, func=None):
        col = isinstance(bias, tuple)
        op("s", lambda: sca.activation(ap(out), ap(in_), F.Identity if func is None else func, bias=ap(bias) if col else float(bias), scale=float(scale)),
           [in_, bias] if col else [in_], [out])

    def quant(q, s, in_):
        op("v", lambda: vec.quantize_mx(ap(q), ap(s), ap(in_)), [in_], [q, s])

    def mm(out, l, ls, r, rs, start=True, stop=True):
        op("t", lambda: ten.matmul_mx(ap(out), ap(l), ap(ls), ap(r), ap(rs), start, stop), [l, ls, r, rs], [out], acc=not start)

    def iota(out, pat, base, cm):
        if SCRATCH[out[0]][2] != I32:
            op("g", lambda: g.iota(ap(out), pat, base, cm, allow_small_or_imprecise_dtypes=True), [], [out])
        else:
            op("g", lambda: g.iota(ap(out), pat, base, cm), [], [out])

    def keep_if(v, pat, cmp, other):
        op("g", lambda: g.affine_select(ap(v), ap(v), pat, cmp, other, 0, 0), [v], [v])

    def pick(qo, so, qi, si, ind):
        op("v", lambda: vec.tensor_copy(ap(qo).bitcast(dt.uint32), ap(qi).bitcast(dt.uint32).indirect(ap(ind))), [qi, ind], [qo])
        act(so, si, ind)

    def L(name, a=0, b=None):
        s, e = LISTS[name]
        return w("ls", s + a, e if b is None else s + b)

    def Z(name, a=0, b=None):
        return ("lz",) + L(name, a, b)[1:]

    def bank(b, n, a=0):
        return w("ps%d" % b, a, n)

    up, down = (rank - 1) % N, (rank + 1) % N
    others = [(rank + i) % N for i in range(1, N)]

    def dst(r):
        rid, pid, _ = topo.addr(T.cores[r])
        return DstId(rid=rid, pnc=pid)

    def bits(es):
        return sum(1 << e for e in es)

    def fused(trs, reads):
        order("g", reads, [], False, True)
        total["loc"] = total.get("loc", 0) + sum(bin(m).count("1") for _, m, _, _, _ in trs)
        g.remote_dma_fused([RemoteDMATransfer(dst_ids=ids, dma_engine_mask=m, remote_sem=T.sem[sem], srcs=[src], dsts=dsts) for ids, m, sem, src, dsts in trs], local_sem=T.sem["loc"])

    def halo(k, n, m):
        e, s = "ext%d" % k, "ha%d" % k
        eu, ed = topo.engines(core, T.cores[up]), topo.engines(core, T.cores[down])
        hu, hd = eu[:len(eu) // 2], ed[len(ed) // 2:]
        lo, hi, top, low = w(e, n, 2 * n), w(e, m, m + n), w(e, 0, n), w(e, n + m, 2 * n + m)
        fused([([dst(up)], bits(hu), s, ap(lo), [ap(low)]), ([dst(down)], bits(hd), s, ap(hi), [ap(top)])], [lo, hi])
        arrive(top, s, len(hu) + len(hd))
        arrive(low, s, len(hu) + len(hd))

    def seeds(k):
        q, s = w("bc%d" % k, 64 * rank, 64 * rank + 64), w("bs%d" % k, 64 * rank, 64 * rank + 64)
        pick(q, s, w("qx%d" % k, 0, C), w("sx%d" % k, 0, C), L("seed"))
        m = bits(topo.engines(core, T.cores[others[0]]))
        ids = [dst(r) for r in others]
        fused([(ids, m, "se%d" % k, ap(q).bitcast(dt.uint8), [ap(q).bitcast(dt.uint8) for r in others])], [q])
        fused([(ids, m, "se%d" % k, ap(s), [ap(s) for r in others])], [s])
        n = 2 * len(others) * bin(m).count("1")
        for r in others:
            arrive(w("bc%d" % k, 64 * r, 64 * r + 64), "se%d" % k, n)
            arrive(w("bs%d" % k, 64 * r, 64 * r + 64), "se%d" % k, n)

    cut = 4 * (C - ROT)
    dma("s", ap(w("ext0", 8, 32)), T.p[:, :], "lp", [], [w("ext0", 8, 32)])
    dma("y", ap(w("xt0", 0, cut)), T.x[:, 4 * ROT:4 * C], "lx", [], [w("xt0", 0, cut)])
    dma("y", ap(w("xt0", cut, 4 * C)), T.x[:, 0:4 * ROT], "lx2", [], [w("xt0", cut, 4 * C)])
    dma("y", ap(w("ut", 0, 512)), T.u[:, :], "lu", [], [w("ut", 0, 512)])

    def fc(i, n=1):
        return w("cf", i, i + n)

    Q, LO, C31, O1, P, G16, H8, B32, X8, PM8, Q6, HI, LO16, E0, LH, LH0, Q16, GF, TMP, QB = [fc(i) for i in range(20)]
    XR = [fc(20 + i) for i in range(3)]
    DR, D2, DROW = w("dd", 0, 1), w("dd", 1, 3), w("dd", 3, 11)
    io2 = lambda n: w("io2", 0, n)

    def ceb(b):
        return w("ce", 128 * b, 128 * b + 128), w("cs", 128 * b, 128 * b + 128)

    def ccw(i, e):
        a = 256 * i + 128 * e
        return w("cc", a, a + 128), w("ccs", a, a + 128)

    def turner(i):
        for e in range(2):
            act(w("wd", 2 * (i % 2) + e, 512, 4), w("eye", 16 * e, 16 * e + 48), L("tn%d" % i))

    def turner_q(i, e):
        o = 2 * (i % 2) + e
        quant(*ccw(i, e), w("wd", o, o + 512))

    def turner_list(i):
        ts(L("tn%d" % i), DROW, float(H[i]), A.mult, Q16, A.add)

    iota(w("ci", 4, 5), [[0, 1]], 0, 1)
    iota(io2(12), [[2, 12]], 0, 0)
    iota(w("i128", 0, 128), [[1, 128]], 0, 0)
    iota(w("ib", 0, 4), [[-8, 2], [16, 2]], 8, 1)
    iota(w("i64", 0, 64), [[0, 2], [-16, 2], [1, 16]], 16, 0)
    iota(w("tb", 0, 6), [[0, 3], [16, 2]], 0, 0)
    iota(w("tb", 6, 22), [[64, 4], [16, 2], [0, 2]], 0, 0)
    halo(0, 8, 24)

    fill(w("wd", 0, 516), 0.0)
    for i, m in enumerate((15, 7, 31, 1)):
        ts(w("ci", i, i + 1), w("ci", 4, 5), m, A.bitwise_and)
    copy(fc(0, 5), w("ci", 0, 5))
    lin(w("da", 3, 11), io2(8), 0.5, -2, F.Abs)
    lin(Q6, Q, 6, 0)
    lin(G16, P, -1, Q)
    lin(B32, C31, -1, P)
    lin(H8, LO, -1, Q)
    lin(w("da", 0, 1), G16, -0.0625, -4, F.Abs)
    lin(w("da", 1, 2), B32, 0.0625, -2, F.Abs)
    lin(w("da", 2, 3), B32, 0.0625, -1, F.Abs)
    lin(PM8, O1, -16, 8)
    lin(Q16, Q, 1, 16)
    ts(w("wd", 3, 515, 4), w("i128", 0, 128), P, A.is_equal)
    ts(w("sw", 0, 4), io2(4), 48.0, A.mult, Q6, A.add)
    ts(w("bt", 8, 12), w("ib", 0, 4), G16, A.add, 8.0, A.mult)
    ts(w("sw", 4, 8), w("sw", 0, 4), float(ROT), A.is_lt, float(C), A.mult)
    ts(w("bt", 12, 16), w("bt", 8, 12), 192.0, A.is_ge, -192.0, A.mult)
    tt(w("sw", 8, 12), w("sw", 0, 4), w("sw", 4, 8), A.add)
    tt(w("bt", 0, 4), w("bt", 8, 12), w("bt", 12, 16), A.add)
    ts(w("da", 0, 11), w("da", 0, 11), -1.0, A.mult, 2.0, A.add)
    ts(L("seed"), w("sw", 8, 12), -float(ROT), A.add)
    ts(w("dd", 0, 11), w("da", 0, 11), -1.0, A.max, 1.0, A.min)
    lin(HI, H8, 2, 0)
    lin(LO16, LO, 16, 0)
    lin(w("bt", 4, 6), w("bt", 2, 4), 1, PM8)
    lin(w("sw", 0, 4), io2(4), 16, HI)
    lin(X8, DR, 8, 8)
    for i, s in enumerate((H[0], H[1] - H[0], -1)):
        lin(w("tw", 2 * i, 2 * i + 2), D2, s, Q)
    for j in range(2):
        lin(w("tw", 6 + j, 22, 2), DROW, H[0], w("tw", j, j + 1))
    lin(Z("rows0"), w("bt", 2, 6), 0.125, X8)
    lin(Z("tn0"), DROW, H[0], Q16)
    lin(E0, LO, 4, B32)
    lin(QB, B32, -2, 192)
    for b in range(2):
        quant(*ceb(b), w("wd", 3 - b, 515 - b))

    quant(w("qx0", 0, C - ROT), w("sx0", 0, C - ROT), w("xt0", 0, cut))
    quant(w("qx0", C - ROT, C), w("sx0", C - ROT, C), w("xt0", cut, 4 * C))
    seeds(0)
    ts(w("tw", 24, 46), w("tw", 0, 22), 0.0, A.is_lt, 48.0, A.mult)
    ts(w("tw", 48, 70), w("tw", 0, 22), 16.0, A.is_ge, 16.0, A.mult)
    lin(w("tb", 6, 22), w("tb", 6, 22), 1, QB)
    lin(TMP, E0, 1, 128)
    lin(Z("spread", 1, 2), H8, 48, E0)
    lin(Z("rot"), w("bt", 0, 2), 0.125, 0)
    lin(Z("spread", 0, 1), H8, 16, TMP)
    ts(w("eye", 0, 64), w("i64", 0, 64), C31, A.is_equal)
    tt(w("tw", 24, 46), w("tw", 24, 46), w("tw", 48, 70), A.add)
    tt(w("tb", 0, 22), w("tb", 0, 22), w("tw", 0, 22), A.add)
    quant(*ceb(2), w("wd", 1, 513))
    tt(Z("turn", 0, 22), w("tw", 24, 46), w("tb", 0, 22), A.add)
    quant(*ceb(3), w("wd", 0, 512))
    copy(w("ls", 0, CAST), w("lz", 0, CAST))
    iota(w("tl", 0, 192), [[0, 192]], 0, 0)
    iota(w("tl", 256, 448), [[0, 192]], 0, 0)
    iota(w("gk", 0, 96), [[0, 12], [-1, 8]], 0, 0)
    iota(w("lsh", 256, 288), [[0, 32]], 0, 0)
    iota(w("i12", 24, 48), [[32, 2], [1, 2], [4, 6]], 0, 0)
    iota(w("sc1", 0, 192), [[0, 192]], 1, 0)
    keep_if(w("sc1", 0, 192), [[0, 3], [1, 8], [-1, 8]], A.not_equal, -1.0)
    keep_if(w("sc1", 0, 192), [[0, 24], [1, 8]], A.is_gt, 0.0)
    iota(w("rk", 192, 256), [[0, 64]], 0, 0)
    iota(w("et", 0, 512), [[0, 512]], 0, 0)
    iota(w("ne", 1, 384, 2), [[0, 192]], 1, 0)
    iota(w("i12", 0, 24), [[24, 2], [1, 2], [4, 6]], 0, 0)

    def fpw(b, a=0, e=C):
        return w("fp", C * b + a, C * b + e)

    def unpack_f(k, b):
        mm(bank(b, C), *ceb(b), w("qx%d" % k, 0, C), w("sx%d" % k, 0, C))
        if b < 2:
            act(fpw(b), bank(b, C))

    def later_columns(part):
        if part == 0:
            lin(Q6, H8, 0.25, 0)
            lin(TMP, O1, -15, 0)
            lin(LH0, LO, 32, Q6)
            lin(w("bt", 8, 12), w("bt", 0, 4), 2, TMP)
        elif part == 1:
            lin(GF, G16, -0.0625, 0)
            lin(XR[0], DR, 32 * H[0], 28)
        elif part == 2:
            lin(w("gk", 0, 96), w("gk", 0, 96), 1, GF)
            lin(PM8, O1, 15, -15)
            lin(XR[1], DR, 32 * H[1], 28)
            lin(w("bt", 12, 14), w("bt", 4, 6), 2, PM8)
        else:
            lin(LH, LO, 24, Q6)
            lin(XR[2], DR, 32 * H[2], 28)

    def rows(k, src, on):
        (copy if on == "v" else act)(w("lfw", 0, 64), src, L("rows%d" % k))

    def turn(k, step, on="v"):
        j = min(k, 2)
        if step == 0:
            flip(w("tl", 192, 256), w("lfw", 0, 64))
        elif step == 1:
            (copy if on == "v" else act)(w("ot" if k == 3 else "tg", 0, 32), w("tl", 192, 256), L("turn", 2 * j, 2 * j + 2))
        elif step == 2:
            flip(w("lf", 0, 32), w("tg", 0, 32))
        else:
            copy(w("lu", 0, 32), w("lf", 0, 32), L("rot"))

    def fan_out(k):
        t, h = T["fan%d" % k], H[k]
        for m in range(8):
            d = (h - H[k - 1]) * DC[m]
            for lo, hi, col in ((-16, 0, 32), (0, 16, 0), (16, 32, 32)):
                a, b = max(lo, d - h), min(hi, 16 + d + h)
                if a < b:
                    v = w("lfw", col, col + 24, 1, 16 * m + a - lo, 16 * m + b - lo)
                    dma("y", t[a - d + h:b - d + h, m, :], ap(v), "fw%d" % k, [v], [])

    def fan_in(k):
        t, h = T["fan%d" % k], H[k]
        for m in range(8):
            o = w("lsh", 0, 192, 1, 16 * m, 16 * m + 16)
            a = h + h * DC[m]
            dma("y", ap(o), t[a:a + 16, :, :], "fr%d" % k, [], [o], ["fw%d" % k, "se%d" % k])

    def row_list(i, j):
        h = H[i]
        if j == 0:
            ts(L("own%d" % i), w("bt", 8, 10), XR[i], A.add, OWN - 1.0, A.min)
        elif j == 1:
            ts(L("all%d" % i), w("bt", 8, 10), XR[i], A.add, 32.0 * h, A.add)
        elif i < 2:
            ts(L("rows%d" % (i + 1)), w("bt", 10, 14), XR[i + 1], A.add, 32.0 * h, A.add)
        else:
            ts(L("rows3"), w("bt", 10, 14), 28.0, A.add)

    unpack_f(0, 0)
    turner(0)
    rows(0, w("ext0", 0, 40), "v")
    ts(L("pair", 0, 4), w("sw", 0, 4), LO16, A.max)
    turn(0, 0)
    for i in range(4):
        for j in range(4):
            if i != j:
                a = 192 + 64 * (i - j)
                v, o = w("tl", 192, 256, 1, 32 * i, 32 * i + 32), w("tl", a, a + 64, 1, 32 * j, 32 * j + 32)
                dma("y", ap(o), ap(v), "fr0", [v], [o])
    dma("y", ap(w("wq", 0, 512)).bitcast(dt.uint8), T.wc[:, :], "lw", [], [w("wq", 0, 512)], ["se0"])
    dma("y", ap(w("wsc", 0, 512)), T.ws[:, :], "lw", [], [w("wsc", 0, 512)])
    dma("y", ap(w("vt", 0, 512)), T.v[:, :], "lv", [], [w("vt", 0, 512)])
    ts(L("pair", 4, 8), w("sw", 0, 4), LO16, A.min)
    turn(0, 1)
    quant(w("qu", 0, 128), w("suu", 0, 128), w("ut", 0, 512))
    turn(0, 2)
    unpack_f(0, 1)
    pick(w("qua", 0, 128), w("sua", 0, 128), w("qu", 0, 128), w("suu", 0, 128), L("pair"))
    turn(0, 3)
    later_columns(0)

    def bwin(b):
        return w("bp", 256 * b, 256 * b + 256)

    def wb(b):
        return w("wq", 128 * b, 128 * b + 128), w("wsc", 128 * b, 128 * b + 128)

    def gather(lst, a, z, bs, on):
        for b in bs:
            out, ind = w("yt", 64 * a + b, 64 * z, 4), w(lst, a, z)
            if on == "v":
                ts(out, bwin(b), 0.015625, A.mult, ind=ind)
            else:
                act(out, bwin(b), ind, 0.015625)

    def add_f(k, a, z, b0):
        for b in range(4):
            mm(bank(b0 + b, z - a), *ceb(b), w("qx%d" % k, a, z), w("sx%d" % k, a, z), True, False)

    def layer(a, z, b0):
        qy, sy = w("qy", a, z), w("sy", a, z)
        quant(qy, sy, w("yt", 4 * a, 4 * z))
        for b in range(4):
            mm(bank(b0 + b, z - a), *wb(b), qy, sy, False, True)

    def new_x(k, a, z, b0):
        for b in range(4):
            tt(w("xt%d" % (k + 1), 4 * a + b, 4 * z, 4), bank(b0 + b, z - a), fpw(b, a, z), A.max)

    def quant_x(k, a, z):
        quant(w("qx%d" % k, a, z), w("sx%d" % k, a, z), w("xt%d" % k, 4 * a, 4 * z))

    def runs(a, z):
        for lo, hi, d in ((0, C - ROT, ROT), (C - ROT, C, ROT - C)):
            if max(a, lo) < min(z, hi):
                yield max(a, lo), min(z, hi), max(a, lo) + d

    def put_codes(a, z):
        for s, e, o in runs(a, z):
            v = w("qx3", s, e)
            dma("y", T.oc[:, 4 * o:4 * (o + e - s)], ap(v).bitcast(dt.uint8), "st", [v], [])

    def put_scales(a, z, q, quarters):
        for s, e, o in runs(a, z):
            for i in quarters:
                dma(q, T.osc[4 * i:4 * i + 4, o:o + e - s], ap(w("sx3", s, e, 1, 32 * i, 32 * i + 4)), "st", [w("sx3", s, e)], [])

    def put_y(a, z, b, on="s"):
        n = max(z - a, 128)
        mm(bank(b, n), w("qv", 0, 128), w("svv", 0, 128), w("qx3", a, a + n), w("sx3", a, a + n))
        (act if on == "s" else copy)(w("yo", a, z), bank(b, z - a))
        for s, e, o in runs(a, z):
            dma("s" if on == "s" else "y", T.y[:, o:o + e - s], ap(w("yo", s, e)), "st", [w("yo", s, e)], [])

    for k in range(3):
        h, last = H[k], k == 2
        e, n = "ext%d" % (k + 1), 32 * h
        own, whole = w(e, n, n + OWN), w(e, 0, 2 * n + OWN)
        lu = w("lu", 0, 24)
        a1, a2 = 16 - 2 * h, 16 + 2 * h
        mid = 16 * a1

        def z_last(t):
            a, z = 128 * t, 128 * t + 128
            tt(w("zt", 4 * a + 3, 4 * z, 4), w("gz", C + a, C + z), bank(3, z, a), A.subtract)

        def scores(t):
            qz, sz = w("qz", 128 * t, 128 * t + 128), w("sz", 128 * t, 128 * t + 128)
            quant(qz, sz, w("zt", 512 * t, 512 * t + 512))
            mm(bank(4 + t, 128), qz, sz, w("qua", 0, 128), w("sua", 0, 128))
            act(w("sc", 64 * t, 64 * t + 64), bank(4 + t, 128, 64))

        for b in (0, 2, 1, 3):
            mm(bank(4 + b, 256), *ceb(b), w("bc%d" % k, 0, 256), w("bs%d" % k, 0, 256))
            (act if b else copy)(bwin(b), bank(4 + b, 256))
        if k == 0:
            turner_q(0, 0)
            unpack_f(0, 2)
            unpack_f(0, 3)
        tt(w("zt", 0, 4 * C, 4), bwin(0), fpw(0), A.subtract, ind=lu)
        act(w("gz", 0, C), bwin(2), lu)
        tt(w("zt", 1, 4 * C, 4), bwin(1), fpw(1), A.subtract, ind=lu)
        tt(w("zt", 2, 4 * C, 4), w("gz", 0, C), bank(2, C), A.subtract)
        for t in range(3):
            act(w("gz", C + 128 * t, C + 128 * t + 128), bwin(3), w("lu", 8 * t, 8 * t + 8))
        if k == 0:
            act(w("gb", 0, 256), w("tl", 0, 448), L("both"))
        z_last(0)
        z_last(1)
        scores(0)
        if k == 0:
            later_columns(1)
        z_last(2)
        scores(1)
        scores(2)
        if k == 0:
            ts(L("cand0"), w("i12", 24, 48), LH0, A.add)
            flip(w("lsh", 0, 256), w("gb", 0, 256))
            turner_q(0, 1)
        cand = "cand" if k else "cand0"
        act(w("lsr", 0, 384, 2), w("lsh", 0, 288), L(cand, 0, 12))
        act(w("lsr", 1, 384, 2), w("lsh", 0, 288), L(cand, 12, 24), -1.0)
        for t in range(3):
            tt(w("fl", 64 * t, 64 * t + 64), bank(4 + t, 64), w("sc", 64 * t, 64 * t + 64), A.is_gt)
        scan(w("rk", 0, 192), w("sc1", 0, 192), w("fl", 0, 192))
        scatter(w("et", 0, 512), L("spread"), w("rk", 7, 256, 8))
        quant(w("qe", 0, 128), w("se", 0, 128), w("et", 0, 512))
        for j in range(2):
            mm(bank(6 + j, 128), *ccw(k, j), w("qe", 0, 128), w("se", 0, 128))
        if k == 0:
            later_columns(2)
            row_list(0, 0)
            row_list(0, 1)
        act(fpw(2), bank(2, C))
        act(fpw(3), bank(3, C))
        for j in range(2):
            tt(w("ne", 192 * j, 192 * j + 192, 2), bank(6 + j, 96), w("gk", 0, 96), A.not_equal)
        for j in range(2):
            scan(w(e, n + j, n + OWN, 2), w("ne", 192 * j, 192 * j + 192), w("lsr", 192 * j, 192 * j + 192))
        halo(k + 1, n, OWN)
        add_f(k, 0, mid, 4)
        if last:
            rows(3, own, "s")
        copy(w("mi", 0, 32), own, L("own%d" % k))
        gather("mi", 0, a1, (0, 1), "v")
        gather("mi", 0, a1, (2, 3), "s")
        if k:
            gather("mi", a2, 24, range(4), "s")
        else:
            row_list(0, 2)
        layer(0, mid, 4)
        add_f(k, mid, C, 0)
        if last:
            turn(3, 0)
            turn(3, 1, "s")
            for m in range(8):
                v = w("ot", 16 * (m % 2), 16 * (m % 2) + 16, 1, 32 * (m // 2), 32 * (m // 2) + 24)
                dma("y", T.op[m:m + 1, :], ap(v), "st", [v], [])
        copy(w("mu", 0, 32), whole, L("all%d" % k))
        gather("mu", a1, a2, (1, 2, 3), "s")
        if not last:
            rows(k + 1, whole, "s")
            fan_out(k + 1)
        gather("mu", a1, a2, (0,), "v")
        new_x(k, 0, mid, 4)
        layer(mid, C, 0)
        if k == 0:
            turner_list(1)
            later_columns(3)
        if not last:
            turner(k + 1)
        quant_x(k + 1, 0, mid)
        if last:
            put_codes(0, mid)
            put_scales(0, mid, "y", range(4))
            put_y(0, mid, 4)
        new_x(k, mid, C, 0)
        quant_x(k + 1, mid, C)
        if last:
            put_codes(mid, C)
            put_scales(mid, C, "y", (0, 1))
            put_scales(mid, C, "s", (2,))
            put_y(C - ROT, C, 5)
            put_y(mid, C - ROT, 6, "v")
            put_scales(mid, C, "s", (3,))
            break
        seeds(k + 1)
        fan_in(k + 1)
        for b in range(4):
            unpack_f(k + 1, b)
        for step in range(4):
            turn(k + 1, step)
            if step < 2:
                turner_q(k + 1, step)
            if step == 2:
                row_list(k + 1, 0)
        row_list(k + 1, 1)
        row_list(k + 1, 2)
        if k == 0:
            ts(L("cand"), w("i12", 0, 24), LH, A.add)
            turner_list(2)
        else:
            quant(w("qv", 0, 128), w("svv", 0, 128), w("vt", 0, 512))
    for sem in SEMAPHORES:
        if total.get(sem, 0):
            wait("g", sem, total[sem])
